import numpy as np, ml_dtypes
CORES = [9,25,41,57]
N = 4
import mx_ref
BF = ml_dtypes.bfloat16
def gcols(t, e):
    v = np.concatenate([t.reshape(8, 16, -1, 4), np.zeros((8, 16, 1, 4), BF)], axis=2)
    return np.ascontiguousarray(np.stack([v[g][:, e[g]] for g in range(8)])).reshape(128, -1)
def tile(rs):
    return np.stack(rs, axis=2).reshape(128, -1).astype(BF)
def cut(t, i, w=512):
    return t[:, w * i:w * i + w]
def pick(q, e):
    c = np.concatenate([q[0].reshape(128, -1, 4), np.zeros((128, 1, 4), np.uint8)], axis=1); s = np.concatenate([q[1], np.ones((16, 1), np.uint8)], axis=1)
    return (np.ascontiguousarray(c[:, e].reshape(128, -1)), np.ascontiguousarray(s[:, e]))
def join(*qs):
    return (np.concatenate([q[0] for q in qs], axis=1), np.concatenate([q[1] for q in qs], axis=1))
def put(q, e, v):
    c, s = q[0].reshape(128, -1, 4).copy(), q[1].copy(); c[:, e] = v[0].reshape(128, -1, 4); s[:, e] = v[1]
    return (c.reshape(128, -1), s)
def pk(c, s):
    return (np.ascontiguousarray(c), mx_ref.live(s))
def emit(q):
    return q[0], q[1]
def packed(v, rng):
    q = [mx_ref.quantize(np.ascontiguousarray(v[r])) for r in range(N)]
    return np.stack([a for a, b in q]), np.stack([mx_ref.plane(b, rng) for a, b in q])
def values_of_codes():
    e, c = np.zeros((128, 128, 4), np.float32), np.zeros((128, 2, 4), np.uint8)
    e[np.arange(128), np.arange(128), 0] = 1
    c[:127, :, 0] = np.arange(256).reshape(2, 128).T[:127]
    return mx_ref.matmul(mx_ref.quantize(e.reshape(128, 512).astype(BF)), (c.reshape(128, 8), np.full((16, 2), 127, np.uint8))).T.reshape(-1).astype(np.float64)
CODE_VALUE, SCALE_VALUE = values_of_codes(), 2.0 ** (np.arange(256) - 127.0)
def decode(q):
    return (CODE_VALUE[q[0]].reshape(16, 8, -1, 4) * SCALE_VALUE[q[1]][:, None, :, None] + 0.0).reshape(128, -1).astype(np.float32)
def f(rng, *shape):
    return mx_ref.flush((rng.standard_normal(shape, dtype=np.float32) * np.exp2(rng.integers(-2, 3, shape[:-1] + (1,)))).astype(BF))
def wide(rng, *shape, cols=0):
    v = rng.standard_normal(shape, dtype=np.float32) * np.exp2(rng.integers(-12, 13, shape)).astype(np.float32)
    if cols: v *= np.repeat(np.exp2(rng.integers(-cols, cols + 1, shape[:-2] + (1, shape[-1] // 4))) * (rng.random(shape[:-2] + (1, shape[-1] // 4)) > 0.0625), 4, axis=-1).astype(np.float32)
    return mx_ref.flush(v.astype(BF))
C, T, R = 448, 96, 2
def match(o):
    m, stack, closes = np.full(C, -1), [], []
    for j in range(C):
        if o[j]:
            stack.append(j)
        elif stack:
            i = stack.pop()
            m[i], m[j] = j, i
        else:
            closes.append(j)
    return m, np.array(stack[::-1], int)[:T], np.array(closes, int)[:T]
def big(v, k):
    v = v.astype(np.float32) * np.float32(k)
    v[np.abs(v) < np.float32(2.0 ** -16)] = 0
    return v.astype(BF)
def same(v):
    return np.stack([v] * N)
def weights(rng, h=-1):
    w = big(f(rng, 128, 2048), 0.25)
    if h >= 0:
        w = w.reshape(128, 4, 128, 4)
        w[:, :, 16 * h:16 * h + 8] = 0
        p = np.arange(16 * h, 16 * h + 8)
        for b in range(2): w[p + 8, b, p, b] = 16
        w = w.reshape(128, 2048)
    c, s = packed(same(w), rng)
    return {"wc": c, "ws": s}
def numbers_of(rng):
    return {"x": big(f(rng, N, 128, 4 * C), 1), "u": same(np.array(f(rng, 128, 512))), "v": np.array(f(rng, N, 128, 512))}
def plant(rng, h, first, then, size=np.ones(8), less=(False, False)):
    d = {**numbers_of(rng), **weights(rng, h)}
    x = d["x"].reshape(N, 128, C, 4)
    x[:, 16 * h:16 * h + 16] = 0
    for t, s in enumerate((first, then)):
        p = 16 * h + 8 * t
        x[:, p:p + 8, :, 0] = (np.where(less[t], -1.25 * s, s) + 0.0).astype(np.float32).astype(BF)
        x[:, p:p + 8, :, 1] = np.roll(np.where(less[t], 1.125 * s, 0.0), 1, axis=1).astype(np.float32).astype(BF)
    d["x"] = x.reshape(N, 128, 4 * C)
    for g in range(8):
        d["u"][:, :, 64 * g:64 * g + 4] = 0
        d["u"][:, 16 * h + g, 64 * g] = float(size[g])
        d["u"][:, 16 * h + (g + 1) % 8, 64 * g + 1] = 1.125 * float(size[g])
    return d
def half(rng, n, b):
    v = rng.permutation(np.repeat([1.0, -1.0], [n + b, n]))
    if n + b == 0: return v
    return np.roll(v, -1 - int(np.argmin(np.cumsum(v))))
def word(rng, a, b):
    n = (C - a - b) // 2
    m = int(rng.integers(0, n + 1))
    return np.concatenate([-half(rng, m, a)[::-1], half(rng, n - m, b)])
def brackets(rng, a, b):
    return np.stack([np.stack([word(rng, int(a[r, g]), int(b[r, g])) for g in range(8)]) for r in range(N)])
def setup_inputs(rng):
    return {**numbers_of(rng), **weights(rng)}
def setup_inputs_zeros(rng):
    h = int(rng.integers(0, 8))
    size = np.exp2(rng.integers(-30, 1, (N, 1, C)))
    first, then = [rng.choice([-1.0, -1.0, 0.0, 1.0], (N, 8, C)) for t in range(2)]
    first[:, h] = rng.integers(0, 2, (N, C))
    less = rng.random((2, N, 8, C)) < 0.5
    return plant(rng, h, first * size, then * size, np.exp2(rng.permutation(np.repeat([-30.0, -12.0, 12.0], [4, 2, 2]))), less)
def counts(rng):
    e = rng.permutation(8) % 2 == 0
    a, b = [np.where(e, rng.choice([0, T, T + 2, 2 * T], (N, 8)), rng.choice([T - 1, T + 1], (N, 8))) for i in range(2)]
    g = np.arange(8)
    i = rng.integers(0, N - 1, 8)
    j = (i + 1) % (N - 1)
    b[i, g] = np.where(e, T, T + 1)
    a[i + 1, g] = np.where(e, T, T + 1)
    b[j, g] = np.where(e, 2 * T, T - 1)
    a[j + 1, g] = np.where(e, 2 * T, T + 1)
    return a, b
def setup_inputs_cap(rng):
    h = int(rng.integers(0, 8))
    first, then = brackets(rng, *counts(rng)), brackets(rng, *counts(rng))
    first[:, h] = 1
    return plant(rng, h, first, then)
def setup_inputs_nest(rng):
    h = int(rng.integers(0, 8))
    n = np.arange(C)
    s = np.stack([np.ones(C), -np.ones(C), np.where(n < C // 2, 1.0, -1.0), np.where(n < C // 2, -1.0, 1.0), 1.0 - 2 * (n % 2), 2.0 * (n % 2) - 1,
                  np.where(n < 7 * C // 8, 1.0, -1.0), np.where(n < C - 1, 1.0, -1.0)] + [np.where((n >= c) & (n < (c + C) // 2), 1.0, -1.0) for c in (3 * C // 4, C - 4, C - 2)])
    o = []
    for t in range(2):
        k = np.zeros((N, 8), int)
        lead = rng.permutation(8) % 3 if N < 8 else np.zeros(8, int)
        deep = rng.permutation(np.repeat([8, 9, 10], [4, 2, 2]))
        for g in range(8):
            pairs = [[0, 1], [2, 3], [7, int(rng.integers(4, 6))]]
            l = int(lead[g])
            e = pairs[l] + [6, int(deep[g])] + pairs[(l + 1) % 3] + pairs[(l + 2) % 3]
            k[(int(rng.integers(0, N - 1)) + np.arange(N)) % N, g] = np.resize(e, N)
        o.append(s[k])
    o[0][:, h] = 1
    return plant(rng, h, *o)
def setup_inputs_turns(rng):
    h = int(rng.integers(0, 8))
    e = rng.permutation(8) % 2 == 0
    a, b = [rng.choice([T, 2 * T], (N, 8)) for i in range(2)]
    first, then = brackets(rng, np.where(e, a, 0), np.where(e, b, 0)), brackets(rng, np.where(e, 0, a), np.where(e, 0, b))
    first[:, h] = 1
    return plant(rng, h, first, then)
def setup_inputs_spread(rng):
    d = setup_inputs(rng)
    d["x"] = big(wide(rng, N, 128, 4 * C, cols=6), 1)
    return d
def check_inputs(d):
    b = []
    for k in ("x", "u", "v"):
        a = np.abs(d[k].astype(np.float32))
        if not (np.isfinite(a).all() and ((a == 0) | (a >= 2.0 ** -30) & (a <= 2.0 ** 30)).all()): b.append("a value of " + k)
    if (d["u"].astype(np.float32) != d["u"][:1].astype(np.float32)).any(): b.append("u differs between ranks")
    if (d["wc"] != d["wc"][:1]).any(): b.append("wc differs between ranks")
    s = [mx_ref.live(p) for p in d["ws"]]
    if any((p != s[0]).any() for p in s): b.append("ws differs between ranks")
    c = d["wc"] & 127
    if (c == 127).any(): b.append("a code of wc")
    zero, low, high = [emit(mx_ref.quantize(np.full((128, 16), k).astype(BF)))[1].astype(int) for k in (0.0, 2.0 ** -30, 2.0 ** 30)]
    full = (c.reshape(N, 16, 8, 512, 4) != 0).any(axis=(2, 4))
    l = np.stack(s).astype(int)
    if (((l < np.min(low)) | (l > np.max(high))) & (full | (l != zero[0, 0]))).any(): b.append("a scale of ws")
    return b
def reference(x, u, v, wc, ws):
    w = pk(wc[0], ws[0])
    w = [pick(w, np.arange(128 * b, 128 * b + 128)) for b in range(4)]
    qu = mx_ref.quantize(np.ascontiguousarray(u[0]))
    a = [mx_ref.quantize(np.ascontiguousarray(x[r])) for r in range(N)]
    none = np.zeros((128, 4 * T), BF)
    for t in range(R):
        p, get, mo, mc = [], [], [], []
        for r in range(N):
            s = mx_ref.matmul(qu, a[r])[::16]
            p.append(tile([mx_ref.matmul(w[b], a[r]) * np.float32(0.0625) for b in range(4)]))
            e, o, c = np.full((8, C), -1), np.full((8, T), -1), np.full((8, T), -1)
            for g in range(8):
                e[g], opens, closes = match(s[g] >= 0)
                o[g, :len(opens)] = opens
                c[g, :len(closes)] = closes
                e[g, closes] = C + np.arange(len(closes))
                e[g, opens] = C + T + np.arange(len(opens))
            get.append(e)
            mo.append(mx_ref.quantize(gcols(p[r], o)))
            mc.append(mx_ref.quantize(gcols(p[r], c)))
        d = decode(join(*mo, *mc)).astype(BF)
        for r in range(N):
            left = cut(d, r - 1, 4 * T) if r > 0 else none
            right = cut(d, N + r + 1, 4 * T) if r < N - 1 else none
            z = gcols(np.concatenate([p[r], left, right], axis=1), get[r])
            a[r] = mx_ref.quantize((p[r].astype(np.float32) + z.astype(np.float32)).astype(BF))
    y, oc, osc = np.zeros((N, 128, C), np.float32), np.zeros((N, 128, 4 * C), np.uint8), np.zeros((N, 16, C), np.uint8)
    for r in range(N):
        y[r] = mx_ref.matmul(mx_ref.quantize(np.ascontiguousarray(v[r])), a[r])
        oc[r], osc[r] = emit(a[r])
    return {"y": y, "oc": oc, "osc": osc}

@@ -1,0 +1,354 @@
+from concourse.bass import DstId, RemoteDMATransfer
+from concourse.mybir import dt, AluOpType, ActivationFunctionType
+
+A = AluOpType
+F = ActivationFunctionType
+C, TM, ROUNDS = 448, 96, 2
+HALF = C // 2
+Z0 = 196608.0
+BIG = 1.0e9
+POFF, ROFF, WINW = 113, 576, 688
+NP = 816
+
+Q4, U8 = "float8_e4m3fn_x4", "uint8"
+SCRATCH = {}
+
+
+def _sb(name, w, d):
+    SCRATCH[name] = ("sbuf", [128, w], d)
+
+
+for _n, _w, _d in [
+    ("xt", 4 * C, "bfloat16"), ("ut", 512, "bfloat16"), ("vt", 512, "bfloat16"),
+    ("wq", 512, Q4), ("wsc", 512, U8), ("uq", 128, Q4), ("us", 128, U8), ("uq2", 128, Q4), ("us2", 128, U8),
+    ("vq", 128, Q4), ("vs", 128, U8), ("et", 520, "bfloat16"), ("eq", 512, Q4), ("es", 512, U8),
+    ("pi", 8, "int32"), ("pj", 8, "int32"), ("cl", 16, "float32"), ("nf", 52, "float32"), ("lui", 8, "int32"),
+    ("lu", 8, "uint16"), ("lq", 52, "uint16"), ("lm", 52, "uint16"), ("lw", 52, "uint16"),
+    ("t0", 52, "float32"), ("wi", 52, "int32"), ("t1", 52, "float32"), ("t2", 52, "float32"), ("t3", 52, "float32"),
+    ("t4", 52, "float32"), ("t5", 52, "float32"), ("t6", 52, "float32"), ("t7", 52, "float32"), ("t8", 52, "float32"),
+    ("tf", 520, "float32"), ("wcf", C, "float16"), ("wcb", C, "float16"), ("wf", C, "float16"), ("wb", C, "float16"),
+    ("ky", 2 * C, "bfloat16"), ("kx", 336, "bfloat16"), ("ks", C, "bfloat16"), ("pat", 928, "bfloat16"),
+    ("mk", 928, "bfloat16"), ("zer", 16, "bfloat16"),
+    ("sg", C, "float16"), ("dp", C + 16, "float16"), ("mm", 2 * C, "bfloat16"), ("yy", 2 * C, "bfloat16"),
+    ("xx", 336, "bfloat16"), ("xs", 336, "float32"), ("lo", C, "float16"), ("nc", C, "float16"),
+    ("sm", C, "bfloat16"), ("mn", 32, "bfloat16"), ("ee", NP, "bfloat16"), ("rr", NP, "float32"),
+    ("ab", 96, "float32"), ("l2", C, "float16"), ("n2", C, "float16"), ("x1", C, "float16"), ("val", 480, "float16"),
+    ("tt", 928, "float16"), ("ss", 928, "float16"), ("ev", 32, "float32"), ("e1", 32, "float32"), ("e2", 32, "float32"),
+    ("zb", C, "bfloat16"), ("ysb", C, "float32"), ("pc", 4 * C, "bfloat16"),
+    ("win0", WINW, "bfloat16"), ("win1", WINW, "bfloat16"), ("win2", WINW, "bfloat16"), ("win3", WINW, "bfloat16"),
+    ("aq0", C, Q4), ("as0", C, U8),
+]:
+    _sb(_n, _w, _d)
+for _r in range(ROUNDS):
+    for _n, _w, _d in [
+        ("za", C + 16, "bfloat16"), ("c2", 2, "float32"), ("cb", 2, "float32"), ("ml", 12, "uint16"),
+        ("mt", 8 * TM, "bfloat16"), ("mq", 2 * TM, Q4), ("ms", 2 * TM, U8), ("lq_", 320, Q4), ("ls_", 320, U8),
+        ("dl", C, "bfloat16"), ("nd", C, "bfloat16"), ("ww", 128, "float32"), ("ze", NP, "float32"),
+        ("wn", NP, "float32"), ("el", 28, "uint16"), ("xn", 4 * C, "bfloat16"),
+    ]:
+        _sb(_n + str(_r), _w, _d)
+    _sb("aq%d" % (_r + 1), C, Q4)
+    _sb("as%d" % (_r + 1), C, U8)
+SCRATCH["pss"] = ("psum", [128, 1024], "float32")
+SCRATCH["psp"] = ("psum", [128, 2048], "float32")
+
+SEMAPHORES = ["cV", "cS", "cT", "cG", "cY", "arr0", "arr1", "loc", "st"] + ["k%d" % _i for _i in range(130)]
+
+
+def rank_program(g, core, T, topo):
+    rank = T.rank_of(core)
+    if rank is None:
+        return
+    n_ranks = len(T.cores)
+    has_l, has_r = rank > 0, rank < n_ranks - 1
+    Q = {"V": g.vector, "S": g.scalar, "T": g.tensor, "G": g, "Y": g.sync}
+    tot, seen, top, nk = {}, {}, {}, [0]
+
+    def fresh():
+        nk[0] += 1
+        return "k%d" % (nk[0] - 1)
+
+    def wait(q, toks):
+        for s in toks:
+            v = tot[s]
+            assert s[0] != "c" or s == "c" + q or q == "G"
+            if seen.get((q, s), 0) < v:
+                Q[q].wait_ge(T.sem[s], v)
+                seen[(q, s)] = v
+                top[s] = max(top.get(s, 0), v)
+
+    def op(q, f, deps=(), sem=None, n=1):
+        wait(q, deps)
+        s = "c" + q if sem is None else (fresh() if sem is True else sem)
+        f().then_inc(T.sem[s], n)
+        tot[s] = tot.get(s, 0) + n
+        return s
+
+    V, S, PE = g.vector, g.scalar, g.tensor
+    cV, cS = "cV", "cS"
+    tot[cV] = tot[cS] = 0
+
+    def ts(out, in0, s1, s2, o0, o1=None, deps=(cV,), sem=None):
+        if o1 is None:
+            return op("V", lambda: V.tensor_scalar(out, in0, s1, None, o0), deps, sem)
+        return op("V", lambda: V.tensor_scalar(out, in0, s1, s2, o0, o1), deps, sem)
+
+    def tt(out, a, b, o, deps=(cV,), sem=None):
+        return op("V", lambda: V.tensor_tensor(out, a, b, o), deps, sem)
+
+    def cp(out, a, deps=(cV,), sem=None):
+        return op("V", lambda: V.tensor_copy(out, a), deps, sem)
+
+    def scan(out, a, b, init, o0, o1, deps=(cV,), sem=None):
+        return op("V", lambda: V.tensor_tensor_scan(out, a, b, init, o0, o1), deps, sem)
+
+    def ms(ap, c, deps=(), sem=None):
+        return op("V", lambda: V.memset(ap, c), deps, sem)
+
+    def quant(oc, osc, src, deps=(cV,), sem=None):
+        return op("V", lambda: V.quantize_mx(oc, osc, src), deps, sem)
+
+    def act(out, a, fn, deps=(), sem=None, **kw):
+        return op("S", lambda: S.activation(out, a, fn, **kw), deps, sem)
+
+    def mm(out, lq, ls, rq, rs, deps=(), sem=True):
+        return op("T", lambda: PE.matmul_mx(out, lq, ls, rq, rs, True, True), deps, sem)
+
+    def dma(q, out, src, deps=(), sem=True):
+        return op(q, lambda: Q[q].dma_start(out, src), deps, sem, 16)
+
+    def iota(out, pat, base, cm, deps=(), sem=True, small=True):
+        if small:
+            return op("G", lambda: g.iota(out, pat, base, cm, allow_small_or_imprecise_dtypes=True), deps, sem)
+        return op("G", lambda: g.iota(out, pat, base, cm), deps, sem)
+
+    win = [T["win%d" % b] for b in range(4)]
+
+    d_u = dma("S", T.ut[:], T.u[:])
+    d_x = [dma("Y", T.xt[:, 4 * HALF * h:4 * HALF * (h + 1)], T.x[:, 4 * HALF * h:4 * HALF * (h + 1)]) for h in range(2)]
+    d_w = fresh()
+    dma("S", T.wq[:].bitcast(dt.uint8), T.wc[:], sem=d_w)
+    dma("S", T.wsc[:], T.ws[:], sem=d_w)
+    d_v = dma("Y", T.vt[:], T.v[:])
+
+    g_p = iota(T.pi[:, 0:1], [[0, 1]], 0, 1, small=False)
+    g_n = iota(T.nf[:], [[16, 52]], 0, 0)
+    g_lu = iota(T.lui[:], [[16, 8]], 0, 0, small=False)
+    g_t = iota(T.tf[:], [[1, 520]], 0, 0)
+    g_pat = iota(T.pat[:], [[0, 29], [1, 2], [0, 16]], 0, 0)
+    s_one = act(T.et[:], T.tf[:], F.Identity, deps=(g_t,), sem=True, scale=0.0, bias=1.0)
+    g_z = fresh()
+    for b in range(4):
+        act(win[b][:, 0:POFF], T.tf[:, 0:POFF], F.Copy, sem=g_z, scale=0.0)
+        act(win[b][:, POFF + C:WINW], T.tf[:, 0:WINW - POFF - C], F.Copy, sem=g_z, scale=0.0)
+    g_e = op("G", lambda: g.affine_select(T.et[:], T.et[:], [[-1, 520]], A.is_equal, 0.0, 3, 4), (s_one,), True)
+
+    ms(T.ky[:], BIG)
+    ms(T.kx[:], -BIG)
+    ms(T.ks[:], -BIG)
+    ms(T.mn[:], 0.0)
+    ms(T.zer[:], 0.0)
+    v_ww = fresh()
+    for r in range(ROUNDS):
+        ms(T["ww%d" % r][:], 0.0, sem=v_ww)
+    ts(T.pj[:, 0:1], T.pi[:, 0:1], 15, None, A.bitwise_and, deps=(g_p,))
+    ts(T.pj[:, 1:2], T.pi[:, 0:1], 4, 1, A.logical_shift_right, A.bitwise_and, deps=())
+    cp(T.lu[:], T.lui[:], deps=(g_lu,))
+    ms(T.ky[:, 0:2 * C:16], -16 * Z0, deps=(cV,))
+    ms(T.ks[:, 0:C:16], BIG)
+    for c in range(6):
+        ms(T.kx[:, 56 * c:56 * c + 56:28], 1024.0 * C * (c + 1))
+    cp(T.dp[:, 0:16], T.zer[:], deps=())
+    cp(T.val[:, 0:16], T.zer[:], deps=())
+    cp(T.val[:, 464:480], T.zer[:], deps=())
+    rho, col1, colc, colf, npar = [T.cl[:, i:i + 1] for i in range(5)]
+    v_cl = fresh()
+    cp(rho, T.pj[:, 0:1], deps=())
+    ts(col1, T.pj[:, 0:1], 64.0, Z0 - 480, A.mult, A.add, deps=())
+    ts(colc, T.pj[:, 0:1], -64.0, Z0 + 960 - 480, A.mult, A.add, deps=())
+    ts(colf, T.pj[:, 0:1], -1.0, TM - Z0 / 64, A.mult, A.add, deps=(), sem=v_cl)
+    ts(npar, T.pj[:, 1:2], -1.0, None, A.add, deps=(), sem=v_cl)
+    nn, wv, iv, bv = T.t0[:], T.t1[:], T.t2[:], T.t3[:]
+    ts(nn, T.nf[:], rho, None, A.add, deps=(cV, g_n))
+    ts(T.t4[:], nn, -14.0, 1.0 / 29, A.add, A.mult)
+    cp(T.wi[:], T.t4[:])
+    cp(wv, T.wi[:])
+    ts(T.t4[:], T.wi[:], -29.0, None, A.mult, deps=())
+    tt(iv, T.t4[:], nn, A.add)
+    ts(T.t5[:], wv, 35.0, None, A.add, deps=())
+    tt(T.t4[:], iv, wv, A.subtract)
+    ts(T.t6[:], iv, 0.0, None, A.is_equal, deps=())
+    ts(T.t7[:], wv, 64.0, None, A.add, deps=())
+    ts(bv, T.t4[:], 0.0, None, A.is_gt)
+    ts(T.t8[:], T.t4[:], 1.0, None, A.is_equal, deps=())
+    tt(T.t6[:], T.t6[:], T.t7[:], A.mult, deps=())
+    tt(T.t4[:], T.t4[:], iv, A.add)
+    tt(T.t8[:], T.t8[:], T.t5[:], A.mult, deps=())
+    tt(T.t7[:], wv, bv, A.add, deps=())
+    ts(T.t4[:], T.t4[:], -1.0, 30.0, A.mult, A.add)
+    v_l = fresh()
+    ts(T.lq[:], T.t7[:], 16.0, None, A.mult, deps=(), sem=v_l)
+    tt(T.t6[:], T.t6[:], T.t8[:], A.add, deps=())
+    ts(T.t5[:], bv, 32.0, None, A.mult, deps=())
+    tt(T.t4[:], T.t4[:], bv, A.mult)
+    tt(T.t6[:], T.t6[:], T.t5[:], A.add, deps=())
+    tt(T.t4[:], T.t4[:], iv, A.add)
+    cp(T.lm[:], T.t4[:])
+    tt(T.t6[:], T.t6[:], T.t4[:], A.add, deps=())
+    cp(T.lw[:], T.t6[:], sem=v_l)
+
+    quant(T.uq[:], T.us[:], T.ut[:], deps=(d_u,))
+    v_u = fresh()
+    cp(T.uq2[:].bitcast(dt.uint32), T.uq[:].bitcast(dt.uint32).indirect(T.lu[:, 0:8]), sem=v_u)
+    cp(T.us2[:], T.us[:].indirect(T.lu[:, 0:8]), deps=(), sem=v_u)
+    v_a = [quant(T.aq0[:, HALF * h:HALF * (h + 1)], T.as0[:, HALF * h:HALF * (h + 1)],
+                 T.xt[:, 4 * HALF * h:4 * HALF * (h + 1)], deps=(d_x[h],), sem=True) for h in range(2)]
+    ts(T.wcf[:], T.tf[:, 0:C], float(POFF), None, A.add, deps=(g_t,))
+    ts(T.wcb[:], T.wcf[:], -672.0, None, A.add)
+    cp(T.wf[:], T.wcf[:], deps=())
+    cp(T.wb[:], T.wcb[:])
+
+    def link(src_rank, dst_rank):
+        src, dst = T.cores[src_rank], T.cores[dst_rank]
+        eng = topo.engines(src, dst)
+        if 0 < src_rank < n_ranks - 1:
+            k = len(eng) // 2
+            eng = eng[:k] if dst_rank < src_rank else eng[k:]
+        rid, pid, _ = topo.addr(dst)
+        return DstId(rid=rid, pnc=pid), sum(1 << e for e in eng), len(eng)
+
+    tot["loc"] = 0
+    s_mk = None
+    v_e = v_v = None
+    prev_d = []
+    for r in range(ROUNDS):
+        R = lambda name: T[name + str(r)]
+        aq, asc = T["aq%d" % r], T["as%d" % r]
+        za, dl, ww = R("za"), R("dl"), R("ww")
+        t_s = [mm(T.pss[:, 512 * h:512 * h + HALF], T.uq2[:], T.us2[:], aq[:, HALF * h:HALF * (h + 1)],
+                  asc[:, HALF * h:HALF * (h + 1)], deps=(v_u, v_a[h])) for h in range(2)]
+        t_p = [mm(T.psp[:, 512 * b:512 * b + C], T.wq[:, 128 * b:128 * b + 128], T.wsc[:, 128 * b:128 * b + 128],
+                  aq[:], asc[:], deps=[d_w] + prev_d) for b in range(4)]
+        s_p = fresh()
+        for b in range(4):
+            act(win[b][:, POFF:POFF + C], T.psp[:, 512 * b:512 * b + C], F.Copy, deps=(t_p[b],), sem=s_p, scale=0.0625)
+        d_p = fresh()
+        for b in range(4):
+            dma("Y", T.pc[:, C * b:C * (b + 1)], win[b][:, POFF:POFF + C], deps=(s_p,), sem=d_p)
+        for h in range(2):
+            ts(T.sg[:, HALF * h:HALF * (h + 1)], T.pss[:, 512 * h:512 * h + HALF], 0.0, 0.5, A.is_ge, A.subtract,
+               deps=(t_s[h],))
+        scan(T.dp[:, 1:C + 1], T.sg[:], T.sg[:], 0.0, A.add, A.add)
+        v_c2 = ts(R("c2")[:, 0:1], T.dp[:, C:C + 1], -64.0, colc, A.mult, A.add, sem=True)
+        v_z = ts(za[:, 0:C + 1], T.dp[:, 0:C + 1], 64.0, col1, A.mult, A.add, deps=(), sem=True)
+        ts(T.zb[:], T.dp[:, C - 1::-1], 64.0, R("c2")[:, 0:1], A.mult, A.add, deps=(v_c2,))
+        scan(T.mm[:, 0:C], za[:, 1:C + 1], za[:, 1:C + 1], Z0, A.min, A.min, deps=(v_z,))
+        scan(T.mm[:, C:2 * C], T.zb[:], T.zb[:], Z0, A.min, A.min)
+        scan(T.yy[:], T.ky[:], T.mm[:], 0.0, A.min, A.add)
+        for c in range(6):
+            ts(T.xx[:, 56 * c:56 * c + 56], T.yy[:, 15:2 * C:16], -16384.0 * (c + 1), -16384.0 * c, A.max, A.min,
+               deps=(cV,) if c == 0 else ())
+        scan(T.xs[:], T.kx[:], T.xx[:], 0.0, A.max, A.add)
+        v_ml = fresh()
+        ts(R("ml")[:, 0:6], T.xs[:, 27:336:56], 1.0 / 1024, 1.0, A.mult, A.add, sem=v_ml)
+        ts(R("ml")[:, 6:12], T.xs[:, 335:54:-56], -1.0 / 1024, float(C), A.mult, A.add, deps=(), sem=v_ml)
+        act(R("cb")[:, 0:1], R("c2")[:, 0:1], F.Identity, deps=(v_c2,), scale=1.0 / 64, bias=88.5 - Z0 / 32)
+        s_ze = act(R("ze")[:], za[:, 0:C + 1].indirect(T.lq[:, 0:51]), F.Identity, deps=(v_z, v_l), sem=True, bias=-64.0)
+        s_m = fresh()
+        for b in range(4):
+            act(R("mt")[:, b:8 * TM:4], win[b][:, POFF - 1:POFF + C + 1].indirect(R("ml")[:, 0:12]), F.Copy,
+                deps=(v_ml, s_p, g_z), sem=s_m)
+        act(ww[:, 64:92], za[:, 0:C:16], F.Relu, deps=(v_ww, v_cl), scale=1.0 / 64, bias=colf)
+        act(ww[:, 96:124], za[:, 16:C + 1:16], F.Relu, deps=(cS,), scale=1.0 / 64, bias=R("cb")[:, 0:1])
+        v_dl = tt(dl[:], za[:, 1:C + 1], za[:, 0:C], A.subtract, deps=(), sem=True)
+        scan(T.sm[:], T.ks[:], za[:, 0:C], 0.0, A.max, A.min, deps=())
+        scan(T.lo[:], dl[:], T.wcf[:], float(POFF - 1), A.max, A.min, deps=(v_dl,))
+        scan(T.nc[:, ::-1], dl[:, ::-1], T.wcb[:, ::-1], -111.0, A.min, A.max, deps=())
+        v_w = fresh()
+        cp(ww[:, 1:29], T.lo[:, 15:C:16], deps=(cV, v_ww), sem=v_w)
+        ts(ww[:, 33:61], T.nc[:, 0:C:16], -1.0, None, A.mult, deps=(), sem=v_w)
+        tt(T.mn[:, 1:29], T.sm[:, 15:C:16], za[:, 16:C + 1:16], A.min, deps=())
+        tt(T.ab[:, 0:28], dl[:, 0:C:16], T.wcf[:, 0:C:16], A.min, deps=())
+        tt(T.ab[:, 32:60], dl[:, 15:C:16], T.wcb[:, 15:C:16], A.max, deps=())
+        s_wn = act(R("wn")[:], ww[:].indirect(T.lw[:, 0:51]), F.Copy, deps=(cS, v_w), sem=True, scale=-1.0)
+        s_nd = act(R("nd")[:], dl[:], F.Copy, deps=(v_dl,), sem=True, scale=-1.0)
+        if r == 0:
+            s_mk = act(T.mk[:], T.pat[:], F.Abs, deps=(g_pat, v_cl), sem=True, bias=npar)
+        lqb, lsb = R("lq_"), R("ls_")
+        v_fill = []
+        if r == 0:
+            v_e = fresh()
+            for b in range(4):
+                quant(T.eq[:, 128 * b:128 * b + 128], T.es[:, 128 * b:128 * b + 128], T.et[:, 3 - b:515 - b],
+                      deps=(g_e,), sem=v_e)
+        else:
+            v_v = quant(T.vq[:], T.vs[:], T.vt[:], deps=(d_v,), sem=True)
+        if not (has_l and has_r):
+            f0 = 2 * TM if has_r else TM
+            v_fill = [quant(lqb[:, f0:f0 + 128], lsb[:, f0:f0 + 128], T.xt[:, 0:512], deps=(), sem=True)]
+        v_mq = quant(R("mq")[:], R("ms")[:], R("mt")[:], deps=(s_m,), sem=True)
+        arr = "arr%d" % r
+        wait("G", (v_mq,))
+        for kind in range(2):
+            trs = []
+            for other, s0, d0 in ((rank - 1, 0, TM), (rank + 1, TM, 0)):
+                if 0 <= other < n_ranks:
+                    did, mask, ne = link(rank, other)
+                    if kind == 0:
+                        src, dst = R("mq")[:, s0:s0 + TM].bitcast(dt.uint8), lqb[:, d0:d0 + TM].bitcast(dt.uint8)
+                    else:
+                        src, dst = R("ms")[:, s0:s0 + TM], lsb[:, d0:d0 + TM]
+                    trs.append(RemoteDMATransfer(dst_ids=[did], dma_engine_mask=mask, remote_sem=T.sem[arr], src=src, dst=dst))
+                    tot["loc"] += ne
+            g.remote_dma_fused(trs, local_sem=T.sem["loc"])
+        tot[arr] = sum(2 * link(o, rank)[2] for o in (rank - 1, rank + 1) if 0 <= o < n_ranks)
+        l0 = 0 if has_l else TM
+        ln = 2 * TM if has_l and has_r else 128
+        prev_d = []
+        for b in range(4):
+            t_d = mm(T.psp[:, 512 * b:512 * b + ln], T.eq[:, 128 * b:128 * b + 128], T.es[:, 128 * b:128 * b + 128],
+                     lqb[:, l0:l0 + ln], lsb[:, l0:l0 + ln], deps=[v_e, s_p, arr] + v_fill)
+            s_d = fresh()
+            if has_l:
+                act(win[b][:, 1:1 + TM], T.psp[:, 512 * b:512 * b + TM], F.Copy, deps=(t_d, g_z), sem=s_d)
+            if has_r:
+                o = 512 * b + (TM if has_l else 0)
+                act(win[b][:, ROFF:ROFF + TM], T.psp[:, o:o + TM], F.Copy, deps=(t_d, g_z), sem=s_d)
+            prev_d.append(s_d)
+        tt(T.ee[:], T.mn[:].indirect(T.lm[:, 0:51]), R("ze")[:], A.subtract, deps=(cV, s_ze))
+        scan(T.rr[:], T.ee[:], R("wn")[:], 0.0, A.min, A.max, deps=(cV, s_wn))
+        ts(T.ab[:, 64:92], T.rr[:, 0:812:30], -1.0, None, A.mult)
+        tt(T.wb[:, 15:C:16], T.rr[:, 28:812:29], T.ab[:, 32:60], A.min, deps=())
+        tt(T.wf[:, 0:C:16], T.ab[:, 64:92], T.ab[:, 0:28], A.max)
+        scan(T.n2[:, ::-1], dl[:, ::-1], T.wb[:, ::-1], -111.0, A.min, A.max, deps=())
+        scan(T.l2[:], dl[:], T.wf[:], float(POFF - 1), A.max, A.min)
+        tt(T.x1[:], T.l2[:], R("nd")[:], A.min, deps=(cV, s_nd))
+        tt(T.val[:, 16:464], T.x1[:], T.n2[:], A.max)
+        op("V", lambda: V.transpose(T.tt[:, 0:C], T.val[:, 16:464]), (cV,))
+        op("V", lambda: V.transpose(T.tt[:, C:928], T.val[:]), ())
+        scan(T.ss[:], T.tt[:], T.mk[:], 0.0, A.add, A.mult, deps=(cV, s_mk))
+        tt(T.ev[:, 0:28:2], T.ss[:, 15:448:32], T.ss[:, 479:896:32], A.add)
+        tt(T.ev[:, 1:28:2], T.ss[:, 495:928:32], T.ss[:, 31:448:32], A.add, deps=())
+        ts(T.e1[:, 0:28], T.ev[:, 0:28], 0.0, 672.0, A.is_lt, A.mult)
+        tt(T.e2[:, 0:28], T.e1[:, 0:28], T.ev[:, 0:28], A.add)
+        cp(R("el")[:], T.e2[:, 0:28])
+        xn, nq, ns = R("xn"), T["aq%d" % (r + 1)], T["as%d" % (r + 1)]
+        v_a = []
+        for h in range(2):
+            a0, a1 = HALF * h, HALF * (h + 1)
+            for b in range(4):
+                tt(xn[:, 4 * a0 + b:4 * a1:4], win[b][:].indirect(R("el")[:, 14 * h:14 * h + 14]),
+                   T.pc[:, C * b + a0:C * b + a1], A.add,
+                   deps=((cV,) if h + b == 0 else ()) + (prev_d[b], s_p, g_z, d_p))
+            v_a.append(quant(nq[:, a0:a1], ns[:, a0:a1], xn[:, 4 * a0:4 * a1], sem=True))
+
+    fq, fs = T["aq%d" % ROUNDS], T["as%d" % ROUNDS]
+    for h in range(2):
+        a0, a1 = HALF * h, HALF * (h + 1)
+        t_y = mm(T.pss[:, 512 * h:512 * h + HALF], T.vq[:], T.vs[:], fq[:, a0:a1], fs[:, a0:a1], deps=(v_v, v_a[h]))
+        dma("Y", T.oc[:, 4 * a0:4 * a1], fq[:, a0:a1].bitcast(dt.uint8), deps=(v_a[h],), sem="st")
+        s_y = act(T.ysb[:, a0:a1], T.pss[:, 512 * h:512 * h + HALF], F.Copy, deps=(t_y,), sem=True)
+        dma("S", T.y[:, a0:a1], T.ysb[:, a0:a1], deps=(s_y,), sem="st")
+    for k in range(4):
+        dma("Y", T.osc[4 * k:4 * k + 4, :], fs[32 * k:32 * k + 4, :], deps=(), sem="st")
+    wait("G", [s for s in tot if top.get(s, 0) < tot[s]])

@@ -26,13 +26,14 @@ for _n, _w, _d in [
     ("lu", 8, "uint16"), ("lq", 52, "uint16"), ("lm", 52, "uint16"), ("lw", 52, "uint16"),
     ("t0", 52, "float32"), ("wi", 52, "int32"), ("t1", 52, "float32"), ("t2", 52, "float32"), ("t3", 52, "float32"),
     ("t4", 52, "float32"), ("t5", 52, "float32"), ("t6", 52, "float32"), ("t7", 52, "float32"), ("t8", 52, "float32"),
+    ("t9", 52, "float32"),
     ("tf", 520, "float32"), ("wcf", C, "float16"), ("wcb", C, "float16"), ("wf", C, "float16"), ("wb", C, "float16"),
     ("ky", 2 * C, "bfloat16"), ("kx", 336, "bfloat16"), ("ks", C, "bfloat16"), ("pat", 928, "bfloat16"),
     ("mk", 928, "bfloat16"), ("zer", 16, "bfloat16"),
     ("sg", C, "float16"), ("dp", C + 16, "float16"), ("mm", 2 * C, "bfloat16"), ("yy", 2 * C, "bfloat16"),
     ("xx", 336, "bfloat16"), ("xs", 336, "float32"), ("lo", C, "float16"), ("nc", C, "float16"),
-    ("sm", C, "bfloat16"), ("mn", 32, "bfloat16"), ("ee", NP, "bfloat16"), ("rr", NP, "float32"),
-    ("ab", 96, "float32"), ("l2", C, "float16"), ("n2", C, "float16"), ("x1", C, "float16"), ("val", 480, "float16"),
+    ("sm", C, "bfloat16"), ("mn", 32, "bfloat16"), ("ee", NP, "bfloat16"), ("rr", NP, "float16"),
+    ("ab", 128, "float32"), ("l2", C, "float16"), ("n2", C, "float16"), ("x1", C, "float16"), ("val", 480, "float16"),
     ("tt", 928, "float16"), ("ss", 928, "float16"), ("ev", 32, "float32"), ("e1", 32, "float32"), ("e2", 32, "float32"),
     ("zb", C, "bfloat16"), ("ysb", C, "float32"), ("pc", 4 * C, "bfloat16"),
     ("win0", WINW, "bfloat16"), ("win1", WINW, "bfloat16"), ("win2", WINW, "bfloat16"), ("win3", WINW, "bfloat16"),
@@ -44,7 +45,7 @@ for _r in range(ROUNDS):
         ("za", C + 16, "bfloat16"), ("c2", 2, "float32"), ("cb", 2, "float32"), ("ml", 12, "uint16"),
         ("mt", 8 * TM, "bfloat16"), ("mq", 2 * TM, Q4), ("ms", 2 * TM, U8), ("lq_", 320, Q4), ("ls_", 320, U8),
         ("dl", C, "bfloat16"), ("nd", C, "bfloat16"), ("ww", 128, "float32"), ("ze", NP, "float32"),
-        ("wn", NP, "float32"), ("el", 28, "uint16"), ("xn", 4 * C, "bfloat16"),
+        ("wn", NP, "bfloat16"), ("el", 28, "uint16"), ("xn", 4 * C, "bfloat16"),
     ]:
         _sb(_n + str(_r), _w, _d)
     _sb("aq%d" % (_r + 1), C, Q4)
@@ -127,9 +128,8 @@ def rank_program(g, core, T, topo):
     d_u = dma("S", T.ut[:], T.u[:])
     d_x = [dma("Y", T.xt[:, 4 * HALF * h:4 * HALF * (h + 1)], T.x[:, 4 * HALF * h:4 * HALF * (h + 1)]) for h in range(2)]
     d_w = fresh()
-    dma("S", T.wq[:].bitcast(dt.uint8), T.wc[:], sem=d_w)
-    dma("S", T.wsc[:], T.ws[:], sem=d_w)
-    d_v = dma("Y", T.vt[:], T.v[:])
+    dma("Y", T.wq[:].bitcast(dt.uint8), T.wc[:], sem=d_w)
+    dma("Y", T.wsc[:], T.ws[:], sem=d_w)
 
     g_p = iota(T.pi[:, 0:1], [[0, 1]], 0, 1, small=False)
     g_n = iota(T.nf[:], [[16, 52]], 0, 0)
@@ -141,61 +141,42 @@ def rank_program(g, core, T, topo):
     for b in range(4):
         act(win[b][:, 0:POFF], T.tf[:, 0:POFF], F.Copy, sem=g_z, scale=0.0)
         act(win[b][:, POFF + C:WINW], T.tf[:, 0:WINW - POFF - C], F.Copy, sem=g_z, scale=0.0)
+    v_ww = fresh()
+    for r in range(ROUNDS):
+        act(T["ww%d" % r][:], T.tf[:, 0:128], F.Copy, sem=v_ww, scale=0.0)
     g_e = op("G", lambda: g.affine_select(T.et[:], T.et[:], [[-1, 520]], A.is_equal, 0.0, 3, 4), (s_one,), True)
 
     ms(T.ky[:], BIG)
     ms(T.kx[:], -BIG)
-    ms(T.ks[:], -BIG)
-    ms(T.mn[:], 0.0)
     ms(T.zer[:], 0.0)
-    v_ww = fresh()
-    for r in range(ROUNDS):
-        ms(T["ww%d" % r][:], 0.0, sem=v_ww)
     ts(T.pj[:, 0:1], T.pi[:, 0:1], 15, None, A.bitwise_and, deps=(g_p,))
     ts(T.pj[:, 1:2], T.pi[:, 0:1], 4, 1, A.logical_shift_right, A.bitwise_and, deps=())
+    ts(T.pj[:, 2:3], T.pi[:, 0:1], 1, None, A.bitwise_and, deps=())
     cp(T.lu[:], T.lui[:], deps=(g_lu,))
-    ms(T.ky[:, 0:2 * C:16], -16 * Z0, deps=(cV,))
-    ms(T.ks[:, 0:C:16], BIG)
+    rho, col1, colc, colf, npar, sig, usig = [T.cl[:, i:i + 1] for i in range(7)]
+    cp(rho, T.pj[:, 0:1])
+    ms(T.ky[:, 0:2 * C:16], -16 * Z0)
     for c in range(6):
         ms(T.kx[:, 56 * c:56 * c + 56:28], 1024.0 * C * (c + 1))
     cp(T.dp[:, 0:16], T.zer[:], deps=())
-    cp(T.val[:, 0:16], T.zer[:], deps=())
-    cp(T.val[:, 464:480], T.zer[:], deps=())
-    rho, col1, colc, colf, npar = [T.cl[:, i:i + 1] for i in range(5)]
     v_cl = fresh()
-    cp(rho, T.pj[:, 0:1], deps=())
     ts(col1, T.pj[:, 0:1], 64.0, Z0 - 480, A.mult, A.add, deps=())
     ts(colc, T.pj[:, 0:1], -64.0, Z0 + 960 - 480, A.mult, A.add, deps=())
     ts(colf, T.pj[:, 0:1], -1.0, TM - Z0 / 64, A.mult, A.add, deps=(), sem=v_cl)
     ts(npar, T.pj[:, 1:2], -1.0, None, A.add, deps=(), sem=v_cl)
-    nn, wv, iv, bv = T.t0[:], T.t1[:], T.t2[:], T.t3[:]
+    ts(sig, T.pj[:, 2:3], 48.0, None, A.add, deps=(), sem=v_cl)
+    ts(usig, T.pj[:, 2:3], -1.0, -47.0, A.mult, A.add, deps=(), sem=v_cl)
+    nn, wv, iv, bv, dv = T.t0[:], T.t1[:], T.t2[:], T.t3[:], T.t9[:]
     ts(nn, T.nf[:], rho, None, A.add, deps=(cV, g_n))
     ts(T.t4[:], nn, -14.0, 1.0 / 29, A.add, A.mult)
     cp(T.wi[:], T.t4[:])
     cp(wv, T.wi[:])
     ts(T.t4[:], T.wi[:], -29.0, None, A.mult, deps=())
     tt(iv, T.t4[:], nn, A.add)
-    ts(T.t5[:], wv, 35.0, None, A.add, deps=())
-    tt(T.t4[:], iv, wv, A.subtract)
-    ts(T.t6[:], iv, 0.0, None, A.is_equal, deps=())
-    ts(T.t7[:], wv, 64.0, None, A.add, deps=())
-    ts(bv, T.t4[:], 0.0, None, A.is_gt)
-    ts(T.t8[:], T.t4[:], 1.0, None, A.is_equal, deps=())
-    tt(T.t6[:], T.t6[:], T.t7[:], A.mult, deps=())
-    tt(T.t4[:], T.t4[:], iv, A.add)
-    tt(T.t8[:], T.t8[:], T.t5[:], A.mult, deps=())
-    tt(T.t7[:], wv, bv, A.add, deps=())
-    ts(T.t4[:], T.t4[:], -1.0, 30.0, A.mult, A.add)
-    v_l = fresh()
-    ts(T.lq[:], T.t7[:], 16.0, None, A.mult, deps=(), sem=v_l)
-    tt(T.t6[:], T.t6[:], T.t8[:], A.add, deps=())
-    ts(T.t5[:], bv, 32.0, None, A.mult, deps=())
-    tt(T.t4[:], T.t4[:], bv, A.mult)
-    tt(T.t6[:], T.t6[:], T.t5[:], A.add, deps=())
-    tt(T.t4[:], T.t4[:], iv, A.add)
-    cp(T.lm[:], T.t4[:])
-    tt(T.t6[:], T.t6[:], T.t4[:], A.add, deps=())
-    cp(T.lw[:], T.t6[:], sem=v_l)
+    tt(dv, iv, wv, A.subtract)
+    ts(bv, dv, 0.0, None, A.is_gt)
+    tt(T.t7[:], wv, bv, A.add)
+    v_lq = ts(T.lq[:], T.t7[:], 16.0, None, A.mult, sem=True)
 
     quant(T.uq[:], T.us[:], T.ut[:], deps=(d_u,))
     v_u = fresh()
@@ -204,9 +185,32 @@ def rank_program(g, core, T, topo):
     v_a = [quant(T.aq0[:, HALF * h:HALF * (h + 1)], T.as0[:, HALF * h:HALF * (h + 1)],
                  T.xt[:, 4 * HALF * h:4 * HALF * (h + 1)], deps=(d_x[h],), sem=True) for h in range(2)]
     ts(T.wcf[:], T.tf[:, 0:C], float(POFF), None, A.add, deps=(g_t,))
-    ts(T.wcb[:], T.wcf[:], -672.0, None, A.add)
-    cp(T.wf[:], T.wcf[:], deps=())
-    cp(T.wb[:], T.wcb[:])
+
+    def late_constants():
+        ts(T.wcb[:], T.wcf[:], -672.0, None, A.add, deps=())
+        cp(T.wf[:], T.wcf[:], deps=())
+        ts(T.wb[:], T.wcf[:], -672.0, None, A.add, deps=())
+        ms(T.ks[:], -BIG)
+        ms(T.mn[:], 0.0)
+        cp(T.val[:, 0:16], T.zer[:], deps=())
+        cp(T.val[:, 464:480], T.zer[:], deps=())
+        ts(T.t5[:], wv, 35.0, None, A.add, deps=())
+        ts(T.t6[:], iv, 0.0, None, A.is_equal, deps=())
+        ts(T.t0[:], wv, 64.0, None, A.add, deps=())
+        ts(T.t8[:], dv, 1.0, None, A.is_equal, deps=())
+        tt(T.t4[:], dv, iv, A.add, deps=())
+        ms(T.ks[:, 0:C:16], BIG, deps=(cV,))
+        tt(T.t6[:], T.t6[:], T.t0[:], A.mult, deps=())
+        tt(T.t8[:], T.t8[:], T.t5[:], A.mult, deps=())
+        ts(T.t4[:], T.t4[:], -1.0, 30.0, A.mult, A.add, deps=())
+        tt(T.t6[:], T.t6[:], T.t8[:], A.add)
+        ts(T.t5[:], bv, 32.0, None, A.mult, deps=())
+        tt(T.t4[:], T.t4[:], bv, A.mult, deps=())
+        tt(T.t6[:], T.t6[:], T.t5[:], A.add)
+        tt(T.t4[:], T.t4[:], iv, A.add, deps=())
+        cp(T.lm[:], T.t4[:])
+        tt(T.t6[:], T.t6[:], T.t4[:], A.add, deps=())
+        return cp(T.lw[:], T.t6[:], sem=True)
 
     def link(src_rank, dst_rank):
         src, dst = T.cores[src_rank], T.cores[dst_rank]
@@ -218,13 +222,13 @@ def rank_program(g, core, T, topo):
         return DstId(rid=rid, pnc=pid), sum(1 << e for e in eng), len(eng)
 
     tot["loc"] = 0
-    s_mk = None
-    v_e = v_v = None
+    s_mk = v_lw = v_e = v_v = d_v = None
     prev_d = []
     for r in range(ROUNDS):
         R = lambda name: T[name + str(r)]
         aq, asc = T["aq%d" % r], T["as%d" % r]
         za, dl, ww = R("za"), R("dl"), R("ww")
+        lqb, lsb = R("lq_"), R("ls_")
         t_s = [mm(T.pss[:, 512 * h:512 * h + HALF], T.uq2[:], T.us2[:], aq[:, HALF * h:HALF * (h + 1)],
                   asc[:, HALF * h:HALF * (h + 1)], deps=(v_u, v_a[h])) for h in range(2)]
         t_p = [mm(T.psp[:, 512 * b:512 * b + C], T.wq[:, 128 * b:128 * b + 128], T.wsc[:, 128 * b:128 * b + 128],
@@ -232,18 +236,17 @@ def rank_program(g, core, T, topo):
         s_p = fresh()
         for b in range(4):
             act(win[b][:, POFF:POFF + C], T.psp[:, 512 * b:512 * b + C], F.Copy, deps=(t_p[b],), sem=s_p, scale=0.0625)
-        d_p = fresh()
-        for b in range(4):
-            dma("Y", T.pc[:, C * b:C * (b + 1)], win[b][:, POFF:POFF + C], deps=(s_p,), sem=d_p)
+        if r == 0:
+            d_v = dma("Y", T.vt[:], T.v[:], deps=(d_w,))
         for h in range(2):
             ts(T.sg[:, HALF * h:HALF * (h + 1)], T.pss[:, 512 * h:512 * h + HALF], 0.0, 0.5, A.is_ge, A.subtract,
                deps=(t_s[h],))
         scan(T.dp[:, 1:C + 1], T.sg[:], T.sg[:], 0.0, A.add, A.add)
         v_c2 = ts(R("c2")[:, 0:1], T.dp[:, C:C + 1], -64.0, colc, A.mult, A.add, sem=True)
         v_z = ts(za[:, 0:C + 1], T.dp[:, 0:C + 1], 64.0, col1, A.mult, A.add, deps=(), sem=True)
-        ts(T.zb[:], T.dp[:, C - 1::-1], 64.0, R("c2")[:, 0:1], A.mult, A.add, deps=(v_c2,))
+        v_zb = ts(T.zb[:], T.dp[:, C - 1::-1], 64.0, R("c2")[:, 0:1], A.mult, A.add, deps=(v_c2,), sem=True)
         scan(T.mm[:, 0:C], za[:, 1:C + 1], za[:, 1:C + 1], Z0, A.min, A.min, deps=(v_z,))
-        scan(T.mm[:, C:2 * C], T.zb[:], T.zb[:], Z0, A.min, A.min)
+        scan(T.mm[:, C:2 * C], T.zb[:], T.zb[:], Z0, A.min, A.min, deps=(v_zb,))
         scan(T.yy[:], T.ky[:], T.mm[:], 0.0, A.min, A.add)
         for c in range(6):
             ts(T.xx[:, 56 * c:56 * c + 56], T.yy[:, 15:2 * C:16], -16384.0 * (c + 1), -16384.0 * c, A.max, A.min,
@@ -252,29 +255,60 @@ def rank_program(g, core, T, topo):
         v_ml = fresh()
         ts(R("ml")[:, 0:6], T.xs[:, 27:336:56], 1.0 / 1024, 1.0, A.mult, A.add, sem=v_ml)
         ts(R("ml")[:, 6:12], T.xs[:, 335:54:-56], -1.0 / 1024, float(C), A.mult, A.add, deps=(), sem=v_ml)
-        act(R("cb")[:, 0:1], R("c2")[:, 0:1], F.Identity, deps=(v_c2,), scale=1.0 / 64, bias=88.5 - Z0 / 32)
-        s_ze = act(R("ze")[:], za[:, 0:C + 1].indirect(T.lq[:, 0:51]), F.Identity, deps=(v_z, v_l), sem=True, bias=-64.0)
+        s_ze = fresh()
+        act(R("cb")[:, 0:1], R("c2")[:, 0:1], F.Identity, deps=(v_c2,), scale=1.0 / 64, bias=89.5 - Z0 / 32)
+        act(R("ze")[:, 0:416], za[:, 0:C + 1].indirect(T.lq[:, 0:26]), F.Identity, deps=(v_z, v_lq), sem=s_ze, bias=-64.0)
         s_m = fresh()
         for b in range(4):
             act(R("mt")[:, b:8 * TM:4], win[b][:, POFF - 1:POFF + C + 1].indirect(R("ml")[:, 0:12]), F.Copy,
                 deps=(v_ml, s_p, g_z), sem=s_m)
+        act(R("ze")[:, 416:NP], za[:, 0:C + 1].indirect(T.lq[:, 26:51]), F.Identity, sem=s_ze, bias=-64.0)
         act(ww[:, 64:92], za[:, 0:C:16], F.Relu, deps=(v_ww, v_cl), scale=1.0 / 64, bias=colf)
         act(ww[:, 96:124], za[:, 16:C + 1:16], F.Relu, deps=(cS,), scale=1.0 / 64, bias=R("cb")[:, 0:1])
+
+        def send():
+            v_mq = quant(R("mq")[:], R("ms")[:], R("mt")[:], deps=(s_m,), sem=True)
+            wait("G", (v_mq,))
+            for kind in range(2):
+                trs = []
+                for other, s0, d0 in ((rank - 1, 0, TM), (rank + 1, TM, 0)):
+                    if 0 <= other < n_ranks:
+                        did, mask, ne = link(rank, other)
+                        if kind == 0:
+                            src, dst = R("mq")[:, s0:s0 + TM].bitcast(dt.uint8), lqb[:, d0:d0 + TM].bitcast(dt.uint8)
+                        else:
+                            src, dst = R("ms")[:, s0:s0 + TM], lsb[:, d0:d0 + TM]
+                        trs.append(RemoteDMATransfer(dst_ids=[did], dma_engine_mask=mask, remote_sem=T.sem[arr],
+                                                     src=src, dst=dst))
+                        tot["loc"] += ne
+                g.remote_dma_fused(trs, local_sem=T.sem["loc"])
+            tot[arr] = sum(2 * link(o, rank)[2] for o in (rank - 1, rank + 1) if 0 <= o < n_ranks)
+
+        arr = "arr%d" % r
+        if r == 0:
+            v_lw = late_constants()
+            send()
         v_dl = tt(dl[:], za[:, 1:C + 1], za[:, 0:C], A.subtract, deps=(), sem=True)
         scan(T.sm[:], T.ks[:], za[:, 0:C], 0.0, A.max, A.min, deps=())
         scan(T.lo[:], dl[:], T.wcf[:], float(POFF - 1), A.max, A.min, deps=(v_dl,))
         scan(T.nc[:, ::-1], dl[:, ::-1], T.wcb[:, ::-1], -111.0, A.min, A.max, deps=())
+        if r > 0:
+            send()
         v_w = fresh()
         cp(ww[:, 1:29], T.lo[:, 15:C:16], deps=(cV, v_ww), sem=v_w)
-        ts(ww[:, 33:61], T.nc[:, 0:C:16], -1.0, None, A.mult, deps=(), sem=v_w)
+        ts(ww[:, 33:61], T.nc[:, 0:C:16], -1.0, 1.0, A.mult, A.add, deps=(), sem=v_w)
         tt(T.mn[:, 1:29], T.sm[:, 15:C:16], za[:, 16:C + 1:16], A.min, deps=())
         tt(T.ab[:, 0:28], dl[:, 0:C:16], T.wcf[:, 0:C:16], A.min, deps=())
         tt(T.ab[:, 32:60], dl[:, 15:C:16], T.wcb[:, 15:C:16], A.max, deps=())
-        s_wn = act(R("wn")[:], ww[:].indirect(T.lw[:, 0:51]), F.Copy, deps=(cS, v_w), sem=True, scale=-1.0)
+        s_wn = act(R("wn")[:], ww[:].indirect(T.lw[:, 0:51]), F.Identity, deps=(cS, v_w, v_lw), sem=True,
+                   scale=-1.0, bias=sig)
         s_nd = act(R("nd")[:], dl[:], F.Copy, deps=(v_dl,), sem=True, scale=-1.0)
         if r == 0:
             s_mk = act(T.mk[:], T.pat[:], F.Abs, deps=(g_pat, v_cl), sem=True, bias=npar)
-        lqb, lsb = R("lq_"), R("ls_")
+        s_pc = fresh()
+        for b in range(4):
+            act(T.pc[:, C * b:C * (b + 1)], win[b][:, POFF:POFF + C], F.Copy, sem=s_pc)
+        tt(T.ee[:], T.mn[:].indirect(T.lm[:, 0:51]), R("ze")[:], A.subtract, deps=(cV, s_ze))
         v_fill = []
         if r == 0:
             v_e = fresh()
@@ -286,22 +320,6 @@ def rank_program(g, core, T, topo):
         if not (has_l and has_r):
             f0 = 2 * TM if has_r else TM
             v_fill = [quant(lqb[:, f0:f0 + 128], lsb[:, f0:f0 + 128], T.xt[:, 0:512], deps=(), sem=True)]
-        v_mq = quant(R("mq")[:], R("ms")[:], R("mt")[:], deps=(s_m,), sem=True)
-        arr = "arr%d" % r
-        wait("G", (v_mq,))
-        for kind in range(2):
-            trs = []
-            for other, s0, d0 in ((rank - 1, 0, TM), (rank + 1, TM, 0)):
-                if 0 <= other < n_ranks:
-                    did, mask, ne = link(rank, other)
-                    if kind == 0:
-                        src, dst = R("mq")[:, s0:s0 + TM].bitcast(dt.uint8), lqb[:, d0:d0 + TM].bitcast(dt.uint8)
-                    else:
-                        src, dst = R("ms")[:, s0:s0 + TM], lsb[:, d0:d0 + TM]
-                    trs.append(RemoteDMATransfer(dst_ids=[did], dma_engine_mask=mask, remote_sem=T.sem[arr], src=src, dst=dst))
-                    tot["loc"] += ne
-            g.remote_dma_fused(trs, local_sem=T.sem["loc"])
-        tot[arr] = sum(2 * link(o, rank)[2] for o in (rank - 1, rank + 1) if 0 <= o < n_ranks)
         l0 = 0 if has_l else TM
         ln = 2 * TM if has_l and has_r else 128
         prev_d = []
@@ -315,15 +333,15 @@ def rank_program(g, core, T, topo):
                 o = 512 * b + (TM if has_l else 0)
                 act(win[b][:, ROFF:ROFF + TM], T.psp[:, o:o + TM], F.Copy, deps=(t_d, g_z), sem=s_d)
             prev_d.append(s_d)
-        tt(T.ee[:], T.mn[:].indirect(T.lm[:, 0:51]), R("ze")[:], A.subtract, deps=(cV, s_ze))
         scan(T.rr[:], T.ee[:], R("wn")[:], 0.0, A.min, A.max, deps=(cV, s_wn))
-        ts(T.ab[:, 64:92], T.rr[:, 0:812:30], -1.0, None, A.mult)
-        tt(T.wb[:, 15:C:16], T.rr[:, 28:812:29], T.ab[:, 32:60], A.min, deps=())
+        ts(T.ab[:, 64:92], T.rr[:, 0:812:30], -1.0, sig, A.mult, A.add, deps=(cV, v_cl))
+        ts(T.ab[:, 96:124], T.rr[:, 28:812:29], usig, 0.0, A.add, A.min, deps=())
         tt(T.wf[:, 0:C:16], T.ab[:, 64:92], T.ab[:, 0:28], A.max)
-        scan(T.n2[:, ::-1], dl[:, ::-1], T.wb[:, ::-1], -111.0, A.min, A.max, deps=())
+        v_wb = tt(T.wb[:, 15:C:16], T.ab[:, 96:124], T.ab[:, 32:60], A.min, deps=(), sem=True)
         scan(T.l2[:], dl[:], T.wf[:], float(POFF - 1), A.max, A.min)
+        v_n2 = scan(T.n2[:, ::-1], dl[:, ::-1], T.wb[:, ::-1], -111.0, A.min, A.max, deps=(v_wb,), sem=True)
         tt(T.x1[:], T.l2[:], R("nd")[:], A.min, deps=(cV, s_nd))
-        tt(T.val[:, 16:464], T.x1[:], T.n2[:], A.max)
+        tt(T.val[:, 16:464], T.x1[:], T.n2[:], A.max, deps=(cV, v_n2))
         op("V", lambda: V.transpose(T.tt[:, 0:C], T.val[:, 16:464]), (cV,))
         op("V", lambda: V.transpose(T.tt[:, C:928], T.val[:]), ())
         scan(T.ss[:], T.tt[:], T.mk[:], 0.0, A.add, A.mult, deps=(cV, s_mk))
@@ -333,14 +351,24 @@ def rank_program(g, core, T, topo):
         tt(T.e2[:, 0:28], T.e1[:, 0:28], T.ev[:, 0:28], A.add)
         cp(R("el")[:], T.e2[:, 0:28])
         xn, nq, ns = R("xn"), T["aq%d" % (r + 1)], T["as%d" % (r + 1)]
-        v_a = []
-        for h in range(2):
+        v_g = [fresh(), fresh()]
+
+        def gather(h, b):
             a0, a1 = HALF * h, HALF * (h + 1)
-            for b in range(4):
-                tt(xn[:, 4 * a0 + b:4 * a1:4], win[b][:].indirect(R("el")[:, 14 * h:14 * h + 14]),
-                   T.pc[:, C * b + a0:C * b + a1], A.add,
-                   deps=((cV,) if h + b == 0 else ()) + (prev_d[b], s_p, g_z, d_p))
-            v_a.append(quant(nq[:, a0:a1], ns[:, a0:a1], xn[:, 4 * a0:4 * a1], sem=True))
+            tt(xn[:, 4 * a0 + b:4 * a1:4], win[b][:].indirect(R("el")[:, 14 * h:14 * h + 14]),
+               T.pc[:, C * b + a0:C * b + a1], A.add, deps=(cV, prev_d[b], s_p, g_z, s_pc), sem=v_g[h])
+
+        def requant(h):
+            a0, a1 = HALF * h, HALF * (h + 1)
+            return quant(nq[:, a0:a1], ns[:, a0:a1], xn[:, 4 * a0:4 * a1], deps=(v_g[h],), sem=True)
+
+        for b in range(4):
+            gather(0, b)
+        gather(1, 0)
+        v_a = [requant(0)]
+        for b in range(1, 4):
+            gather(1, b)
+        v_a.append(requant(1))
 
     fq, fs = T["aq%d" % ROUNDS], T["as%d" % ROUNDS]
     for h in range(2):

@@ -9,6 +9,7 @@ Z0 = 196608.0
 BIG = 1.0e9
 POFF, ROFF, WINW = 113, 576, 688
 NP = 816
+NROT = 6
 
 Q4, U8 = "float8_e4m3fn_x4", "uint8"
 SCRATCH = {}
@@ -26,9 +27,11 @@ for _n, _w, _d in [
     ("lu", 8, "uint16"), ("lq", 52, "uint16"), ("lm", 52, "uint16"), ("lw", 52, "uint16"),
     ("t0", 52, "float32"), ("wi", 52, "int32"), ("t1", 52, "float32"), ("t2", 52, "float32"), ("t3", 52, "float32"),
     ("t4", 52, "float32"), ("t5", 52, "float32"), ("t6", 52, "float32"), ("t7", 52, "float32"), ("t8", 52, "float32"),
-    ("t9", 52, "float32"),
-    ("tf", 520, "float32"), ("wcf", C, "float16"), ("wcb", C, "float16"), ("wf", C, "float16"), ("wb", C, "float16"),
-    ("ky", 2 * C, "bfloat16"), ("kx", 336, "bfloat16"), ("ks", C, "bfloat16"), ("pat", 928, "bfloat16"),
+    ("t9", 52, "float32"), ("ta", 52, "float32"), ("tb", 52, "float32"), ("tc", 52, "float32"), ("td", 52, "float32"),
+    ("te", 52, "float32"), ("tg", 52, "float32"), ("th", 52, "float32"), ("ti", 52, "float32"), ("tj", 52, "float32"),
+    ("tk", 52, "float32"), ("tl", 52, "float32"),
+    ("tf", 520, "float32"), ("wf", C, "float16"), ("wb", C, "float16"),
+    ("ky", C, "bfloat16"), ("kx", 336, "bfloat16"), ("ks", C, "bfloat16"), ("pat", 928, "bfloat16"),
     ("mk", 928, "bfloat16"), ("zer", 16, "bfloat16"),
     ("sg", C, "float16"), ("dp", C + 16, "float16"), ("mm", 2 * C, "bfloat16"), ("yy", 2 * C, "bfloat16"),
     ("xx", 336, "bfloat16"), ("xs", 336, "float32"), ("lo", C, "float16"), ("nc", C, "float16"),
@@ -53,7 +56,8 @@ for _r in range(ROUNDS):
 SCRATCH["pss"] = ("psum", [128, 1024], "float32")
 SCRATCH["psp"] = ("psum", [128, 2048], "float32")
 
-SEMAPHORES = ["cV", "cS", "cT", "cG", "cY", "arr0", "arr1", "loc", "st"] + ["k%d" % _i for _i in range(130)]
+SEMAPHORES = (["cV", "cS", "arr0", "arr1", "loc", "st"] + ["cV%d" % _i for _i in range(NROT)]
+              + ["k%d" % _i for _i in range(130)])
 
 
 def rank_program(g, core, T, topo):
@@ -63,7 +67,7 @@ def rank_program(g, core, T, topo):
     n_ranks = len(T.cores)
     has_l, has_r = rank > 0, rank < n_ranks - 1
     Q = {"V": g.vector, "S": g.scalar, "T": g.tensor, "G": g, "Y": g.sync}
-    tot, seen, top, nk = {}, {}, {}, [0]
+    tot, seen, top, nk, nrot = {}, {}, {}, [0], [0]
 
     def fresh():
         nk[0] += 1
@@ -72,7 +76,7 @@ def rank_program(g, core, T, topo):
     def wait(q, toks):
         for s in toks:
             v = tot[s]
-            assert s[0] != "c" or s == "c" + q or q == "G"
+            assert s[0] != "c" or s[1] == q or q == "G"
             if seen.get((q, s), 0) < v:
                 Q[q].wait_ge(T.sem[s], v)
                 seen[(q, s)] = v
@@ -80,33 +84,43 @@ def rank_program(g, core, T, topo):
 
     def op(q, f, deps=(), sem=None, n=1):
         wait(q, deps)
-        s = "c" + q if sem is None else (fresh() if sem is True else sem)
+        if sem is None and q == "V":
+            s = "cV%d" % (nrot[0] % NROT)
+            nrot[0] += 1
+        else:
+            s = "c" + q if sem is None else (fresh() if sem is True else sem)
         f().then_inc(T.sem[s], n)
         tot[s] = tot.get(s, 0) + n
         return s
 
     V, S, PE = g.vector, g.scalar, g.tensor
-    cV, cS = "cV", "cS"
-    tot[cV] = tot[cS] = 0
+    cS = "cS"
+    tot[cS] = 0
+    ALLV = ["cV%d" % i for i in range(NROT)]
+    for s in ALLV:
+        tot[s] = 0
 
-    def ts(out, in0, s1, s2, o0, o1=None, deps=(cV,), sem=None):
+    def ts(out, in0, s1, s2, o0, o1=None, deps=(), sem=None):
         if o1 is None:
             return op("V", lambda: V.tensor_scalar(out, in0, s1, None, o0), deps, sem)
         return op("V", lambda: V.tensor_scalar(out, in0, s1, s2, o0, o1), deps, sem)
 
-    def tt(out, a, b, o, deps=(cV,), sem=None):
+    def tt(out, a, b, o, deps=(), sem=None):
         return op("V", lambda: V.tensor_tensor(out, a, b, o), deps, sem)
 
-    def cp(out, a, deps=(cV,), sem=None):
+    def cp(out, a, deps=(), sem=None):
         return op("V", lambda: V.tensor_copy(out, a), deps, sem)
 
-    def scan(out, a, b, init, o0, o1, deps=(cV,), sem=None):
+    def scan(out, a, b, init, o0, o1, deps=(), sem=None):
         return op("V", lambda: V.tensor_tensor_scan(out, a, b, init, o0, o1), deps, sem)
+
+    def tr(out, a, deps=(), sem=None):
+        return op("V", lambda: V.transpose(out, a), deps, sem)
 
     def ms(ap, c, deps=(), sem=None):
         return op("V", lambda: V.memset(ap, c), deps, sem)
 
-    def quant(oc, osc, src, deps=(cV,), sem=None):
+    def quant(oc, osc, src, deps=(), sem=None):
         return op("V", lambda: V.quantize_mx(oc, osc, src), deps, sem)
 
     def act(out, a, fn, deps=(), sem=None, **kw):
@@ -130,10 +144,11 @@ def rank_program(g, core, T, topo):
     d_w = fresh()
     dma("Y", T.wq[:].bitcast(dt.uint8), T.wc[:], sem=d_w)
     dma("Y", T.wsc[:], T.ws[:], sem=d_w)
+    d_v = dma("Y", T.vt[:], T.v[:], deps=(d_w,))
 
     g_p = iota(T.pi[:, 0:1], [[0, 1]], 0, 1, small=False)
-    g_n = iota(T.nf[:], [[16, 52]], 0, 0)
     g_lu = iota(T.lui[:], [[16, 8]], 0, 0, small=False)
+    g_n = iota(T.nf[:], [[16, 52]], 0, 0)
     g_t = iota(T.tf[:], [[1, 520]], 0, 0)
     g_pat = iota(T.pat[:], [[0, 29], [1, 2], [0, 16]], 0, 0)
     s_one = act(T.et[:], T.tf[:], F.Identity, deps=(g_t,), sem=True, scale=0.0, bias=1.0)
@@ -146,71 +161,77 @@ def rank_program(g, core, T, topo):
         act(T["ww%d" % r][:], T.tf[:, 0:128], F.Copy, sem=v_ww, scale=0.0)
     g_e = op("G", lambda: g.affine_select(T.et[:], T.et[:], [[-1, 520]], A.is_equal, 0.0, 3, 4), (s_one,), True)
 
+    ms(T.zer[:], 0.0)
     ms(T.ky[:], BIG)
     ms(T.kx[:], -BIG)
-    ms(T.zer[:], 0.0)
+    ms(T.ks[:], -BIG)
+    ms(T.mn[:], 0.0)
     ts(T.pj[:, 0:1], T.pi[:, 0:1], 15, None, A.bitwise_and, deps=(g_p,))
-    ts(T.pj[:, 1:2], T.pi[:, 0:1], 4, 1, A.logical_shift_right, A.bitwise_and, deps=())
-    ts(T.pj[:, 2:3], T.pi[:, 0:1], 1, None, A.bitwise_and, deps=())
+    ts(T.pj[:, 1:2], T.pi[:, 0:1], 4, 1, A.logical_shift_right, A.bitwise_and)
+    ts(T.pj[:, 2:3], T.pi[:, 0:1], 1, None, A.bitwise_and)
     cp(T.lu[:], T.lui[:], deps=(g_lu,))
     rho, col1, colc, colf, npar, sig, usig = [T.cl[:, i:i + 1] for i in range(7)]
-    cp(rho, T.pj[:, 0:1])
-    ms(T.ky[:, 0:2 * C:16], -16 * Z0)
-    for c in range(6):
-        ms(T.kx[:, 56 * c:56 * c + 56:28], 1024.0 * C * (c + 1))
-    cp(T.dp[:, 0:16], T.zer[:], deps=())
+    k0 = cp(rho, T.pj[:, 0:1], deps=ALLV)
     v_cl = fresh()
-    ts(col1, T.pj[:, 0:1], 64.0, Z0 - 480, A.mult, A.add, deps=())
-    ts(colc, T.pj[:, 0:1], -64.0, Z0 + 960 - 480, A.mult, A.add, deps=())
-    ts(colf, T.pj[:, 0:1], -1.0, TM - Z0 / 64, A.mult, A.add, deps=(), sem=v_cl)
-    ts(npar, T.pj[:, 1:2], -1.0, None, A.add, deps=(), sem=v_cl)
-    ts(sig, T.pj[:, 2:3], 48.0, None, A.add, deps=(), sem=v_cl)
-    ts(usig, T.pj[:, 2:3], -1.0, -47.0, A.mult, A.add, deps=(), sem=v_cl)
+    ts(col1, T.pj[:, 0:1], 64.0, Z0 - 480, A.mult, A.add)
     nn, wv, iv, bv, dv = T.t0[:], T.t1[:], T.t2[:], T.t3[:], T.t9[:]
-    ts(nn, T.nf[:], rho, None, A.add, deps=(cV, g_n))
-    ts(T.t4[:], nn, -14.0, 1.0 / 29, A.add, A.mult)
-    cp(T.wi[:], T.t4[:])
-    cp(wv, T.wi[:])
-    ts(T.t4[:], T.wi[:], -29.0, None, A.mult, deps=())
-    tt(iv, T.t4[:], nn, A.add)
-    tt(dv, iv, wv, A.subtract)
-    ts(bv, dv, 0.0, None, A.is_gt)
-    tt(T.t7[:], wv, bv, A.add)
-    v_lq = ts(T.lq[:], T.t7[:], 16.0, None, A.mult, sem=True)
+    k1 = ts(nn, T.nf[:], rho, None, A.add, deps=(k0, g_n))
+    ts(colc, T.pj[:, 0:1], -64.0, Z0 + 960 - 480, A.mult, A.add)
+    k2 = ts(T.t4[:], nn, -14.0, 1.0 / 29, A.add, A.mult, deps=(k1,))
+    ts(colf, T.pj[:, 0:1], -1.0, TM - Z0 / 64, A.mult, A.add, sem=v_cl)
+    k3 = cp(T.wi[:], T.t4[:], deps=(k2,))
+    ts(npar, T.pj[:, 1:2], -1.0, None, A.add, sem=v_cl)
+    k4 = ts(T.t5[:], T.wi[:], -29.0, None, A.mult, deps=(k3,))
+    k5 = cp(wv, T.wi[:])
+    k6 = tt(iv, T.t5[:], nn, A.add, deps=(k4,))
+    ts(sig, T.pj[:, 2:3], 48.0, None, A.add, sem=v_cl)
+    k7 = tt(dv, iv, wv, A.subtract, deps=(k5, k6))
+    ts(usig, T.pj[:, 2:3], -1.0, -47.0, A.mult, A.add, sem=v_cl)
+    k8 = ts(bv, dv, 0.0, None, A.is_gt, deps=(k7,))
+    ms(T.ky[:, 0:C:16], -16 * Z0)
+    k9 = tt(T.t7[:], wv, bv, A.add, deps=(k8,))
+    cp(T.dp[:, 0:16], T.zer[:])
+    v_lq = ts(T.lq[:], T.t7[:], 16.0, None, A.mult, deps=(k9,), sem=True)
 
-    quant(T.uq[:], T.us[:], T.ut[:], deps=(d_u,))
+    k0 = quant(T.uq[:], T.us[:], T.ut[:], deps=(d_u,))
+    ms(T.ks[:, 0:C:16], BIG)
     v_u = fresh()
-    cp(T.uq2[:].bitcast(dt.uint32), T.uq[:].bitcast(dt.uint32).indirect(T.lu[:, 0:8]), sem=v_u)
-    cp(T.us2[:], T.us[:].indirect(T.lu[:, 0:8]), deps=(), sem=v_u)
+    cp(T.uq2[:].bitcast(dt.uint32), T.uq[:].bitcast(dt.uint32).indirect(T.lu[:, 0:8]), deps=(k0,), sem=v_u)
+    cp(T.us2[:], T.us[:].indirect(T.lu[:, 0:8]), sem=v_u)
     v_a = [quant(T.aq0[:, HALF * h:HALF * (h + 1)], T.as0[:, HALF * h:HALF * (h + 1)],
                  T.xt[:, 4 * HALF * h:4 * HALF * (h + 1)], deps=(d_x[h],), sem=True) for h in range(2)]
-    ts(T.wcf[:], T.tf[:, 0:C], float(POFF), None, A.add, deps=(g_t,))
+    for c in range(6):
+        ms(T.kx[:, 56 * c:56 * c + 56:28], 1024.0 * C * (c + 1))
+
+    late = [
+        lambda: ts(T.ta[:], wv, 35.0, None, A.add),
+        lambda: ts(T.t6[:], iv, 0.0, None, A.is_equal),
+        lambda: ts(T.tb[:], wv, 64.0, None, A.add),
+        lambda: ts(T.t8[:], dv, 1.0, None, A.is_equal),
+        lambda: tt(T.tc[:], dv, iv, A.add),
+        lambda: ts(T.td[:], bv, 32.0, None, A.mult),
+    ]
+
+    def fill():
+        if late:
+            late.pop(0)()
 
     def late_constants():
-        ts(T.wcb[:], T.wcf[:], -672.0, None, A.add, deps=())
-        cp(T.wf[:], T.wcf[:], deps=())
-        ts(T.wb[:], T.wcf[:], -672.0, None, A.add, deps=())
-        ms(T.ks[:], -BIG)
-        ms(T.mn[:], 0.0)
-        cp(T.val[:, 0:16], T.zer[:], deps=())
-        cp(T.val[:, 464:480], T.zer[:], deps=())
-        ts(T.t5[:], wv, 35.0, None, A.add, deps=())
-        ts(T.t6[:], iv, 0.0, None, A.is_equal, deps=())
-        ts(T.t0[:], wv, 64.0, None, A.add, deps=())
-        ts(T.t8[:], dv, 1.0, None, A.is_equal, deps=())
-        tt(T.t4[:], dv, iv, A.add, deps=())
-        ms(T.ks[:, 0:C:16], BIG, deps=(cV,))
-        tt(T.t6[:], T.t6[:], T.t0[:], A.mult, deps=())
-        tt(T.t8[:], T.t8[:], T.t5[:], A.mult, deps=())
-        ts(T.t4[:], T.t4[:], -1.0, 30.0, A.mult, A.add, deps=())
-        tt(T.t6[:], T.t6[:], T.t8[:], A.add)
-        ts(T.t5[:], bv, 32.0, None, A.mult, deps=())
-        tt(T.t4[:], T.t4[:], bv, A.mult, deps=())
-        tt(T.t6[:], T.t6[:], T.t5[:], A.add)
-        tt(T.t4[:], T.t4[:], iv, A.add, deps=())
-        cp(T.lm[:], T.t4[:])
-        tt(T.t6[:], T.t6[:], T.t4[:], A.add, deps=())
-        return cp(T.lw[:], T.t6[:], sem=True)
+        a = tt(T.te[:], T.t6[:], T.tb[:], A.mult, deps=ALLV)
+        b = tt(T.tg[:], T.t8[:], T.ta[:], A.mult)
+        c = ts(T.th[:], T.tc[:], -1.0, 30.0, A.mult, A.add)
+        d = tt(T.ti[:], T.te[:], T.tg[:], A.add, deps=(a, b))
+        e = tt(T.tj[:], T.th[:], bv, A.mult, deps=(c,))
+        f = tt(T.tk[:], T.ti[:], T.td[:], A.add, deps=(d,))
+        h = tt(T.tl[:], T.tj[:], iv, A.add, deps=(e,))
+        k = ts(T.wf[:], T.tf[:, 0:C], float(POFF), None, A.add, deps=(g_t,))
+        cp(T.lm[:], T.tl[:], deps=(h,))
+        m = tt(T.t4[:], T.tk[:], T.tl[:], A.add, deps=(f,))
+        ts(T.wb[:], T.wf[:], -672.0, None, A.add, deps=(k,))
+        lw = cp(T.lw[:], T.t4[:], deps=(m,), sem=True)
+        cp(T.val[:, 0:16], T.zer[:])
+        cp(T.val[:, 464:480], T.zer[:])
+        return lw
 
     def link(src_rank, dst_rank):
         src, dst = T.cores[src_rank], T.cores[dst_rank]
@@ -222,7 +243,7 @@ def rank_program(g, core, T, topo):
         return DstId(rid=rid, pnc=pid), sum(1 << e for e in eng), len(eng)
 
     tot["loc"] = 0
-    s_mk = v_lw = v_e = v_v = d_v = None
+    s_mk = v_lw = v_e = v_v = None
     prev_d = []
     for r in range(ROUNDS):
         R = lambda name: T[name + str(r)]
@@ -236,25 +257,35 @@ def rank_program(g, core, T, topo):
         s_p = fresh()
         for b in range(4):
             act(win[b][:, POFF:POFF + C], T.psp[:, 512 * b:512 * b + C], F.Copy, deps=(t_p[b],), sem=s_p, scale=0.0625)
-        if r == 0:
-            d_v = dma("Y", T.vt[:], T.v[:], deps=(d_w,))
+        wait("V", ALLV)
+        k_s = []
         for h in range(2):
-            ts(T.sg[:, HALF * h:HALF * (h + 1)], T.pss[:, 512 * h:512 * h + HALF], 0.0, 0.5, A.is_ge, A.subtract,
-               deps=(t_s[h],))
-        scan(T.dp[:, 1:C + 1], T.sg[:], T.sg[:], 0.0, A.add, A.add)
-        v_c2 = ts(R("c2")[:, 0:1], T.dp[:, C:C + 1], -64.0, colc, A.mult, A.add, sem=True)
-        v_z = ts(za[:, 0:C + 1], T.dp[:, 0:C + 1], 64.0, col1, A.mult, A.add, deps=(), sem=True)
-        v_zb = ts(T.zb[:], T.dp[:, C - 1::-1], 64.0, R("c2")[:, 0:1], A.mult, A.add, deps=(v_c2,), sem=True)
-        scan(T.mm[:, 0:C], za[:, 1:C + 1], za[:, 1:C + 1], Z0, A.min, A.min, deps=(v_z,))
-        scan(T.mm[:, C:2 * C], T.zb[:], T.zb[:], Z0, A.min, A.min, deps=(v_zb,))
-        scan(T.yy[:], T.ky[:], T.mm[:], 0.0, A.min, A.add)
-        for c in range(6):
-            ts(T.xx[:, 56 * c:56 * c + 56], T.yy[:, 15:2 * C:16], -16384.0 * (c + 1), -16384.0 * c, A.max, A.min,
-               deps=(cV,) if c == 0 else ())
-        scan(T.xs[:], T.kx[:], T.xx[:], 0.0, A.max, A.add)
+            k_s.append(ts(T.sg[:, HALF * h:HALF * (h + 1)], T.pss[:, 512 * h:512 * h + HALF], 0.0, 0.5, A.is_ge,
+                          A.subtract, deps=(t_s[h],)))
+            if r > 0 and h == 0:
+                v_v = quant(T.vq[:], T.vs[:], T.vt[:], deps=(d_v,), sem=True)
+                ts(T.wf[:, 0:C:16], T.tf[:, 0:C:16], float(POFF), None, A.add)
+        if r > 0:
+            ts(T.wb[:, 15:C:16], T.tf[:, 15:C:16], POFF - 672.0, None, A.add)
+        fill()
+        k_d = scan(T.dp[:, 1:C + 1], T.sg[:], T.sg[:], 0.0, A.add, A.add, deps=k_s)
+        fill()
+        v_c2 = ts(R("c2")[:, 0:1], T.dp[:, C:C + 1], -64.0, colc, A.mult, A.add, deps=(k_d,), sem=True)
+        v_z = ts(za[:, 0:C + 1], T.dp[:, 0:C + 1], 64.0, col1, A.mult, A.add, sem=True)
+        k_zb = ts(T.zb[:], T.dp[:, C - 1::-1], 64.0, R("c2")[:, 0:1], A.mult, A.add, deps=(v_c2,))
+        k_m0 = scan(T.mm[:, 0:C], za[:, 1:C + 1], za[:, 1:C + 1], Z0, A.min, A.min, deps=(v_z,))
+        k_m1 = scan(T.mm[:, C:2 * C], T.zb[:], T.zb[:], Z0, A.min, A.min, deps=(k_zb,))
+        k_y0 = scan(T.yy[:, 0:C], T.ky[:], T.mm[:, 0:C], 0.0, A.min, A.add, deps=(k_m0,))
+        k_y1 = scan(T.yy[:, C:2 * C], T.ky[:], T.mm[:, C:2 * C], 0.0, A.min, A.add, deps=(k_m1,))
+        k_sm = scan(T.sm[:], T.ks[:], za[:, 0:C], 0.0, A.max, A.min, sem=True)
+        k_c = [ts(T.xx[:, 56 * c:56 * c + 56], T.yy[:, 15:2 * C:16], -16384.0 * (c + 1), -16384.0 * c, A.max, A.min,
+                  deps=(k_y0, k_y1) if c == 0 else ()) for c in range(6)]
+        k_xa = scan(T.xs[:, 0:224], T.kx[:, 0:224], T.xx[:, 0:224], 0.0, A.max, A.add, deps=k_c[0:4], sem=True)
+        k_xb = scan(T.xs[:, 224:336], T.kx[:, 224:336], T.xx[:, 224:336], 0.0, A.max, A.add, deps=k_c[4:6], sem=True)
+        k_mn = tt(T.mn[:, 1:29], T.sm[:, 15:C:16], za[:, 16:C + 1:16], A.min, deps=(k_sm,), sem=True)
         v_ml = fresh()
-        ts(R("ml")[:, 0:6], T.xs[:, 27:336:56], 1.0 / 1024, 1.0, A.mult, A.add, sem=v_ml)
-        ts(R("ml")[:, 6:12], T.xs[:, 335:54:-56], -1.0 / 1024, float(C), A.mult, A.add, deps=(), sem=v_ml)
+        ts(R("ml")[:, 0:6], T.xs[:, 27:336:56], 1.0 / 1024, 1.0, A.mult, A.add, deps=(k_xa, k_xb), sem=v_ml)
+        ts(R("ml")[:, 6:12], T.xs[:, 335:54:-56], -1.0 / 1024, float(C), A.mult, A.add, sem=v_ml)
         s_ze = fresh()
         act(R("cb")[:, 0:1], R("c2")[:, 0:1], F.Identity, deps=(v_c2,), scale=1.0 / 64, bias=89.5 - Z0 / 32)
         act(R("ze")[:, 0:416], za[:, 0:C + 1].indirect(T.lq[:, 0:26]), F.Identity, deps=(v_z, v_lq), sem=s_ze, bias=-64.0)
@@ -285,21 +316,23 @@ def rank_program(g, core, T, topo):
             tot[arr] = sum(2 * link(o, rank)[2] for o in (rank - 1, rank + 1) if 0 <= o < n_ranks)
 
         arr = "arr%d" % r
+        v_dl = tt(dl[:], za[:, 1:C + 1], za[:, 0:C], A.subtract, sem=True)
         if r == 0:
+            while late:
+                fill()
             v_lw = late_constants()
             send()
-        v_dl = tt(dl[:], za[:, 1:C + 1], za[:, 0:C], A.subtract, deps=(), sem=True)
-        scan(T.sm[:], T.ks[:], za[:, 0:C], 0.0, A.max, A.min, deps=())
-        scan(T.lo[:], dl[:], T.wcf[:], float(POFF - 1), A.max, A.min, deps=(v_dl,))
-        scan(T.nc[:, ::-1], dl[:, ::-1], T.wcb[:, ::-1], -111.0, A.min, A.max, deps=())
+            wait("V", ALLV)
+        k_lo = scan(T.lo[:], dl[:], T.wf[:], float(POFF - 1), A.max, A.min, deps=[v_dl] + ALLV)
+        k_nc = scan(T.nc[:, ::-1], dl[:, ::-1], T.wb[:, ::-1], -111.0, A.min, A.max)
+        v_w = fresh()
+        cp(ww[:, 1:29], T.lo[:, 15:C:16], deps=(k_lo, v_ww), sem=v_w)
+        ts(ww[:, 33:61], T.nc[:, 0:C:16], -1.0, 1.0, A.mult, A.add, deps=(k_nc,), sem=v_w)
+        k_ab = fresh()
+        tt(T.ab[:, 0:28], dl[:, 0:C:16], T.wf[:, 0:C:16], A.min, sem=k_ab)
+        tt(T.ab[:, 32:60], dl[:, 15:C:16], T.wb[:, 15:C:16], A.max, sem=k_ab)
         if r > 0:
             send()
-        v_w = fresh()
-        cp(ww[:, 1:29], T.lo[:, 15:C:16], deps=(cV, v_ww), sem=v_w)
-        ts(ww[:, 33:61], T.nc[:, 0:C:16], -1.0, 1.0, A.mult, A.add, deps=(), sem=v_w)
-        tt(T.mn[:, 1:29], T.sm[:, 15:C:16], za[:, 16:C + 1:16], A.min, deps=())
-        tt(T.ab[:, 0:28], dl[:, 0:C:16], T.wcf[:, 0:C:16], A.min, deps=())
-        tt(T.ab[:, 32:60], dl[:, 15:C:16], T.wcb[:, 15:C:16], A.max, deps=())
         s_wn = act(R("wn")[:], ww[:].indirect(T.lw[:, 0:51]), F.Identity, deps=(cS, v_w, v_lw), sem=True,
                    scale=-1.0, bias=sig)
         s_nd = act(R("nd")[:], dl[:], F.Copy, deps=(v_dl,), sem=True, scale=-1.0)
@@ -308,18 +341,16 @@ def rank_program(g, core, T, topo):
         s_pc = fresh()
         for b in range(4):
             act(T.pc[:, C * b:C * (b + 1)], win[b][:, POFF:POFF + C], F.Copy, sem=s_pc)
-        tt(T.ee[:], T.mn[:].indirect(T.lm[:, 0:51]), R("ze")[:], A.subtract, deps=(cV, s_ze))
+        k_e = tt(T.ee[:], T.mn[:].indirect(T.lm[:, 0:51]), R("ze")[:], A.subtract, deps=(k_mn, s_ze))
         v_fill = []
         if r == 0:
             v_e = fresh()
             for b in range(4):
                 quant(T.eq[:, 128 * b:128 * b + 128], T.es[:, 128 * b:128 * b + 128], T.et[:, 3 - b:515 - b],
                       deps=(g_e,), sem=v_e)
-        else:
-            v_v = quant(T.vq[:], T.vs[:], T.vt[:], deps=(d_v,), sem=True)
         if not (has_l and has_r):
             f0 = 2 * TM if has_r else TM
-            v_fill = [quant(lqb[:, f0:f0 + 128], lsb[:, f0:f0 + 128], T.xt[:, 0:512], deps=(), sem=True)]
+            v_fill = [quant(lqb[:, f0:f0 + 128], lsb[:, f0:f0 + 128], T.xt[:, 0:512], sem=True)]
         l0 = 0 if has_l else TM
         ln = 2 * TM if has_l and has_r else 128
         prev_d = []
@@ -333,30 +364,34 @@ def rank_program(g, core, T, topo):
                 o = 512 * b + (TM if has_l else 0)
                 act(win[b][:, ROFF:ROFF + TM], T.psp[:, o:o + TM], F.Copy, deps=(t_d, g_z), sem=s_d)
             prev_d.append(s_d)
-        scan(T.rr[:], T.ee[:], R("wn")[:], 0.0, A.min, A.max, deps=(cV, s_wn))
-        ts(T.ab[:, 64:92], T.rr[:, 0:812:30], -1.0, sig, A.mult, A.add, deps=(cV, v_cl))
-        ts(T.ab[:, 96:124], T.rr[:, 28:812:29], usig, 0.0, A.add, A.min, deps=())
-        tt(T.wf[:, 0:C:16], T.ab[:, 64:92], T.ab[:, 0:28], A.max)
-        v_wb = tt(T.wb[:, 15:C:16], T.ab[:, 96:124], T.ab[:, 32:60], A.min, deps=(), sem=True)
-        scan(T.l2[:], dl[:], T.wf[:], float(POFF - 1), A.max, A.min)
-        v_n2 = scan(T.n2[:, ::-1], dl[:, ::-1], T.wb[:, ::-1], -111.0, A.min, A.max, deps=(v_wb,), sem=True)
-        tt(T.x1[:], T.l2[:], R("nd")[:], A.min, deps=(cV, s_nd))
-        tt(T.val[:, 16:464], T.x1[:], T.n2[:], A.max, deps=(cV, v_n2))
-        op("V", lambda: V.transpose(T.tt[:, 0:C], T.val[:, 16:464]), (cV,))
-        op("V", lambda: V.transpose(T.tt[:, C:928], T.val[:]), ())
-        scan(T.ss[:], T.tt[:], T.mk[:], 0.0, A.add, A.mult, deps=(cV, s_mk))
-        tt(T.ev[:, 0:28:2], T.ss[:, 15:448:32], T.ss[:, 479:896:32], A.add)
-        tt(T.ev[:, 1:28:2], T.ss[:, 495:928:32], T.ss[:, 31:448:32], A.add, deps=())
-        ts(T.e1[:, 0:28], T.ev[:, 0:28], 0.0, 672.0, A.is_lt, A.mult)
-        tt(T.e2[:, 0:28], T.e1[:, 0:28], T.ev[:, 0:28], A.add)
-        cp(R("el")[:], T.e2[:, 0:28])
+        k_r = scan(T.rr[:], T.ee[:], R("wn")[:], 0.0, A.min, A.max, deps=(k_e, s_wn))
+        k1 = ts(T.ab[:, 64:92], T.rr[:, 0:812:30], -1.0, sig, A.mult, A.add, deps=(k_r, v_cl))
+        k2 = ts(T.ab[:, 96:124], T.rr[:, 28:812:29], usig, 0.0, A.add, A.min)
+        k1 = tt(T.wf[:, 0:C:16], T.ab[:, 64:92], T.ab[:, 0:28], A.max, deps=(k1, k_ab))
+        k2 = tt(T.wb[:, 15:C:16], T.ab[:, 96:124], T.ab[:, 32:60], A.min, deps=(k2,))
+        k1 = scan(T.l2[:], dl[:], T.wf[:], float(POFF - 1), A.max, A.min, deps=(k1,))
+        k2 = scan(T.n2[:, ::-1], dl[:, ::-1], T.wb[:, ::-1], -111.0, A.min, A.max, deps=(k2,))
+        xa = tt(T.x1[:, 0:HALF], T.l2[:, 0:HALF], R("nd")[:, 0:HALF], A.min, deps=(k1, s_nd))
+        xb = tt(T.x1[:, HALF:C], T.l2[:, HALF:C], R("nd")[:, HALF:C], A.min)
+        va = tt(T.val[:, 16:16 + HALF], T.x1[:, 0:HALF], T.n2[:, 0:HALF], A.max, deps=(xa, k2))
+        vb = tt(T.val[:, 16 + HALF:16 + C], T.x1[:, HALF:C], T.n2[:, HALF:C], A.max, deps=(xb,))
+        k0 = tr(T.tt[:, C:C + HALF], T.val[:, 0:HALF], deps=(va,))
+        k1 = tr(T.tt[:, 0:C], T.val[:, 16:16 + C], deps=(vb,))
+        k2 = tr(T.tt[:, C + HALF:928], T.val[:, HALF:480])
+        k1 = scan(T.ss[:, 0:C], T.tt[:, 0:C], T.mk[:, 0:C], 0.0, A.add, A.mult, deps=(k1, s_mk))
+        k2 = scan(T.ss[:, C:928], T.tt[:, C:928], T.mk[:, C:928], 0.0, A.add, A.mult, deps=(k0, k2))
+        k1 = tt(T.ev[:, 0:28:2], T.ss[:, 15:448:32], T.ss[:, 479:896:32], A.add, deps=(k1, k2))
+        k2 = tt(T.ev[:, 1:28:2], T.ss[:, 495:928:32], T.ss[:, 31:448:32], A.add)
+        k1 = ts(T.e1[:, 0:28], T.ev[:, 0:28], 0.0, 672.0, A.is_lt, A.mult, deps=(k1, k2))
+        k1 = tt(T.e2[:, 0:28], T.e1[:, 0:28], T.ev[:, 0:28], A.add, deps=(k1,))
+        k_el = cp(R("el")[:], T.e2[:, 0:28], deps=(k1,))
         xn, nq, ns = R("xn"), T["aq%d" % (r + 1)], T["as%d" % (r + 1)]
         v_g = [fresh(), fresh()]
 
         def gather(h, b):
             a0, a1 = HALF * h, HALF * (h + 1)
             tt(xn[:, 4 * a0 + b:4 * a1:4], win[b][:].indirect(R("el")[:, 14 * h:14 * h + 14]),
-               T.pc[:, C * b + a0:C * b + a1], A.add, deps=(cV, prev_d[b], s_p, g_z, s_pc), sem=v_g[h])
+               T.pc[:, C * b + a0:C * b + a1], A.add, deps=(k_el, prev_d[b], s_p, g_z, s_pc), sem=v_g[h])
 
         def requant(h):
             a0, a1 = HALF * h, HALF * (h + 1)

@@ -7,9 +7,11 @@ C, TM, ROUNDS = 448, 96, 2
 HALF = C // 2
 Z0 = 196608.0
 BIG = 1.0e9
-POFF, ROFF, WINW = 113, 576, 688
+MID, POFF = 560, 113
+WINW = MID + POFF + C
 NP = 816
 NROT = 6
+CUTS = [(0, HALF, C), (0, 320, C), (0, 320, C)]
 
 Q4, U8 = "float8_e4m3fn_x4", "uint8"
 SCRATCH = {}
@@ -37,10 +39,10 @@ for _n, _w, _d in [
     ("xx", 336, "bfloat16"), ("xs", 336, "float32"), ("lo", C, "float16"), ("nc", C, "float16"),
     ("sm", C, "bfloat16"), ("mn", 32, "bfloat16"), ("ee", NP, "bfloat16"), ("rr", NP, "float16"),
     ("ab", 128, "float32"), ("l2", C, "float16"), ("n2", C, "float16"), ("x1", C, "float16"), ("val", 480, "float16"),
-    ("tt", 928, "float16"), ("ss", 928, "float16"), ("ev", 32, "float32"), ("e1", 32, "float32"), ("e2", 32, "float32"),
+    ("tt", 928, "float16"), ("ss", 928, "float16"), ("ev", 32, "float32"),
     ("zb", C, "bfloat16"), ("ysb", C, "float32"), ("pc", 4 * C, "bfloat16"),
-    ("win0", WINW, "bfloat16"), ("win1", WINW, "bfloat16"), ("win2", WINW, "bfloat16"), ("win3", WINW, "bfloat16"),
-    ("aq0", C, Q4), ("as0", C, U8),
+    ("win0", WINW + 15, "bfloat16"), ("win1", WINW + 15, "bfloat16"), ("win2", WINW + 15, "bfloat16"),
+    ("win3", WINW + 15, "bfloat16"), ("aq0", C, Q4), ("as0", C, U8),
 ]:
     _sb(_n, _w, _d)
 for _r in range(ROUNDS):
@@ -56,7 +58,7 @@ for _r in range(ROUNDS):
 SCRATCH["pss"] = ("psum", [128, 1024], "float32")
 SCRATCH["psp"] = ("psum", [128, 2048], "float32")
 
-SEMAPHORES = (["cV", "cS", "arr0", "arr1", "loc", "st"] + ["cV%d" % _i for _i in range(NROT)]
+SEMAPHORES = (["cS", "arr0", "arr1", "loc", "st"] + ["cV%d" % _i for _i in range(NROT)]
               + ["k%d" % _i for _i in range(130)])
 
 
@@ -154,8 +156,8 @@ def rank_program(g, core, T, topo):
     s_one = act(T.et[:], T.tf[:], F.Identity, deps=(g_t,), sem=True, scale=0.0, bias=1.0)
     g_z = fresh()
     for b in range(4):
-        act(win[b][:, 0:POFF], T.tf[:, 0:POFF], F.Copy, sem=g_z, scale=0.0)
-        act(win[b][:, POFF + C:WINW], T.tf[:, 0:WINW - POFF - C], F.Copy, sem=g_z, scale=0.0)
+        act(win[b][:, 0:1], T.tf[:, 0:1], F.Copy, sem=g_z, scale=0.0)
+        act(win[b][:, 1 + C:MID + POFF], T.tf[:, 0:MID + POFF - 1 - C], F.Copy, sem=g_z, scale=0.0)
     v_ww = fresh()
     for r in range(ROUNDS):
         act(T["ww%d" % r][:], T.tf[:, 0:128], F.Copy, sem=v_ww, scale=0.0)
@@ -243,30 +245,31 @@ def rank_program(g, core, T, topo):
         return DstId(rid=rid, pnc=pid), sum(1 << e for e in eng), len(eng)
 
     tot["loc"] = 0
-    s_mk = v_lw = v_e = v_v = None
+    s_mk = v_lw = None
+    v_e, v_v = fresh(), fresh()
     prev_d = []
     for r in range(ROUNDS):
         R = lambda name: T[name + str(r)]
         aq, asc = T["aq%d" % r], T["as%d" % r]
         za, dl, ww = R("za"), R("dl"), R("ww")
         lqb, lsb = R("lq_"), R("ls_")
-        t_s = [mm(T.pss[:, 512 * h:512 * h + HALF], T.uq2[:], T.us2[:], aq[:, HALF * h:HALF * (h + 1)],
-                  asc[:, HALF * h:HALF * (h + 1)], deps=(v_u, v_a[h])) for h in range(2)]
+        cut = CUTS[r]
+        t_s = [mm(T.pss[:, 512 * h:512 * h + cut[h + 1] - cut[h]], T.uq2[:], T.us2[:], aq[:, cut[h]:cut[h + 1]],
+                  asc[:, cut[h]:cut[h + 1]], deps=(v_u, v_a[h])) for h in range(2)]
         t_p = [mm(T.psp[:, 512 * b:512 * b + C], T.wq[:, 128 * b:128 * b + 128], T.wsc[:, 128 * b:128 * b + 128],
                   aq[:], asc[:], deps=[d_w] + prev_d) for b in range(4)]
         s_p = fresh()
         for b in range(4):
-            act(win[b][:, POFF:POFF + C], T.psp[:, 512 * b:512 * b + C], F.Copy, deps=(t_p[b],), sem=s_p, scale=0.0625)
+            act(win[b][:, 1:1 + C], T.psp[:, 512 * b:512 * b + C], F.Copy, deps=(t_p[b],), sem=s_p, scale=0.0625)
+        d_p = fresh()
+        for b in range(4):
+            dma("Y", win[b][:, MID + POFF:WINW], win[b][:, 1:1 + C], deps=(s_p, g_z), sem=d_p)
         wait("V", ALLV)
-        k_s = []
-        for h in range(2):
-            k_s.append(ts(T.sg[:, HALF * h:HALF * (h + 1)], T.pss[:, 512 * h:512 * h + HALF], 0.0, 0.5, A.is_ge,
-                          A.subtract, deps=(t_s[h],)))
-            if r > 0 and h == 0:
-                v_v = quant(T.vq[:], T.vs[:], T.vt[:], deps=(d_v,), sem=True)
-                ts(T.wf[:, 0:C:16], T.tf[:, 0:C:16], float(POFF), None, A.add)
         if r > 0:
-            ts(T.wb[:, 15:C:16], T.tf[:, 15:C:16], POFF - 672.0, None, A.add)
+            late.append(lambda: ts(T.wf[:, 0:C:16], T.tf[:, 0:C:16], float(POFF), None, A.add))
+            late.append(lambda: ts(T.wb[:, 15:C:16], T.tf[:, 15:C:16], POFF - 672.0, None, A.add))
+        k_s = [ts(T.sg[:, cut[h]:cut[h + 1]], T.pss[:, 512 * h:512 * h + cut[h + 1] - cut[h]], 0.0, 0.5, A.is_ge,
+                  A.subtract, deps=(t_s[h],)) for h in range(2)]
         fill()
         k_d = scan(T.dp[:, 1:C + 1], T.sg[:], T.sg[:], 0.0, A.add, A.add, deps=k_s)
         fill()
@@ -282,18 +285,18 @@ def rank_program(g, core, T, topo):
                   deps=(k_y0, k_y1) if c == 0 else ()) for c in range(6)]
         k_xa = scan(T.xs[:, 0:224], T.kx[:, 0:224], T.xx[:, 0:224], 0.0, A.max, A.add, deps=k_c[0:4], sem=True)
         k_xb = scan(T.xs[:, 224:336], T.kx[:, 224:336], T.xx[:, 224:336], 0.0, A.max, A.add, deps=k_c[4:6], sem=True)
-        k_mn = tt(T.mn[:, 1:29], T.sm[:, 15:C:16], za[:, 16:C + 1:16], A.min, deps=(k_sm,), sem=True)
+        v_dl = fresh()
+        tt(dl[:, 0:128], za[:, 1:129], za[:, 0:128], A.subtract, sem=v_dl)
         v_ml = fresh()
         ts(R("ml")[:, 0:6], T.xs[:, 27:336:56], 1.0 / 1024, 1.0, A.mult, A.add, deps=(k_xa, k_xb), sem=v_ml)
         ts(R("ml")[:, 6:12], T.xs[:, 335:54:-56], -1.0 / 1024, float(C), A.mult, A.add, sem=v_ml)
-        s_ze = fresh()
         act(R("cb")[:, 0:1], R("c2")[:, 0:1], F.Identity, deps=(v_c2,), scale=1.0 / 64, bias=89.5 - Z0 / 32)
-        act(R("ze")[:, 0:416], za[:, 0:C + 1].indirect(T.lq[:, 0:26]), F.Identity, deps=(v_z, v_lq), sem=s_ze, bias=-64.0)
+        s_ze = act(R("ze")[:], za[:, 0:C + 1].indirect(T.lq[:, 0:51]), F.Identity, deps=(v_z, v_lq), sem=True,
+                   bias=-64.0)
         s_m = fresh()
         for b in range(4):
-            act(R("mt")[:, b:8 * TM:4], win[b][:, POFF - 1:POFF + C + 1].indirect(R("ml")[:, 0:12]), F.Copy,
+            act(R("mt")[:, b:8 * TM:4], win[b][:, 0:C + 2].indirect(R("ml")[:, 0:12]), F.Copy,
                 deps=(v_ml, s_p, g_z), sem=s_m)
-        act(R("ze")[:, 416:NP], za[:, 0:C + 1].indirect(T.lq[:, 26:51]), F.Identity, sem=s_ze, bias=-64.0)
         act(ww[:, 64:92], za[:, 0:C:16], F.Relu, deps=(v_ww, v_cl), scale=1.0 / 64, bias=colf)
         act(ww[:, 96:124], za[:, 16:C + 1:16], F.Relu, deps=(cS,), scale=1.0 / 64, bias=R("cb")[:, 0:1])
 
@@ -316,20 +319,21 @@ def rank_program(g, core, T, topo):
             tot[arr] = sum(2 * link(o, rank)[2] for o in (rank - 1, rank + 1) if 0 <= o < n_ranks)
 
         arr = "arr%d" % r
-        v_dl = tt(dl[:], za[:, 1:C + 1], za[:, 0:C], A.subtract, sem=True)
+        tt(dl[:, 128:C], za[:, 129:C + 1], za[:, 128:C], A.subtract, sem=v_dl)
         if r == 0:
             while late:
                 fill()
             v_lw = late_constants()
             send()
-            wait("V", ALLV)
-        k_lo = scan(T.lo[:], dl[:], T.wf[:], float(POFF - 1), A.max, A.min, deps=[v_dl] + ALLV)
+        wait("V", ALLV)
+        k_mn = tt(T.mn[:, 1:29], T.sm[:, 15:C:16], za[:, 16:C + 1:16], A.min, deps=(k_sm,), sem=True)
+        k_lo = scan(T.lo[:], dl[:], T.wf[:], float(POFF - 1), A.max, A.min, deps=(v_dl,))
         k_nc = scan(T.nc[:, ::-1], dl[:, ::-1], T.wb[:, ::-1], -111.0, A.min, A.max)
         v_w = fresh()
         cp(ww[:, 1:29], T.lo[:, 15:C:16], deps=(k_lo, v_ww), sem=v_w)
-        ts(ww[:, 33:61], T.nc[:, 0:C:16], -1.0, 1.0, A.mult, A.add, deps=(k_nc,), sem=v_w)
         k_ab = fresh()
         tt(T.ab[:, 0:28], dl[:, 0:C:16], T.wf[:, 0:C:16], A.min, sem=k_ab)
+        ts(ww[:, 33:61], T.nc[:, 0:C:16], -1.0, 1.0, A.mult, A.add, deps=(k_nc,), sem=v_w)
         tt(T.ab[:, 32:60], dl[:, 15:C:16], T.wb[:, 15:C:16], A.max, sem=k_ab)
         if r > 0:
             send()
@@ -340,17 +344,25 @@ def rank_program(g, core, T, topo):
             s_mk = act(T.mk[:], T.pat[:], F.Abs, deps=(g_pat, v_cl), sem=True, bias=npar)
         s_pc = fresh()
         for b in range(4):
-            act(T.pc[:, C * b:C * (b + 1)], win[b][:, POFF:POFF + C], F.Copy, sem=s_pc)
+            act(T.pc[:, C * b:C * (b + 1)], win[b][:, 1:1 + C], F.Copy, sem=s_pc)
         k_e = tt(T.ee[:], T.mn[:].indirect(T.lm[:, 0:51]), R("ze")[:], A.subtract, deps=(k_mn, s_ze))
+
+        def quant_e(b):
+            quant(T.eq[:, 128 * b:128 * b + 128], T.es[:, 128 * b:128 * b + 128], T.et[:, 3 - b:515 - b],
+                  deps=(g_e,), sem=v_e)
+
         v_fill = []
         if r == 0:
-            v_e = fresh()
-            for b in range(4):
-                quant(T.eq[:, 128 * b:128 * b + 128], T.es[:, 128 * b:128 * b + 128], T.et[:, 3 - b:515 - b],
-                      deps=(g_e,), sem=v_e)
+            for b in range(3):
+                quant_e(b)
         if not (has_l and has_r):
             f0 = 2 * TM if has_r else TM
             v_fill = [quant(lqb[:, f0:f0 + 128], lsb[:, f0:f0 + 128], T.xt[:, 0:512], sem=True)]
+        k_r = scan(T.rr[:], T.ee[:], R("wn")[:], 0.0, A.min, A.max, deps=(k_e, s_wn))
+        if r == 0:
+            quant_e(3)
+        else:
+            quant(T.vq[:], T.vs[:], T.vt[:], deps=(d_v,), sem=v_v)
         l0 = 0 if has_l else TM
         ln = 2 * TM if has_l and has_r else 128
         prev_d = []
@@ -359,12 +371,11 @@ def rank_program(g, core, T, topo):
                      lqb[:, l0:l0 + ln], lsb[:, l0:l0 + ln], deps=[v_e, s_p, arr] + v_fill)
             s_d = fresh()
             if has_l:
-                act(win[b][:, 1:1 + TM], T.psp[:, 512 * b:512 * b + TM], F.Copy, deps=(t_d, g_z), sem=s_d)
+                act(win[b][:, MID + 1:MID + 1 + TM], T.psp[:, 512 * b:512 * b + TM], F.Copy, deps=(t_d, g_z), sem=s_d)
             if has_r:
                 o = 512 * b + (TM if has_l else 0)
-                act(win[b][:, ROFF:ROFF + TM], T.psp[:, o:o + TM], F.Copy, deps=(t_d, g_z), sem=s_d)
+                act(win[b][:, MID - TM:MID], T.psp[:, o:o + TM], F.Copy, deps=(t_d, g_z), sem=s_d)
             prev_d.append(s_d)
-        k_r = scan(T.rr[:], T.ee[:], R("wn")[:], 0.0, A.min, A.max, deps=(k_e, s_wn))
         k1 = ts(T.ab[:, 64:92], T.rr[:, 0:812:30], -1.0, sig, A.mult, A.add, deps=(k_r, v_cl))
         k2 = ts(T.ab[:, 96:124], T.rr[:, 28:812:29], usig, 0.0, A.add, A.min)
         k1 = tt(T.wf[:, 0:C:16], T.ab[:, 64:92], T.ab[:, 0:28], A.max, deps=(k1, k_ab))
@@ -382,19 +393,18 @@ def rank_program(g, core, T, topo):
         k2 = scan(T.ss[:, C:928], T.tt[:, C:928], T.mk[:, C:928], 0.0, A.add, A.mult, deps=(k0, k2))
         k1 = tt(T.ev[:, 0:28:2], T.ss[:, 15:448:32], T.ss[:, 479:896:32], A.add, deps=(k1, k2))
         k2 = tt(T.ev[:, 1:28:2], T.ss[:, 495:928:32], T.ss[:, 31:448:32], A.add)
-        k1 = ts(T.e1[:, 0:28], T.ev[:, 0:28], 0.0, 672.0, A.is_lt, A.mult, deps=(k1, k2))
-        k1 = tt(T.e2[:, 0:28], T.e1[:, 0:28], T.ev[:, 0:28], A.add, deps=(k1,))
-        k_el = cp(R("el")[:], T.e2[:, 0:28], deps=(k1,))
+        k_el = ts(R("el")[:], T.ev[:, 0:28], float(MID), None, A.add, deps=(k1, k2))
         xn, nq, ns = R("xn"), T["aq%d" % (r + 1)], T["as%d" % (r + 1)]
         v_g = [fresh(), fresh()]
+        cut = CUTS[r + 1]
 
         def gather(h, b):
-            a0, a1 = HALF * h, HALF * (h + 1)
-            tt(xn[:, 4 * a0 + b:4 * a1:4], win[b][:].indirect(R("el")[:, 14 * h:14 * h + 14]),
-               T.pc[:, C * b + a0:C * b + a1], A.add, deps=(k_el, prev_d[b], s_p, g_z, s_pc), sem=v_g[h])
+            a0, a1 = cut[h], cut[h + 1]
+            tt(xn[:, 4 * a0 + b:4 * a1:4], win[b][:, 0:WINW].indirect(R("el")[:, a0 // 16:a1 // 16]),
+               T.pc[:, C * b + a0:C * b + a1], A.add, deps=(k_el, prev_d[b], s_p, g_z, s_pc, d_p), sem=v_g[h])
 
         def requant(h):
-            a0, a1 = HALF * h, HALF * (h + 1)
+            a0, a1 = cut[h], cut[h + 1]
             return quant(nq[:, a0:a1], ns[:, a0:a1], xn[:, 4 * a0:4 * a1], deps=(v_g[h],), sem=True)
 
         for b in range(4):
@@ -406,11 +416,12 @@ def rank_program(g, core, T, topo):
         v_a.append(requant(1))
 
     fq, fs = T["aq%d" % ROUNDS], T["as%d" % ROUNDS]
+    cut = CUTS[ROUNDS]
     for h in range(2):
-        a0, a1 = HALF * h, HALF * (h + 1)
-        t_y = mm(T.pss[:, 512 * h:512 * h + HALF], T.vq[:], T.vs[:], fq[:, a0:a1], fs[:, a0:a1], deps=(v_v, v_a[h]))
+        a0, a1 = cut[h], cut[h + 1]
+        t_y = mm(T.pss[:, 512 * h:512 * h + a1 - a0], T.vq[:], T.vs[:], fq[:, a0:a1], fs[:, a0:a1], deps=(v_v, v_a[h]))
         dma("Y", T.oc[:, 4 * a0:4 * a1], fq[:, a0:a1].bitcast(dt.uint8), deps=(v_a[h],), sem="st")
-        s_y = act(T.ysb[:, a0:a1], T.pss[:, 512 * h:512 * h + HALF], F.Copy, deps=(t_y,), sem=True)
+        s_y = act(T.ysb[:, a0:a1], T.pss[:, 512 * h:512 * h + a1 - a0], F.Copy, deps=(t_y,), sem=True)
         dma("S", T.y[:, a0:a1], T.ysb[:, a0:a1], deps=(s_y,), sem="st")
     for k in range(4):
         dma("Y", T.osc[4 * k:4 * k + 4, :], fs[32 * k:32 * k + 4, :], deps=(), sem="st")

@@ -4,62 +4,39 @@ from concourse.mybir import dt, AluOpType, ActivationFunctionType
 A = AluOpType
 F = ActivationFunctionType
 C, TM, ROUNDS = 448, 96, 2
-HALF = C // 2
-Z0 = 196608.0
-BIG = 1.0e9
-MID, POFF = 560, 113
-WINW = MID + POFF + C
+MID = 320
+H = 464
+Z0 = 3072.0
+LOW = Z0 - 480
+U1 = 2.0 ** -24
+CAP = (1024 + C + TM) / 4096.0
+POFF = 2 + TM
+WS = 656
 NP = 816
+SEL, C2 = 480, 480 + 2 * C
 NROT = 6
-CUTS = [(0, HALF, C), (0, 320, C), (0, 320, C)]
-
-Q4, U8 = "float8_e4m3fn_x4", "uint8"
+D1 = 12
+CUT = (0, MID, C)
+Q4, U8, BF, F16, F32, I32, U16 = "float8_e4m3fn_x4", "uint8", "bfloat16", "float16", "float32", "int32", "uint16"
 SCRATCH = {}
-
-
-def _sb(name, w, d):
-    SCRATCH[name] = ("sbuf", [128, w], d)
-
-
 for _n, _w, _d in [
-    ("xt", 4 * C, "bfloat16"), ("ut", 512, "bfloat16"), ("vt", 512, "bfloat16"),
-    ("wq", 512, Q4), ("wsc", 512, U8), ("uq", 128, Q4), ("us", 128, U8), ("uq2", 128, Q4), ("us2", 128, U8),
-    ("vq", 128, Q4), ("vs", 128, U8), ("et", 520, "bfloat16"), ("eq", 512, Q4), ("es", 512, U8),
-    ("pi", 8, "int32"), ("pj", 8, "int32"), ("cl", 16, "float32"), ("nf", 52, "float32"), ("lui", 8, "int32"),
-    ("lu", 8, "uint16"), ("lq", 52, "uint16"), ("lm", 52, "uint16"), ("lw", 52, "uint16"),
-    ("t0", 52, "float32"), ("wi", 52, "int32"), ("t1", 52, "float32"), ("t2", 52, "float32"), ("t3", 52, "float32"),
-    ("t4", 52, "float32"), ("t5", 52, "float32"), ("t6", 52, "float32"), ("t7", 52, "float32"), ("t8", 52, "float32"),
-    ("t9", 52, "float32"), ("ta", 52, "float32"), ("tb", 52, "float32"), ("tc", 52, "float32"), ("td", 52, "float32"),
-    ("te", 52, "float32"), ("tg", 52, "float32"), ("th", 52, "float32"), ("ti", 52, "float32"), ("tj", 52, "float32"),
-    ("tk", 52, "float32"), ("tl", 52, "float32"),
-    ("tf", 520, "float32"), ("wf", C, "float16"), ("wb", C, "float16"),
-    ("ky", C, "bfloat16"), ("kx", 336, "bfloat16"), ("ks", C, "bfloat16"), ("pat", 928, "bfloat16"),
-    ("mk", 928, "bfloat16"), ("zer", 16, "bfloat16"),
-    ("sg", C, "float16"), ("dp", C + 16, "float16"), ("mm", 2 * C, "bfloat16"), ("yy", 2 * C, "bfloat16"),
-    ("xx", 336, "bfloat16"), ("xs", 336, "float32"), ("lo", C, "float16"), ("nc", C, "float16"),
-    ("sm", C, "bfloat16"), ("mn", 32, "bfloat16"), ("ee", NP, "bfloat16"), ("rr", NP, "float16"),
-    ("ab", 128, "float32"), ("l2", C, "float16"), ("n2", C, "float16"), ("x1", C, "float16"), ("val", 480, "float16"),
-    ("tt", 928, "float16"), ("ss", 928, "float16"), ("ev", 32, "float32"),
-    ("zb", C, "bfloat16"), ("ysb", C, "float32"), ("pc", 4 * C, "bfloat16"),
-    ("win0", WINW + 15, "bfloat16"), ("win1", WINW + 15, "bfloat16"), ("win2", WINW + 15, "bfloat16"),
-    ("win3", WINW + 15, "bfloat16"), ("aq0", C, Q4), ("as0", C, U8),
-]:
-    _sb(_n, _w, _d)
-for _r in range(ROUNDS):
-    for _n, _w, _d in [
-        ("za", C + 16, "bfloat16"), ("c2", 2, "float32"), ("cb", 2, "float32"), ("ml", 12, "uint16"),
-        ("mt", 8 * TM, "bfloat16"), ("mq", 2 * TM, Q4), ("ms", 2 * TM, U8), ("lq_", 320, Q4), ("ls_", 320, U8),
-        ("dl", C, "bfloat16"), ("nd", C, "bfloat16"), ("ww", 128, "float32"), ("ze", NP, "float32"),
-        ("wn", NP, "bfloat16"), ("el", 28, "uint16"), ("xn", 4 * C, "bfloat16"),
-    ]:
-        _sb(_n + str(_r), _w, _d)
-    _sb("aq%d" % (_r + 1), C, Q4)
-    _sb("as%d" % (_r + 1), C, U8)
-SCRATCH["pss"] = ("psum", [128, 1024], "float32")
-SCRATCH["psp"] = ("psum", [128, 2048], "float32")
-
-SEMAPHORES = (["cS", "arr0", "arr1", "loc", "st"] + ["cV%d" % _i for _i in range(NROT)]
-              + ["k%d" % _i for _i in range(130)])
+    ("xt", 4 * C, BF), ("ut", 512, BF), ("vt", 512, BF), ("wq", 512, Q4), ("wsc", 512, U8), ("uq", 128, Q4),
+    ("us", 128, U8), ("uq2", 128, Q4), ("us2", 128, U8), ("vq", 128, Q4), ("vs", 128, U8), ("et", 520, BF),
+    ("eq", 512, Q4), ("es", 512, U8), ("pi", 8, I32), ("pj", 8, I32), ("cl", 8, F32), ("nf", 52, F32),
+    ("lui", 8, I32), ("lu", 8, U16), ("lp", 52, U16), ("tw", 16 * 52, F32), ("one", C, BF), ("sb", C, BF),
+    ("wi", 52, I32), ("c1", 480, F16), ("fb", C2 + 2 * H, F16), ("pat", 928, BF), ("mk", 928, BF),
+    ("mask", NP, BF), ("sg", 2 * C, BF), ("ysb", C, F32), ("aq0", C, Q4), ("as0", C, U8), ("z", 2 * H, BF),
+    ("kt", 192, BF), ("tb", 128, F32), ("nc", 2 * H, F16), ("m", 2 * H, BF), ("win", 4 * WS, BF),
+] + [(_n + str(_r), _w, _d) for _r in range(ROUNDS) for _n, _w, _d in [
+    ("dz", 2 * H, BF), ("vv", 64, BF), ("acc", 8, F32), ("ec", 384, BF), ("rm", 384, F32),
+    ("ml", 12, U16), ("mt", 8 * TM, BF), ("mq", 2 * TM, Q4), ("ms", 2 * TM, U8), ("lq_", 320, Q4), ("ls_", 320, U8),
+    ("dg", NP, BF), ("ee", NP, BF), ("wn", NP, BF), ("rr", NP, F16), ("ab", 2 * C, F16), ("tr", 928, F16),
+    ("ss", 928, F16), ("ev", 96, F32), ("el", 28, U16), ("xn", 4 * C, BF), ("pc", 4 * C, BF)]
+] + [("aq1", C, Q4), ("as1", C, U8), ("aq2", C, Q4), ("as2", C, U8)]:
+    SCRATCH[_n] = ("sbuf", [128, _w], _d)
+SCRATCH["pss"] = ("psum", [128, 1024], F32)
+SCRATCH["psp"] = ("psum", [128, 2048], F32)
+SEMAPHORES = (["arr0", "arr1", "loc", "st"] + ["cV%d" % _i for _i in range(NROT)] + ["k%d" % _i for _i in range(139)])
 
 
 def rank_program(g, core, T, topo):
@@ -86,21 +63,16 @@ def rank_program(g, core, T, topo):
 
     def op(q, f, deps=(), sem=None, n=1):
         wait(q, deps)
-        if sem is None and q == "V":
+        if sem is None:
             s = "cV%d" % (nrot[0] % NROT)
             nrot[0] += 1
         else:
-            s = "c" + q if sem is None else (fresh() if sem is True else sem)
+            s = fresh() if sem is True else sem
         f().then_inc(T.sem[s], n)
         tot[s] = tot.get(s, 0) + n
         return s
 
     V, S, PE = g.vector, g.scalar, g.tensor
-    cS = "cS"
-    tot[cS] = 0
-    ALLV = ["cV%d" % i for i in range(NROT)]
-    for s in ALLV:
-        tot[s] = 0
 
     def ts(out, in0, s1, s2, o0, o1=None, deps=(), sem=None):
         if o1 is None:
@@ -125,8 +97,11 @@ def rank_program(g, core, T, topo):
     def quant(oc, osc, src, deps=(), sem=None):
         return op("V", lambda: V.quantize_mx(oc, osc, src), deps, sem)
 
-    def act(out, a, fn, deps=(), sem=None, **kw):
+    def act(out, a, fn, deps=(), sem=True, **kw):
         return op("S", lambda: S.activation(out, a, fn, **kw), deps, sem)
+
+    def pick(q, out, a, deps, sem):
+        return cp(out, a, deps, sem) if q == "V" else act(out, a, F.Copy, deps, sem)
 
     def mm(out, lq, ls, rq, rs, deps=(), sem=True):
         return op("T", lambda: PE.matmul_mx(out, lq, ls, rq, rs, True, True), deps, sem)
@@ -134,106 +109,96 @@ def rank_program(g, core, T, topo):
     def dma(q, out, src, deps=(), sem=True):
         return op(q, lambda: Q[q].dma_start(out, src), deps, sem, 16)
 
-    def iota(out, pat, base, cm, deps=(), sem=True, small=True):
+    def iota(out, pat, base, cm=0, sem=True, small=True):
         if small:
-            return op("G", lambda: g.iota(out, pat, base, cm, allow_small_or_imprecise_dtypes=True), deps, sem)
-        return op("G", lambda: g.iota(out, pat, base, cm), deps, sem)
-
-    win = [T["win%d" % b] for b in range(4)]
+            return op("G", lambda: g.iota(out, pat, base, cm, allow_small_or_imprecise_dtypes=True), (), sem)
+        return op("G", lambda: g.iota(out, pat, base, cm), (), sem)
 
     d_u = dma("S", T.ut[:], T.u[:])
-    d_x = [dma("Y", T.xt[:, 4 * HALF * h:4 * HALF * (h + 1)], T.x[:, 4 * HALF * h:4 * HALF * (h + 1)]) for h in range(2)]
+    d_x = [dma("Y", T.xt[:, 4 * CUT[h]:4 * CUT[h + 1]], T.x[:, 4 * CUT[h]:4 * CUT[h + 1]]) for h in range(2)]
     d_w = fresh()
     dma("Y", T.wq[:].bitcast(dt.uint8), T.wc[:], sem=d_w)
     dma("Y", T.wsc[:], T.ws[:], sem=d_w)
     d_v = dma("Y", T.vt[:], T.v[:], deps=(d_w,))
 
+    win, z, nc, tb, m, fb = T.win, T.z, T.nc, T.tb, T.m, T.fb
+    key, td = T.kt, T.kt[:, 64:192]
     g_p = iota(T.pi[:, 0:1], [[0, 1]], 0, 1, small=False)
-    g_lu = iota(T.lui[:], [[16, 8]], 0, 0, small=False)
-    g_n = iota(T.nf[:], [[16, 52]], 0, 0)
-    g_t = iota(T.tf[:], [[1, 520]], 0, 0)
-    g_pat = iota(T.pat[:], [[0, 29], [1, 2], [0, 16]], 0, 0)
-    s_one = act(T.et[:], T.tf[:], F.Identity, deps=(g_t,), sem=True, scale=0.0, bias=1.0)
-    g_z = fresh()
-    for b in range(4):
-        act(win[b][:, 0:1], T.tf[:, 0:1], F.Copy, sem=g_z, scale=0.0)
-        act(win[b][:, 1 + C:MID + POFF], T.tf[:, 0:MID + POFF - 1 - C], F.Copy, sem=g_z, scale=0.0)
-    v_ww = fresh()
-    for r in range(ROUNDS):
-        act(T["ww%d" % r][:], T.tf[:, 0:128], F.Copy, sem=v_ww, scale=0.0)
-    g_e = op("G", lambda: g.affine_select(T.et[:], T.et[:], [[-1, 520]], A.is_equal, 0.0, 3, 4), (s_one,), True)
+    g_lu = iota(T.lui[:], [[16, 8]], 0, small=False)
+    g_n = iota(T.nf[:], [[16, 52]], 0)
+    g_k, g_z = fresh(), fresh()
+    iota(z[:, 0:2 * H:H], [[0, 2]], int(Z0), sem=g_k)
+    iota(m[:, C:2 * H:H], [[0, 2]], 0, sem=g_k)
+    iota(T.kt[:], [[0, 192]], int(LOW), sem=g_k)
+    iota(win[:, 0:POFF], [[0, POFF]], 0, sem=g_z)
+    iota(win[:, 3 * WS + POFF + C:4 * WS], [[0, WS - POFF - C]], 0, sem=g_z)
+    v_one = ms(T.mask[:], 1.0, sem=True)
+    g_e = op("G", lambda: g.affine_select(T.et[:], T.mask[:, 0:520], [[-1, 520]], A.is_equal, 0.0, 3, 4), (v_one,), True)
+    g_pat = iota(T.pat[:], [[0, 29], [1, 2], [0, 16]], 0)
+    s_1 = act(T.one[:], T.mask[:, 0:C], F.Copy, deps=(v_one,))
+    for b in range(3):
+        act(win[:, WS * b + POFF + C:WS * (b + 1) + POFF], T.mask[:, 0:WS - C], F.Copy, sem=g_z, scale=0.0)
+    s_ev = act(T.sg[:, 0:2 * C:2], T.mask[:, 0:C], F.Copy, scale=-1.0)
 
-    ms(T.zer[:], 0.0)
-    ms(T.ky[:], BIG)
-    ms(T.kx[:], -BIG)
-    ms(T.ks[:], -BIG)
-    ms(T.mn[:], 0.0)
-    ts(T.pj[:, 0:1], T.pi[:, 0:1], 15, None, A.bitwise_and, deps=(g_p,))
-    ts(T.pj[:, 1:2], T.pi[:, 0:1], 4, 1, A.logical_shift_right, A.bitwise_and)
-    ts(T.pj[:, 2:3], T.pi[:, 0:1], 1, None, A.bitwise_and)
-    cp(T.lu[:], T.lui[:], deps=(g_lu,))
-    rho, col1, colc, colf, npar, sig, usig = [T.cl[:, i:i + 1] for i in range(7)]
-    k0 = cp(rho, T.pj[:, 0:1], deps=ALLV)
-    v_cl = fresh()
-    ts(col1, T.pj[:, 0:1], 64.0, Z0 - 480, A.mult, A.add)
-    nn, wv, iv, bv, dv = T.t0[:], T.t1[:], T.t2[:], T.t3[:], T.t9[:]
-    k1 = ts(nn, T.nf[:], rho, None, A.add, deps=(k0, g_n))
-    ts(colc, T.pj[:, 0:1], -64.0, Z0 + 960 - 480, A.mult, A.add)
-    k2 = ts(T.t4[:], nn, -14.0, 1.0 / 29, A.add, A.mult, deps=(k1,))
-    ts(colf, T.pj[:, 0:1], -1.0, TM - Z0 / 64, A.mult, A.add, sem=v_cl)
-    k3 = cp(T.wi[:], T.t4[:], deps=(k2,))
-    ts(npar, T.pj[:, 1:2], -1.0, None, A.add, sem=v_cl)
-    k4 = ts(T.t5[:], T.wi[:], -29.0, None, A.mult, deps=(k3,))
-    k5 = cp(wv, T.wi[:])
-    k6 = tt(iv, T.t5[:], nn, A.add, deps=(k4,))
-    ts(sig, T.pj[:, 2:3], 48.0, None, A.add, sem=v_cl)
-    k7 = tt(dv, iv, wv, A.subtract, deps=(k5, k6))
-    ts(usig, T.pj[:, 2:3], -1.0, -47.0, A.mult, A.add, sem=v_cl)
-    k8 = ts(bv, dv, 0.0, None, A.is_gt, deps=(k7,))
-    ms(T.ky[:, 0:C:16], -16 * Z0)
-    k9 = tt(T.t7[:], wv, bv, A.add, deps=(k8,))
-    cp(T.dp[:, 0:16], T.zer[:])
-    v_lq = ts(T.lq[:], T.t7[:], 16.0, None, A.mult, deps=(k9,), sem=True)
-
+    v_p, v_c, v_l, v_u = fresh(), fresh(), fresh(), fresh()
+    res, hi, par = T.pj[:, 0:1], T.pj[:, 1:2], T.pj[:, 2:3]
+    colz, col0, colw, nhi = [T.cl[:, i:i + 1] for i in range(4)]
+    tw = [T.tw[:, 52 * i:52 * i + 52] for i in range(16)]
+    qv = T.wi[:]
+    ts(res, T.pi[:, 0:1], 15, None, A.bitwise_and, deps=(g_p,), sem=v_p)
+    ts(hi, T.pi[:, 0:1], 4, 1, A.logical_shift_right, A.bitwise_and, sem=v_p)
+    ts(par, T.pi[:, 0:1], 1, None, A.bitwise_and, sem=v_p)
+    k_lu = cp(T.lu[:], T.lui[:], deps=(g_lu,), sem=True)
+    k_ci = scan(fb[:, 0:480], T.mask[:, 0:480], T.mask[:, 0:480], 1023.0, A.add, A.mult, deps=(v_one,))
+    k0 = ts(colz, res, Z0 - 7.5, None, A.add, deps=(v_p,))
+    ts(col0, res, 1024 + C + Z0, None, A.add, sem=v_c)
+    ms(tb[:], (1024 + C + TM) * 2.0 ** -20, sem=v_c)
+    k_ci = ts(fb[:, C:C + 1], T.nf[:, 0:1], 2048.0, None, A.add, deps=(k_ci, g_n), sem=True)
+    k1 = ts(tw[0], T.nf[:], colz, 7.5 - Z0, A.add, A.add, deps=(k0,))
     k0 = quant(T.uq[:], T.us[:], T.ut[:], deps=(d_u,))
-    ms(T.ks[:, 0:C:16], BIG)
-    v_u = fresh()
-    cp(T.uq2[:].bitcast(dt.uint32), T.uq[:].bitcast(dt.uint32).indirect(T.lu[:, 0:8]), deps=(k0,), sem=v_u)
+    ts(colw, par, -1.0 / 64, -1296.0 / 64, A.mult, A.add, sem=v_c)
+    ts(nhi, hi, -CAP, None, A.mult, sem=v_c)
+    k2 = ts(tw[1], tw[0], -14.0, 1.0 / 29, A.add, A.mult, deps=(k1,))
+    cp(T.uq2[:].bitcast(dt.uint32), T.uq[:].bitcast(dt.uint32).indirect(T.lu[:, 0:8]), deps=(k0, k_lu), sem=v_u)
+    k3 = cp(qv, tw[1], deps=(k2,))
     cp(T.us2[:], T.us[:].indirect(T.lu[:, 0:8]), sem=v_u)
-    v_a = [quant(T.aq0[:, HALF * h:HALF * (h + 1)], T.as0[:, HALF * h:HALF * (h + 1)],
-                 T.xt[:, 4 * HALF * h:4 * HALF * (h + 1)], deps=(d_x[h],), sem=True) for h in range(2)]
-    for c in range(6):
-        ms(T.kx[:, 56 * c:56 * c + 56:28], 1024.0 * C * (c + 1))
+    k4 = ts(tw[2], qv, -29.0, None, A.mult, deps=(k3,))
 
+    def scores(r, h, dep):
+        a0, a1 = CUT[h:h + 2]
+        return mm(T.pss[:, 512 * h:512 * h + a1 - a0], T.uq2[:], T.us2[:], T["aq%d" % r][:, a0:a1],
+                  T["as%d" % r][:, a0:a1], deps=(v_u, dep))
+
+    def signs(h, dep):
+        a0, a1 = CUT[h:h + 2]
+        return ts(T.sb[:, a0:a1], T.pss[:, 512 * h:512 * h + a1 - a0], 0.0, 2.0, A.is_ge, A.mult, deps=(dep,), sem=True)
+
+    v_a = [quant(T.aq0[:, CUT[h]:CUT[h + 1]], T.as0[:, CUT[h]:CUT[h + 1]], T.xt[:, 4 * CUT[h]:4 * CUT[h + 1]],
+                 deps=(d_x[h],), sem=True) for h in range(2)]
+    t_s0 = scores(0, 0, v_a[0])
+    k5 = tt(tw[3], tw[2], tw[0], A.add, deps=(k4,), sem=True)
+    ts(T.c1[:], fb[:, 0:480], U1, None, A.mult, deps=(k_ci,), sem=v_c)
+    e = tt(tw[4], tw[3], qv, A.add, deps=(k5,))
+    ts(tw[6], qv, -1.0, 57.0, A.mult, A.add, sem=v_l)
+    v_s0 = signs(0, t_s0)
+    ts(tw[9], qv, 37.0, None, A.add, sem=v_l)
+    ts(tw[8], tw[3], 0.0, None, A.is_equal, sem=v_l)
+    ts(tw[5], tw[4], 28.0, None, A.is_ge, deps=(e,), sem=v_l)
+    ts(tw[11], qv, -1.0, 64.0, A.mult, A.add, sem=v_l)
+    kl = {}
     late = [
-        lambda: ts(T.ta[:], wv, 35.0, None, A.add),
-        lambda: ts(T.t6[:], iv, 0.0, None, A.is_equal),
-        lambda: ts(T.tb[:], wv, 64.0, None, A.add),
-        lambda: ts(T.t8[:], dv, 1.0, None, A.is_equal),
-        lambda: tt(T.tc[:], dv, iv, A.add),
-        lambda: ts(T.td[:], bv, 32.0, None, A.mult),
+        lambda: kl.update(c=ts(tw[10], tw[4], 28.0, None, A.is_equal)),
+        lambda: kl.update(e=ts(tw[7], tw[3], -1.0, 28.0, A.mult, A.add, sem=True)),
+        lambda: kl.update(d=tt(tw[12], tw[5], tw[6], A.mult, deps=(v_l,), sem=True)),
+        lambda: kl.update(c=tt(tw[14], tw[10], tw[11], A.mult, deps=(kl["c"],), sem=True)),
+        lambda: kl.update(b=tt(tw[13], tw[8], tw[9], A.mult, sem=True)),
+        lambda: kl.update(a=tt(tw[15], tw[12], tw[7], A.add, deps=(kl["d"], kl["e"]), sem=True)),
+        lambda: kl.update(b=tt(tw[1], tw[13], tw[14], A.add, deps=(kl["b"], kl["c"]), sem=True)),
     ]
 
-    def fill():
-        if late:
-            late.pop(0)()
-
-    def late_constants():
-        a = tt(T.te[:], T.t6[:], T.tb[:], A.mult, deps=ALLV)
-        b = tt(T.tg[:], T.t8[:], T.ta[:], A.mult)
-        c = ts(T.th[:], T.tc[:], -1.0, 30.0, A.mult, A.add)
-        d = tt(T.ti[:], T.te[:], T.tg[:], A.add, deps=(a, b))
-        e = tt(T.tj[:], T.th[:], bv, A.mult, deps=(c,))
-        f = tt(T.tk[:], T.ti[:], T.td[:], A.add, deps=(d,))
-        h = tt(T.tl[:], T.tj[:], iv, A.add, deps=(e,))
-        k = ts(T.wf[:], T.tf[:, 0:C], float(POFF), None, A.add, deps=(g_t,))
-        cp(T.lm[:], T.tl[:], deps=(h,))
-        m = tt(T.t4[:], T.tk[:], T.tl[:], A.add, deps=(f,))
-        ts(T.wb[:], T.wf[:], -672.0, None, A.add, deps=(k,))
-        lw = cp(T.lw[:], T.t4[:], deps=(m,), sem=True)
-        cp(T.val[:, 0:16], T.zer[:])
-        cp(T.val[:, 464:480], T.zer[:])
-        return lw
+    def quant_e(b):
+        quant(T.eq[:, 128 * b:128 * b + 128], T.es[:, 128 * b:128 * b + 128], T.et[:, 3 - b:515 - b],
+              deps=(g_e,), sem=v_e)
 
     def link(src_rank, dst_rank):
         src, dst = T.cores[src_rank], T.cores[dst_rank]
@@ -245,184 +210,258 @@ def rank_program(g, core, T, topo):
         return DstId(rid=rid, pnc=pid), sum(1 << e for e in eng), len(eng)
 
     tot["loc"] = 0
-    s_mk = v_lw = None
-    v_e, v_v = fresh(), fresh()
+    s_mk = v_lp = None
+    v_e, v_v, v_m, v_c2 = fresh(), fresh(), fresh(), fresh()
     prev_d = []
+    both = [fresh() for _ in range(14)]
     for r in range(ROUNDS):
         R = lambda name: T[name + str(r)]
         aq, asc = T["aq%d" % r], T["as%d" % r]
-        za, dl, ww = R("za"), R("dl"), R("ww")
+        dz, acc = R("dz"), R("acc")
         lqb, lsb = R("lq_"), R("ls_")
-        cut = CUTS[r]
-        t_s = [mm(T.pss[:, 512 * h:512 * h + cut[h + 1] - cut[h]], T.uq2[:], T.us2[:], aq[:, cut[h]:cut[h + 1]],
-                  asc[:, cut[h]:cut[h + 1]], deps=(v_u, v_a[h])) for h in range(2)]
-        t_p = [mm(T.psp[:, 512 * b:512 * b + C], T.wq[:, 128 * b:128 * b + 128], T.wsc[:, 128 * b:128 * b + 128],
-                  aq[:], asc[:], deps=[d_w] + prev_d) for b in range(4)]
-        s_p = fresh()
-        for b in range(4):
-            act(win[b][:, 1:1 + C], T.psp[:, 512 * b:512 * b + C], F.Copy, deps=(t_p[b],), sem=s_p, scale=0.0625)
-        d_p = fresh()
-        for b in range(4):
-            dma("Y", win[b][:, MID + POFF:WINW], win[b][:, 1:1 + C], deps=(s_p, g_z), sem=d_p)
-        wait("V", ALLV)
-        if r > 0:
-            late.append(lambda: ts(T.wf[:, 0:C:16], T.tf[:, 0:C:16], float(POFF), None, A.add))
-            late.append(lambda: ts(T.wb[:, 15:C:16], T.tf[:, 15:C:16], POFF - 672.0, None, A.add))
-        k_s = [ts(T.sg[:, cut[h]:cut[h + 1]], T.pss[:, 512 * h:512 * h + cut[h + 1] - cut[h]], 0.0, 0.5, A.is_ge,
-                  A.subtract, deps=(t_s[h],)) for h in range(2)]
-        fill()
-        k_d = scan(T.dp[:, 1:C + 1], T.sg[:], T.sg[:], 0.0, A.add, A.add, deps=k_s)
-        fill()
-        v_c2 = ts(R("c2")[:, 0:1], T.dp[:, C:C + 1], -64.0, colc, A.mult, A.add, deps=(k_d,), sem=True)
-        v_z = ts(za[:, 0:C + 1], T.dp[:, 0:C + 1], 64.0, col1, A.mult, A.add, sem=True)
-        k_zb = ts(T.zb[:], T.dp[:, C - 1::-1], 64.0, R("c2")[:, 0:1], A.mult, A.add, deps=(v_c2,))
-        k_m0 = scan(T.mm[:, 0:C], za[:, 1:C + 1], za[:, 1:C + 1], Z0, A.min, A.min, deps=(v_z,))
-        k_m1 = scan(T.mm[:, C:2 * C], T.zb[:], T.zb[:], Z0, A.min, A.min, deps=(k_zb,))
-        k_y0 = scan(T.yy[:, 0:C], T.ky[:], T.mm[:, 0:C], 0.0, A.min, A.add, deps=(k_m0,))
-        k_y1 = scan(T.yy[:, C:2 * C], T.ky[:], T.mm[:, C:2 * C], 0.0, A.min, A.add, deps=(k_m1,))
-        k_sm = scan(T.sm[:], T.ks[:], za[:, 0:C], 0.0, A.max, A.min, sem=True)
-        k_c = [ts(T.xx[:, 56 * c:56 * c + 56], T.yy[:, 15:2 * C:16], -16384.0 * (c + 1), -16384.0 * c, A.max, A.min,
-                  deps=(k_y0, k_y1) if c == 0 else ()) for c in range(6)]
-        k_xa = scan(T.xs[:, 0:224], T.kx[:, 0:224], T.xx[:, 0:224], 0.0, A.max, A.add, deps=k_c[0:4], sem=True)
-        k_xb = scan(T.xs[:, 224:336], T.kx[:, 224:336], T.xx[:, 224:336], 0.0, A.max, A.add, deps=k_c[4:6], sem=True)
-        v_dl = fresh()
-        tt(dl[:, 0:128], za[:, 1:129], za[:, 0:128], A.subtract, sem=v_dl)
-        v_ml = fresh()
-        ts(R("ml")[:, 0:6], T.xs[:, 27:336:56], 1.0 / 1024, 1.0, A.mult, A.add, deps=(k_xa, k_xb), sem=v_ml)
-        ts(R("ml")[:, 6:12], T.xs[:, 335:54:-56], -1.0 / 1024, float(C), A.mult, A.add, sem=v_ml)
-        act(R("cb")[:, 0:1], R("c2")[:, 0:1], F.Identity, deps=(v_c2,), scale=1.0 / 64, bias=89.5 - Z0 / 32)
-        s_ze = act(R("ze")[:], za[:, 0:C + 1].indirect(T.lq[:, 0:51]), F.Identity, deps=(v_z, v_lq), sem=True,
-                   bias=-64.0)
+        arr = "arr%d" % r
+        t_s1 = scores(r, 1, v_a[1])
+        v_z, zb, v_t, v_k, v_d, v_w = both[0:6]
+        s_p, d_p, v_f, v_rm, v_ml = both[6:10], both[10], both[11], both[12], both[13]
+        vv, ec, rm = R("vv"), R("ec"), R("rm")
+
+        def plane(b):
+            t = mm(T.psp[:, 512 * b:512 * b + C], T.wq[:, 128 * b:128 * b + 128], T.wsc[:, 128 * b:128 * b + 128],
+                   aq[:], asc[:], deps=[d_w] + prev_d)
+            act(win[:, WS * b + POFF:WS * b + POFF + C], T.psp[:, 512 * b:512 * b + C], F.Copy, deps=(t,), sem=s_p[b],
+                scale=0.0625)
+
+        def level(a0, a1, init, deps):
+            return scan(z[:, a0 + 1:a1 + 1], T.sb[:, a0:a1], T.one[:, a0:a1], init, A.add, A.subtract, deps=deps,
+                        sem=v_z)
+
+        def event(a0, a1, deps):
+            return scan(dz[:, a0:a1], z[:, a0 + 1:a1 + 1], z[:, a0:a1], 0.0, A.max, A.subtract, deps=deps)
+
+        def factor(a0, a1, deps, sem=None):
+            return ts(m[:, a0:a1], dz[:, a0:a1], 1.0 / 16, 1.0, A.mult, A.add, deps=deps, sem=sem)
+
+        def valid(h, d):
+            return ts(vv[:, 29 * h:29 * h + 28], nc[:, H * h:H * h + C:16], 2048 * U1, 16.0, A.is_lt, A.mult, deps=(d,))
+
+        def keys(h, d):
+            tt(key[:, 29 * h:29 * h + 28], z[:, H * h:H * h + C:16], vv[:, 29 * h:29 * h + 28], A.subtract,
+               deps=(d,), sem=v_k)
+            tt(tb[:, 29 * h:29 * h + 28], nc[:, H * h:H * h + C:16], vv[:, 29 * h:29 * h + 28], A.mult, sem=v_t)
+
+        def total(h, dep):
+            a0, a1 = CUT[h:h + 2]
+            return act(T.sg[:, 2 * a0 + 1:2 * a1:2], T.sb[:, a0:a1], F.Identity, deps=(dep,), bias=-1.0,
+                       accum_out=acc[:, h:h + 1])
+
+        def copy_p(b):
+            cp(R("pc")[:, C * b:C * (b + 1)], win[:, WS * b + POFF:WS * b + POFF + C], deps=(s_p[b],), sem=d_p)
+
+        s_a0 = total(0, v_s0)
+        level(0, MID, colz, (v_s0, s_1))
+        if r == 0:
+            for f in late[0:3]:
+                f()
+        k1 = event(0, MID, (v_z, g_k))
+        v_s1 = signs(1, t_s1)
+        plane(0)
+        s_a1 = total(1, v_s1)
+        for b in range(1, 4):
+            plane(b)
+        factor(0, MID, (k1,), v_f)
+        k0 = ts(acc[:, 5:6], acc[:, 0:1], colz, None, A.add, deps=(s_a0,))
+        scan(z[:, H + 1:H + C + 1], T.one[:], T.sb[:, ::-1], colz, A.add, A.subtract, deps=(v_s1,), sem=zb)
+        level(MID, C, acc[:, 5:6], (k0,))
+        if r == 0:
+            for f in late[3:5]:
+                f()
+        k3 = event(H, H + C, (zb,))
+        k2 = event(MID, C, (v_z,))
+        ka = ts(acc[:, 3:4], acc[:, 0:1], acc[:, 1:2], col0, A.add, A.add, deps=(s_a1, v_c), sem=True)
+        kb = ts(acc[:, 4:5], acc[:, 0:1], acc[:, 1:2], col0, A.add, A.subtract, sem=True)
+        k3 = factor(H, H + C, (k3,))
+        factor(MID, C, (k2,), v_f)
+        ts(tb[:, 64:93], z[:, 0:C + 1:16], acc[:, 3:4], -2.0 ** -20, A.subtract, A.mult, deps=(ka,), sem=v_w)
+        ts(tb[:, 93:122], z[:, H:H + C + 1:16], acc[:, 4:5], -2.0 ** -20, A.add, A.mult, deps=(kb,), sem=v_w)
+        if r == 0:
+            late[5]()
+        k_nb = scan(nc[:, H + C:H - 1:-1], m[:, H + C:H - 1:-1], T.c1[:, C::-1], 0.0, A.mult, A.max, deps=(k3,))
+        if r == 0:
+            late[6]()
+        k_na = scan(nc[:, C::-1], m[:, C::-1], T.c1[:, C::-1], 0.0, A.mult, A.max, deps=(v_f,))
+        k0 = valid(1, k_nb)
+        if r == 0:
+            kl.update(a=tt(tw[2], tw[15], tw[1], A.add, deps=(kl["a"], kl["b"]), sem=True))
+        copy_p(0)
+        k1 = valid(0, k_na)
+        keys(1, k0)
+        if r == 0:
+            v_lp = ts(T.lp[:], tw[2], 121.0, None, A.min, deps=(kl["a"],), sem=True)
+        ts(key[:, 128:186], z[:, 0:2 * H:16], -1.0, LOW + 8, A.mult, A.add, sem=v_d)
+        keys(0, k1)
+        copy_p(1)
+        k_e = [ts(ec[:, 64 * c:64 * c + 58], key[:, 57::-1], 16.0 * c + 8 - Z0, None, A.add, deps=(v_k,))
+               for c in range(6)]
+        for c in range(6):
+            scan(rm[:, 64 * c:64 * c + 58], ec[:, 64 * c:64 * c + 58], tb[:, 57::-1], 0.0, A.min, A.max,
+                 deps=(k_e[c], v_t), sem=v_rm)
+        tt(key[:, 64:121], key[:, 0:57], key[:, 1:58], A.subtract, sem=v_d)
+        k_ms = ms(m[:, 0:2 * H:16], 0.0, sem=True)
+        if r == 0:
+            ms(T.mask[:, 0:812:29], 0.0, deps=(g_z, g_e, s_ev, s_1), sem=v_m)
+        ts(R("ml")[:, 0:6], rm[:, 57:384:64], 2.0 ** 20, POFF - 1024.0, A.mult, A.add, deps=(v_rm,), sem=v_ml)
+        ts(R("ml")[:, 6:12], rm[:, 28:384:64], -2.0 ** 20, POFF + C - 1 + 1024.0, A.mult, A.add, sem=v_ml)
+        dg, ee, rr = R("dg"), R("ee"), R("rr")
+        v_dg, s_wn = [fresh(), fresh()], fresh()
+
+        def steps(a0, a1):
+            cp(dg[:, 16 * a0:16 * a1], td.indirect(T.lp[:, a0:a1]), deps=(v_d, v_lp), sem=v_dg[0])
+
+        steps(0, D1)
+        act(R("wn")[:], tb[:].indirect(T.lp[:, 0:51]), F.Identity, deps=(v_t, v_w, v_lp, v_c), sem=s_wn,
+            scale=2.0 ** 14, bias=colw)
         s_m = fresh()
         for b in range(4):
-            act(R("mt")[:, b:8 * TM:4], win[b][:, 0:C + 2].indirect(R("ml")[:, 0:12]), F.Copy,
-                deps=(v_ml, s_p, g_z), sem=s_m)
-        act(ww[:, 64:92], za[:, 0:C:16], F.Relu, deps=(v_ww, v_cl), scale=1.0 / 64, bias=colf)
-        act(ww[:, 96:124], za[:, 16:C + 1:16], F.Relu, deps=(cS,), scale=1.0 / 64, bias=R("cb")[:, 0:1])
-
-        def send():
-            v_mq = quant(R("mq")[:], R("ms")[:], R("mt")[:], deps=(s_m,), sem=True)
-            wait("G", (v_mq,))
-            for kind in range(2):
-                trs = []
-                for other, s0, d0 in ((rank - 1, 0, TM), (rank + 1, TM, 0)):
-                    if 0 <= other < n_ranks:
-                        did, mask, ne = link(rank, other)
-                        if kind == 0:
-                            src, dst = R("mq")[:, s0:s0 + TM].bitcast(dt.uint8), lqb[:, d0:d0 + TM].bitcast(dt.uint8)
-                        else:
-                            src, dst = R("ms")[:, s0:s0 + TM], lsb[:, d0:d0 + TM]
-                        trs.append(RemoteDMATransfer(dst_ids=[did], dma_engine_mask=mask, remote_sem=T.sem[arr],
-                                                     src=src, dst=dst))
-                        tot["loc"] += ne
-                g.remote_dma_fused(trs, local_sem=T.sem["loc"])
-            tot[arr] = sum(2 * link(o, rank)[2] for o in (rank - 1, rank + 1) if 0 <= o < n_ranks)
-
-        arr = "arr%d" % r
-        tt(dl[:, 128:C], za[:, 129:C + 1], za[:, 128:C], A.subtract, sem=v_dl)
+            pick("V" if b < 2 else "S", R("mt")[:, b:8 * TM:4],
+                 win[:, WS * b:WS * (b + 1)].indirect(R("ml")[:, 0:12]), (v_ml, s_p[b], g_z), s_m)
+        steps(D1, 28)
         if r == 0:
-            while late:
-                fill()
-            v_lw = late_constants()
-            send()
-        wait("V", ALLV)
-        k_mn = tt(T.mn[:, 1:29], T.sm[:, 15:C:16], za[:, 16:C + 1:16], A.min, deps=(k_sm,), sem=True)
-        k_lo = scan(T.lo[:], dl[:], T.wf[:], float(POFF - 1), A.max, A.min, deps=(v_dl,))
-        k_nc = scan(T.nc[:, ::-1], dl[:, ::-1], T.wb[:, ::-1], -111.0, A.min, A.max)
-        v_w = fresh()
-        cp(ww[:, 1:29], T.lo[:, 15:C:16], deps=(k_lo, v_ww), sem=v_w)
-        k_ab = fresh()
-        tt(T.ab[:, 0:28], dl[:, 0:C:16], T.wf[:, 0:C:16], A.min, sem=k_ab)
-        ts(ww[:, 33:61], T.nc[:, 0:C:16], -1.0, 1.0, A.mult, A.add, deps=(k_nc,), sem=v_w)
-        tt(T.ab[:, 32:60], dl[:, 15:C:16], T.wb[:, 15:C:16], A.max, sem=k_ab)
-        if r > 0:
-            send()
-        s_wn = act(R("wn")[:], ww[:].indirect(T.lw[:, 0:51]), F.Identity, deps=(cS, v_w, v_lw), sem=True,
-                   scale=-1.0, bias=sig)
-        s_nd = act(R("nd")[:], dl[:], F.Copy, deps=(v_dl,), sem=True, scale=-1.0)
+            ms(T.mask[:, 28:812:28], 0.0, sem=v_m)
+        v_mq = quant(R("mq")[:], R("ms")[:], R("mt")[:], deps=(s_m,), sem=True)
+        wait("G", (v_mq,))
+        for kind in range(2):
+            trs = []
+            for other, s0, d0 in ((rank - 1, 0, TM), (rank + 1, TM, 0)):
+                if 0 <= other < n_ranks:
+                    did, mask, ne = link(rank, other)
+                    if kind == 0:
+                        src, dst = R("mq")[:, s0:s0 + TM].bitcast(dt.uint8), lqb[:, d0:d0 + TM].bitcast(dt.uint8)
+                    else:
+                        src, dst = R("ms")[:, s0:s0 + TM], lsb[:, d0:d0 + TM]
+                    trs.append(RemoteDMATransfer(dst_ids=[did], dma_engine_mask=mask, remote_sem=T.sem[arr],
+                                                 src=src, dst=dst))
+                    tot["loc"] += ne
+            g.remote_dma_fused(trs, local_sem=T.sem["loc"])
+        tot[arr] = sum(2 * link(o, rank)[2] for o in (rank - 1, rank + 1) if 0 <= o < n_ranks)
+
+        act(dg[:, C:NP], td.indirect(T.lp[:, 28:51]), F.Copy, deps=(v_d,), sem=v_dg[1])
         if r == 0:
-            s_mk = act(T.mk[:], T.pat[:], F.Abs, deps=(g_pat, v_cl), sem=True, bias=npar)
-        s_pc = fresh()
-        for b in range(4):
-            act(T.pc[:, C * b:C * (b + 1)], win[b][:, 1:1 + C], F.Copy, sem=s_pc)
-        k_e = tt(T.ee[:], T.mn[:].indirect(T.lm[:, 0:51]), R("ze")[:], A.subtract, deps=(k_mn, s_ze))
-
-        def quant_e(b):
-            quant(T.eq[:, 128 * b:128 * b + 128], T.es[:, 128 * b:128 * b + 128], T.et[:, 3 - b:515 - b],
-                  deps=(g_e,), sem=v_e)
-
+            s_mk = act(T.mk[:], T.pat[:], F.Abs, deps=(g_pat,), scale=CAP, bias=nhi)
+        k0 = scan(ee[:, 0:C], T.mask[:, 0:C], dg[:, 0:C], 0.0, A.mult, A.add, deps=(v_dg[0], v_m))
+        if r == 0:
+            ts(fb[:, C2:C2 + C + 1], fb[:, 0:C + 1], 2.0 ** -12, None, A.mult, sem=v_c2)
+        k1 = scan(ee[:, C:NP], T.mask[:, C:NP], dg[:, C:NP], 0.0, A.mult, A.add, deps=(v_dg[1],))
+        if r == 0:
+            ts(fb[:, C2 + H:C2 + H + C + 1], fb[:, 0:C + 1], 2.0 ** -14, None, A.mult, sem=v_c2)
+        k0 = scan(rr[:, 0:C], ee[:, 0:C], R("wn")[:, 0:C], 0.0, A.min, A.max, deps=(k0, s_wn))
+        k1 = scan(rr[:, C:NP], ee[:, C:NP], R("wn")[:, C:NP], 0.0, A.min, A.max, deps=(k1,))
         v_fill = []
-        if r == 0:
-            for b in range(3):
-                quant_e(b)
         if not (has_l and has_r):
             f0 = 2 * TM if has_r else TM
             v_fill = [quant(lqb[:, f0:f0 + 128], lsb[:, f0:f0 + 128], T.xt[:, 0:512], sem=True)]
-        k_r = scan(T.rr[:], T.ee[:], R("wn")[:], 0.0, A.min, A.max, deps=(k_e, s_wn))
-        if r == 0:
-            quant_e(3)
-        else:
+        if r > 0:
             quant(T.vq[:], T.vs[:], T.vt[:], deps=(d_v,), sem=v_v)
+        else:
+            quant_e(0)
+            quant_e(1)
+        ab, trb, ss, ev = R("ab"), R("tr"), R("ss"), R("ev")
+        ca, cb = C2, C2 + H
+        k1 = ts(fb[:, ca + 16:ca + C + 1:16], rr[:, 27:784:28], colw, 1.0 / 64, A.subtract, A.mult,
+                deps=(k0, k1, v_c2))
+        k2 = ts(fb[:, cb + C:cb:-16], rr[:, 28:812:29], colw, 1.0 / 256, A.subtract, A.mult)
+        if r == 0:
+            quant_e(2)
+            quant_e(3)
+        v_ab = fresh()
+        scan(ab[:, 2 * C - 2::-2], m[:, C:0:-1], fb[:, ca + C:ca:-1], 0.0, A.mult, A.max, deps=(k1, k_ms), sem=v_ab)
+        scan(ab[:, 1:2 * C:2], m[:, H + C:H:-1], fb[:, cb + C:cb:-1], 0.0, A.mult, A.max, deps=(k2,), sem=v_ab)
+        copy_p(2)
         l0 = 0 if has_l else TM
         ln = 2 * TM if has_l and has_r else 128
         prev_d = []
         for b in range(4):
             t_d = mm(T.psp[:, 512 * b:512 * b + ln], T.eq[:, 128 * b:128 * b + 128], T.es[:, 128 * b:128 * b + 128],
-                     lqb[:, l0:l0 + ln], lsb[:, l0:l0 + ln], deps=[v_e, s_p, arr] + v_fill)
+                     lqb[:, l0:l0 + ln], lsb[:, l0:l0 + ln], deps=[v_e, s_p[b], arr] + v_fill)
             s_d = fresh()
             if has_l:
-                act(win[b][:, MID + 1:MID + 1 + TM], T.psp[:, 512 * b:512 * b + TM], F.Copy, deps=(t_d, g_z), sem=s_d)
+                act(win[:, WS * b + POFF - 1:WS * b + 1:-1], T.psp[:, 512 * b:512 * b + TM], F.Copy,
+                    deps=(t_d, s_m), sem=s_d)
             if has_r:
                 o = 512 * b + (TM if has_l else 0)
-                act(win[b][:, MID - TM:MID], T.psp[:, o:o + TM], F.Copy, deps=(t_d, g_z), sem=s_d)
+                act(win[:, WS * b + POFF + C:WS * b + POFF + C + TM], T.psp[:, o:o + TM], F.Copy,
+                    deps=(t_d, s_m), sem=s_d)
             prev_d.append(s_d)
-        k1 = ts(T.ab[:, 64:92], T.rr[:, 0:812:30], -1.0, sig, A.mult, A.add, deps=(k_r, v_cl))
-        k2 = ts(T.ab[:, 96:124], T.rr[:, 28:812:29], usig, 0.0, A.add, A.min)
-        k1 = tt(T.wf[:, 0:C:16], T.ab[:, 64:92], T.ab[:, 0:28], A.max, deps=(k1, k_ab))
-        k2 = tt(T.wb[:, 15:C:16], T.ab[:, 96:124], T.ab[:, 32:60], A.min, deps=(k2,))
-        k1 = scan(T.l2[:], dl[:], T.wf[:], float(POFF - 1), A.max, A.min, deps=(k1,))
-        k2 = scan(T.n2[:, ::-1], dl[:, ::-1], T.wb[:, ::-1], -111.0, A.min, A.max, deps=(k2,))
-        xa = tt(T.x1[:, 0:HALF], T.l2[:, 0:HALF], R("nd")[:, 0:HALF], A.min, deps=(k1, s_nd))
-        xb = tt(T.x1[:, HALF:C], T.l2[:, HALF:C], R("nd")[:, HALF:C], A.min)
-        va = tt(T.val[:, 16:16 + HALF], T.x1[:, 0:HALF], T.n2[:, 0:HALF], A.max, deps=(xa, k2))
-        vb = tt(T.val[:, 16 + HALF:16 + C], T.x1[:, HALF:C], T.n2[:, HALF:C], A.max, deps=(xb,))
-        k0 = tr(T.tt[:, C:C + HALF], T.val[:, 0:HALF], deps=(va,))
-        k1 = tr(T.tt[:, 0:C], T.val[:, 16:16 + C], deps=(vb,))
-        k2 = tr(T.tt[:, C + HALF:928], T.val[:, HALF:480])
-        k1 = scan(T.ss[:, 0:C], T.tt[:, 0:C], T.mk[:, 0:C], 0.0, A.add, A.mult, deps=(k1, s_mk))
-        k2 = scan(T.ss[:, C:928], T.tt[:, C:928], T.mk[:, C:928], 0.0, A.add, A.mult, deps=(k0, k2))
-        k1 = tt(T.ev[:, 0:28:2], T.ss[:, 15:448:32], T.ss[:, 479:896:32], A.add, deps=(k1, k2))
-        k2 = tt(T.ev[:, 1:28:2], T.ss[:, 495:928:32], T.ss[:, 31:448:32], A.add)
-        k_el = ts(R("el")[:], T.ev[:, 0:28], float(MID), None, A.add, deps=(k1, k2))
         xn, nq, ns = R("xn"), T["aq%d" % (r + 1)], T["as%d" % (r + 1)]
-        v_g = [fresh(), fresh()]
-        cut = CUTS[r + 1]
+        v_g, k_el = [fresh(), fresh()], [fresh(), fresh()]
+        part = ((0, 8), (8, 28))
 
-        def gather(h, b):
-            a0, a1 = cut[h], cut[h + 1]
-            tt(xn[:, 4 * a0 + b:4 * a1:4], win[b][:, 0:WINW].indirect(R("el")[:, a0 // 16:a1 // 16]),
-               T.pc[:, C * b + a0:C * b + a1], A.add, deps=(k_el, prev_d[b], s_p, g_z, s_pc, d_p), sem=v_g[h])
+        def least(a0, a1, d, sem=None):
+            return scan(ss[:, a0:a1], trb[:, a0:a1], T.mk[:, a0:a1], CAP, A.min, A.max, deps=(d, s_mk), sem=sem)
+
+        def decode(h, i, d):
+            a0, a1 = part[h]
+            if i == 0:
+                return tt(ev[:, a0:a1], ss[:, 15 + 16 * a0:16 * a1:16], ss[:, 479 + 16 * a0:464 + 16 * a1:16], A.min,
+                          deps=d)
+            if i == 1:
+                return ts(ev[:, 32 + a0:32 + a1], ev[:, a0:a1], -4.0, (2048.0 + C - 1) / 4096, A.mult, A.add, deps=d)
+            if i == 2:
+                return tt(ev[:, 64 + a0:64 + a1], ev[:, a0:a1], ev[:, 32 + a0:32 + a1], A.max, deps=d)
+            return ts(R("el")[:, a0:a1], ev[:, 64 + a0:64 + a1], 4096.0, POFF - 1024.0, A.mult, A.add, deps=d,
+                      sem=k_el[h])
+
+        def gather(a0, a1, b):
+            tt(xn[:, 4 * a0 + b:4 * a1:4], win[:, WS * b:WS * (b + 1)].indirect(R("el")[:, a0 // 16:a1 // 16]),
+               R("pc")[:, C * b + a0:C * b + a1], A.add, deps=(k_el[min(a0, 1)], prev_d[b], d_p), sem=v_g[a0 // MID])
 
         def requant(h):
-            a0, a1 = cut[h], cut[h + 1]
+            a0, a1 = CUT[h:h + 2]
             return quant(nq[:, a0:a1], ns[:, a0:a1], xn[:, 4 * a0:4 * a1], deps=(v_g[h],), sem=True)
 
+        va = scan(fb[:, SEL:SEL + 288], T.sg[:, 0:288], ab[:, 0:288], 0.0, A.min, A.max, deps=(v_ab, s_ev, s_a0, s_a1))
+        vb = scan(fb[:, SEL + 288:C2], T.sg[:, 288:2 * C], ab[:, 288:2 * C], 0.0, A.min, A.max)
+        k0 = tr(trb[:, C:608], fb[:, SEL - 31:SEL + 288:2], deps=(va,))
+        k1 = tr(trb[:, 0:128], fb[:, SEL + 1:SEL + 256:2])
+        k2 = tr(trb[:, 608:928], fb[:, SEL + 289:C2 + 32:2], deps=(vb,), sem=True)
+        k0 = least(C, 608, k0)
+        k1 = least(0, 128, k1)
+        k3 = tr(trb[:, 128:C], fb[:, SEL + 257:C2:2], sem=True)
+        k0 = decode(0, 0, (k0, k1))
+        k2 = least(608, 928, k2, True)
+        k0 = decode(0, 1, (k0,))
+        k3 = least(128, C, k3, True)
+        k0 = decode(0, 2, (k0,))
+        copy_p(3)
+        decode(0, 3, (k0,))
+        k1 = decode(1, 0, (k2, k3))
         for b in range(4):
-            gather(0, b)
-        gather(1, 0)
+            gather(0, 128, b)
+            if b < 3:
+                k1 = decode(1, b + 1, (k1,))
+        for b in range(4):
+            gather(128, MID, b)
+        gather(MID, C, 0)
         v_a = [requant(0)]
+        if r + 1 < ROUNDS:
+            t = scores(r + 1, 0, v_a[0])
+        else:
+            t = mm(T.pss[:, 0:MID], T.vq[:], T.vs[:], nq[:, 0:MID], ns[:, 0:MID], deps=(v_v, v_a[0]))
         for b in range(1, 4):
-            gather(1, b)
+            gather(MID, C, b)
+        if r + 1 < ROUNDS:
+            v_s0 = signs(0, t)
+        else:
+            v_y = cp(T.ysb[:, 0:MID], T.pss[:, 0:MID], deps=(t,), sem=True)
         v_a.append(requant(1))
 
     fq, fs = T["aq%d" % ROUNDS], T["as%d" % ROUNDS]
-    cut = CUTS[ROUNDS]
-    for h in range(2):
-        a0, a1 = cut[h], cut[h + 1]
-        t_y = mm(T.pss[:, 512 * h:512 * h + a1 - a0], T.vq[:], T.vs[:], fq[:, a0:a1], fs[:, a0:a1], deps=(v_v, v_a[h]))
-        dma("Y", T.oc[:, 4 * a0:4 * a1], fq[:, a0:a1].bitcast(dt.uint8), deps=(v_a[h],), sem="st")
-        s_y = act(T.ysb[:, a0:a1], T.pss[:, 512 * h:512 * h + a1 - a0], F.Copy, deps=(t_y,), sem=True)
-        dma("S", T.y[:, a0:a1], T.ysb[:, a0:a1], deps=(s_y,), sem="st")
-    for k in range(4):
-        dma("Y", T.osc[4 * k:4 * k + 4, :], fs[32 * k:32 * k + 4, :], deps=(), sem="st")
+    t = mm(T.pss[:, 512:512 + C - MID], T.vq[:], T.vs[:], fq[:, MID:C], fs[:, MID:C], deps=(v_a[1],))
+    dma("Y", T.oc[:, 0:4 * MID], fq[:, 0:MID].bitcast(dt.uint8), deps=(v_a[0],), sem="st")
+    dma("Y", T.y[:, 0:MID], T.ysb[:, 0:MID], deps=(v_y,), sem="st")
+    dma("Y", T.oc[:, 4 * MID:4 * C], fq[:, MID:C].bitcast(dt.uint8), deps=(v_a[1],), sem="st")
+    for k in range(3):
+        dma("Y", T.osc[4 * k:4 * k + 4, :], fs[32 * k:32 * k + 4, :], sem="st")
+    s_y = act(T.ysb[:, MID:C], T.pss[:, 512:512 + C - MID], F.Copy, deps=(t,))
+    dma("S", T.osc[12:16, :], fs[96:100, :], sem="st")
+    dma("S", T.y[:, MID:C], T.ysb[:, MID:C], deps=(s_y,), sem="st")
     wait("G", [s for s in tot if top.get(s, 0) < tot[s]])

@@ -8,35 +8,95 @@ MID = 320
 H = 464
 Z0 = 3072.0
 LOW = Z0 - 480
-U1 = 2.0 ** -24
-CAP = (1024 + C + TM) / 4096.0
+CAP = 1024.0 + C + TM
 POFF = 2 + TM
 WS = 656
 NP = 816
-SEL, C2 = 480, 480 + 2 * C
-NROT = 6
-D1 = 12
+SEL, C2 = 32, 32 + 2 * C
 CUT = (0, MID, C)
+GP = (0, 128, MID, C)
+PP = (0, 14, 28, 40, 51)
 Q4, U8, BF, F16, F32, I32, U16 = "float8_e4m3fn_x4", "uint8", "bfloat16", "float16", "float32", "int32", "uint16"
 SCRATCH = {}
 for _n, _w, _d in [
     ("xt", 4 * C, BF), ("ut", 512, BF), ("vt", 512, BF), ("wq", 512, Q4), ("wsc", 512, U8), ("uq", 128, Q4),
     ("us", 128, U8), ("uq2", 128, Q4), ("us2", 128, U8), ("vq", 128, Q4), ("vs", 128, U8), ("et", 520, BF),
     ("eq", 512, Q4), ("es", 512, U8), ("pi", 8, I32), ("pj", 8, I32), ("cl", 8, F32), ("nf", 52, F32),
-    ("lui", 8, I32), ("lu", 8, U16), ("lp", 52, U16), ("tw", 16 * 52, F32), ("one", C, BF), ("sb", C, BF),
-    ("wi", 52, I32), ("c1", 480, F16), ("fb", C2 + 2 * H, F16), ("pat", 928, BF), ("mk", 928, BF),
-    ("mask", NP, BF), ("sg", 2 * C, BF), ("ysb", C, F32), ("aq0", C, Q4), ("as0", C, U8), ("z", 2 * H, BF),
-    ("kt", 192, BF), ("tb", 128, F32), ("nc", 2 * H, F16), ("m", 2 * H, BF), ("win", 4 * WS, BF),
+    ("lui", 8, I32), ("lu", 8, U16), ("lp", 52, U16), ("tw", 17 * 52, F32), ("wi", 52, I32),
+    ("fb", C2 + 2 * H, F16), ("pat", 928, BF), ("mk", 928, BF), ("mask", NP, BF), ("sg", 2 * C, BF),
+    ("ysb", C, F32), ("z", 2 * H, BF), ("kt", 448, BF), ("nw", 64, BF), ("fd", 608, BF), ("nc", 2 * H, F16),
+    ("m", 2 * H, BF), ("win", 4 * WS, BF), ("m01", 768, BF), ("dz", 2 * H, BF), ("acc", 8, F32), ("ec", 348, BF),
+    ("rm", 348, BF), ("ml", 12, U16), ("mt", 8 * TM, BF), ("dg", NP, BF), ("ee", NP, BF), ("wn", NP, BF),
+    ("rr", NP, BF), ("ab", 2 * C, F16), ("tr", 928, F16), ("ss", 928, F16), ("ev", 96, F32), ("el", 28, U16),
+    ("xn", 4 * C, BF), ("pc", 2 * C, BF), ("ib", 4 * C, BF),
 ] + [(_n + str(_r), _w, _d) for _r in range(ROUNDS) for _n, _w, _d in [
-    ("dz", 2 * H, BF), ("vv", 64, BF), ("acc", 8, F32), ("ec", 384, BF), ("rm", 384, F32),
-    ("ml", 12, U16), ("mt", 8 * TM, BF), ("mq", 2 * TM, Q4), ("ms", 2 * TM, U8), ("lq_", 320, Q4), ("ls_", 320, U8),
-    ("dg", NP, BF), ("ee", NP, BF), ("wn", NP, BF), ("rr", NP, F16), ("ab", 2 * C, F16), ("tr", 928, F16),
-    ("ss", 928, F16), ("ev", 96, F32), ("el", 28, U16), ("xn", 4 * C, BF), ("pc", 4 * C, BF)]
-] + [("aq1", C, Q4), ("as1", C, U8), ("aq2", C, Q4), ("as2", C, U8)]:
+    ("mq", 2 * TM, Q4), ("ms", 2 * TM, U8), ("lq", 320, Q4), ("ls", 320, U8)]
+] + [(_n + str(_r), C, _d) for _r in range(ROUNDS + 1) for _n, _d in [("aq", Q4), ("as", U8)]]:
     SCRATCH[_n] = ("sbuf", [128, _w], _d)
 SCRATCH["pss"] = ("psum", [128, 1024], F32)
 SCRATCH["psp"] = ("psum", [128, 2048], F32)
-SEMAPHORES = (["arr0", "arr1", "loc", "st"] + ["cV%d" % _i for _i in range(NROT)] + ["k%d" % _i for _i in range(139)])
+NSEM = 140
+SEMAPHORES = ["arr0", "arr1", "loc", "st"] + ["k%d" % _i for _i in range(NSEM)]
+
+ON_V = "dg0 dl3 dr0 dr1 mo0 mo1 wn2 yc1"
+ORDER = {
+    "V": "one res kt par hi colz ca z1 l0 colw lu l1 cb lq uq cmb nhi l9 l2 uq2 us2 l6 col0 l3 z2 q0_0 l4 l7 l11 fil l5 "
+         "l8 q1_0 e3 e1 l13 l10 l12 za_0 z0 k0_0 zb_0 l14 zc_0 kb_0 fa_0 fx_0 ka_0 l15 e0_0 kp_0 e1_0 l16 nz_0 ta_0 "
+         "t2_0 key_0 l17 e2_0 t1_0 e3_0 tb_0 df_0 lp rm1_0 rm0_0 rm2_0 da_0 mlb_0 mla_0 ma_0 mo0_0 mo1_0 e0 mq_0 dg0_0 "
+         "wn2_0 dx_0 ee0_0 mx_0 ee1_0 rr0_0 rr1_0 e2 fl_0 ib_0 ia_0 sb_0 sa_0 vq vb_0 va_0 r2_0 r3_0 r1_0 r0_0 n3_0 "
+         "n1_0 n0_0 n2_0 o00_0 dl3_0 o01_0 o10_0 o11_0 o20_0 dr1_0 o21_0 el0_0 el1_0 dr0_0 x03_0 x01_0 x02_0 x00_0 "
+         "ad1_0 ad2_0 x12_0 x10_0 x22_0 q0_1 x20_0 q1_1 fl_1 za_1 k0_1 da_1 zb_1 zc_1 fa_1 fx_1 kb_1 ka_1 kp_1 key_1 "
+         "e1_1 e0_1 tb_1 dx_1 nz_1 df_1 e2_1 ta_1 t1_1 e3_1 t2_1 ma_1 rm2_1 rm1_1 rm0_1 wn2_1 mlb_1 mla_1 mx_1 mo0_1 "
+         "mo1_1 dg0_1 mq_1 ee0_1 ee1_1 rr0_1 rr1_1 ib_1 ia_1 sb_1 sa_1 vb_1 va_1 r2_1 r0_1 r1_1 r3_1 n2_1 n1_1 n0_1 "
+         "n3_1 o00_1 dl3_1 o01_1 o10_1 dr0_1 o11_1 o20_1 o21_1 el0_1 dr1_1 el1_1 x00_1 x03_1 x01_1 x02_1 ad1_1 x12_1 "
+         "x10_1 ad2_1 q0_2 x20_1 x22_1 q1_2 yc0 yc1",
+    "S": "du w2 m0 w0 w1 m1 w4 sev w3 sg0_0 sg1_0 c1_0 c0_0 c3_0 c2_0 mo3_0 mo2_0 dg1_0 dg3_0 wn0_0 dg2_0 wn1_0 wn3_0 "
+         "mk dl1_0 dl0_0 dl2_0 dr3_0 dr2_0 h13_0 h11_0 h21_0 h23_0 sg0_1 sg1_1 c3_1 c1_1 c2_1 c0_1 dg3_1 dg2_1 dg1_1 "
+         "mo2_1 mo3_1 wn0_1 wn1_1 wn3_1 dl0_1 dl2_1 dl1_1 dr3_1 dr2_1 h11_1 h13_1 h21_1 h23_1 yc0 sy1 ss3",
+    "T": "sc0_0 sc1_0 p1_0 p0_0 p3_0 p2_0 u1_0 u0_0 u3_0 u2_0 sc0_1 sc1_1 p3_1 p1_1 p2_1 p0_1 u0_1 u3_1 u2_1 u1_1 y0 y1",
+    "G": "gp gn glu gf0 gw0 gf2 ge gm1 gf1 gw1 gm0 gpat sd0_0 sd1_0 gz_0 ib1_0 ib3_0 ib3_1 gz_1 sd0_1 sd1_1 ib1_1 end",
+    "Y": "dx0 dx1 dw dws dv pc0_0 pc2_0 pc2_1 pc0_1 so0 so1 ss1 sy0 ss0 ss2",
+}
+
+
+def emit(g, T, ops, fixed):
+    Q = {"V": g.vector, "S": g.scalar, "T": g.tensor, "G": g, "Y": g.sync}
+    order = {q: [n for n in ORDER[q].split() if n in ops and ops[n][0] == q] for q in Q}
+    assert sum(len(v) for v in order.values()) == len(ops)
+    pos, know, done, seq, waits = {q: 0 for q in Q}, {q: set() for q in Q}, {}, [], {}
+    while len(seq) < len(ops):
+        n0 = len(seq)
+        for q in Q:
+            while pos[q] < len(order[q]) and all(d in done or d in fixed for d in ops[order[q][pos[q]]][2]):
+                n = order[q][pos[q]]
+                deps = [d for d in ops[n][2] if d not in know[q]]
+                deps = [d for d in deps if not any(e != d and d in done.get(e, ()) for e in deps)]
+                for d in deps:
+                    know[q] |= done.get(d, {d})
+                waits[n], done[n] = deps, know[q] | {n}
+                seq.append(n)
+                pos[q] += 1
+        assert len(seq) > n0
+    needed = {d for w in waits.values() for d in w}
+    last, count, sig, n_dma = {}, {}, dict(fixed), [0]
+    for n in seq:
+        q, f, _, inc = ops[n]
+        for s, v in sorted({sig[d] for d in waits[n]}):
+            Q[q].wait_ge(T.sem[s], v)
+        if f is None:
+            continue
+        call = f()
+        if inc == "st":
+            call.then_inc(T.sem["st"], 16)
+        elif n in needed:
+            if inc == 16:
+                n_dma[0] += 1
+                s = "k%d" % (NSEM - n_dma[0])
+            else:
+                s = next("k%d" % i for i in range(NSEM - 16) if last.get("k%d" % i, n) in done[n])
+            last[s], count[s] = n, count.get(s, 0) + inc
+            sig[n] = (s, count[s])
+            call.then_inc(T.sem[s], inc)
 
 
 def rank_program(g, core, T, topo):
@@ -45,160 +105,140 @@ def rank_program(g, core, T, topo):
         return
     n_ranks = len(T.cores)
     has_l, has_r = rank > 0, rank < n_ranks - 1
-    Q = {"V": g.vector, "S": g.scalar, "T": g.tensor, "G": g, "Y": g.sync}
-    tot, seen, top, nk, nrot = {}, {}, {}, [0], [0]
-
-    def fresh():
-        nk[0] += 1
-        return "k%d" % (nk[0] - 1)
-
-    def wait(q, toks):
-        for s in toks:
-            v = tot[s]
-            assert s[0] != "c" or s[1] == q or q == "G"
-            if seen.get((q, s), 0) < v:
-                Q[q].wait_ge(T.sem[s], v)
-                seen[(q, s)] = v
-                top[s] = max(top.get(s, 0), v)
-
-    def op(q, f, deps=(), sem=None, n=1):
-        wait(q, deps)
-        if sem is None:
-            s = "cV%d" % (nrot[0] % NROT)
-            nrot[0] += 1
-        else:
-            s = fresh() if sem is True else sem
-        f().then_inc(T.sem[s], n)
-        tot[s] = tot.get(s, 0) + n
-        return s
-
     V, S, PE = g.vector, g.scalar, g.tensor
+    ops, fixed, rnd = {}, {}, [0]
 
-    def ts(out, in0, s1, s2, o0, o1=None, deps=(), sem=None):
+    def op(name, q, f, deps="", inc=1):
+        fix = lambda s: s.replace("#", "_%d" % rnd[0]).replace("$", "_%d" % (rnd[0] + 1))
+        ops[fix(name)] = (q, f, fix(deps).split(), inc)
+
+    def ts(n, d, out, in0, s1, s2, o0, o1=None):
         if o1 is None:
-            return op("V", lambda: V.tensor_scalar(out, in0, s1, None, o0), deps, sem)
-        return op("V", lambda: V.tensor_scalar(out, in0, s1, s2, o0, o1), deps, sem)
+            op(n, "V", lambda: V.tensor_scalar(out, in0, s1, None, o0), d)
+        else:
+            op(n, "V", lambda: V.tensor_scalar(out, in0, s1, s2, o0, o1), d)
 
-    def tt(out, a, b, o, deps=(), sem=None):
-        return op("V", lambda: V.tensor_tensor(out, a, b, o), deps, sem)
+    def tt(n, d, out, a, b, o):
+        op(n, "V", lambda: V.tensor_tensor(out, a, b, o), d)
 
-    def cp(out, a, deps=(), sem=None):
-        return op("V", lambda: V.tensor_copy(out, a), deps, sem)
+    def cp(n, d, out, a):
+        op(n, "V", lambda: V.tensor_copy(out, a), d)
 
-    def scan(out, a, b, init, o0, o1, deps=(), sem=None):
-        return op("V", lambda: V.tensor_tensor_scan(out, a, b, init, o0, o1), deps, sem)
+    def scan(n, d, out, a, b, init, o0, o1):
+        op(n, "V", lambda: V.tensor_tensor_scan(out, a, b, init, o0, o1), d)
 
-    def tr(out, a, deps=(), sem=None):
-        return op("V", lambda: V.transpose(out, a), deps, sem)
+    def tr(n, d, out, a):
+        op(n, "V", lambda: V.transpose(out, a), d)
 
-    def ms(ap, c, deps=(), sem=None):
-        return op("V", lambda: V.memset(ap, c), deps, sem)
+    def ms(n, d, ap, c):
+        op(n, "V", lambda: V.memset(ap, c), d)
 
-    def quant(oc, osc, src, deps=(), sem=None):
-        return op("V", lambda: V.quantize_mx(oc, osc, src), deps, sem)
+    def quant(n, d, oc, osc, src):
+        op(n, "V", lambda: V.quantize_mx(oc, osc, src), d)
 
-    def act(out, a, fn, deps=(), sem=True, **kw):
-        return op("S", lambda: S.activation(out, a, fn, **kw), deps, sem)
+    def act(n, d, out, a, fn, **kw):
+        op(n, "S", lambda: S.activation(out, a, fn, **kw), d)
 
-    def pick(q, out, a, deps, sem):
-        return cp(out, a, deps, sem) if q == "V" else act(out, a, F.Copy, deps, sem)
+    def pick(n, d, out, a, scale=None):
+        if n.rstrip("#") not in ON_V.split():
+            act(n, d, out, a, F.Copy, scale=scale or 1.0)
+        elif scale:
+            ts(n, d, out, a, scale, None, A.mult)
+        else:
+            cp(n, d, out, a)
 
-    def mm(out, lq, ls, rq, rs, deps=(), sem=True):
-        return op("T", lambda: PE.matmul_mx(out, lq, ls, rq, rs, True, True), deps, sem)
+    def mm(n, d, out, lq, ls, rq, rs):
+        op(n, "T", lambda: PE.matmul_mx(out, lq, ls, rq, rs, True, True), d)
 
-    def dma(q, out, src, deps=(), sem=True):
-        return op(q, lambda: Q[q].dma_start(out, src), deps, sem, 16)
+    def dma(n, q, d, out, src, inc=16):
+        op(n, q, lambda: (g.sync if q == "Y" else S).dma_start(out, src), d, inc)
 
-    def iota(out, pat, base, cm=0, sem=True, small=True):
+    def iota(n, d, out, pat, base, cm=0, small=True):
         if small:
-            return op("G", lambda: g.iota(out, pat, base, cm, allow_small_or_imprecise_dtypes=True), (), sem)
-        return op("G", lambda: g.iota(out, pat, base, cm), (), sem)
+            op(n, "G", lambda: g.iota(out, pat, base, cm, allow_small_or_imprecise_dtypes=True), d)
+        else:
+            op(n, "G", lambda: g.iota(out, pat, base, cm), d)
 
-    d_u = dma("S", T.ut[:], T.u[:])
-    d_x = [dma("Y", T.xt[:, 4 * CUT[h]:4 * CUT[h + 1]], T.x[:, 4 * CUT[h]:4 * CUT[h + 1]]) for h in range(2)]
-    d_w = fresh()
-    dma("Y", T.wq[:].bitcast(dt.uint8), T.wc[:], sem=d_w)
-    dma("Y", T.wsc[:], T.ws[:], sem=d_w)
-    d_v = dma("Y", T.vt[:], T.v[:], deps=(d_w,))
+    win, z, nc, m, fb, kt, fd, mask, sg, dz, acc = (T.win, T.z, T.nc, T.m, T.fb, T.kt, T.fd, T.mask, T.sg, T.dz,
+                                                    T.acc)
+    dma("du", "S", "", T.ut[:], T.u[:])
+    for h in range(2):
+        dma("dx%d" % h, "Y", "", T.xt[:, 4 * CUT[h]:4 * CUT[h + 1]], T.x[:, 4 * CUT[h]:4 * CUT[h + 1]])
+    dma("dw", "Y", "", T.wq[:].bitcast(dt.uint8), T.wc[:])
+    dma("dws", "Y", "", T.wsc[:], T.ws[:])
+    dma("dv", "Y", "dw", T.vt[:], T.v[:])
 
-    win, z, nc, tb, m, fb = T.win, T.z, T.nc, T.tb, T.m, T.fb
-    key, td = T.kt, T.kt[:, 64:192]
-    g_p = iota(T.pi[:, 0:1], [[0, 1]], 0, 1, small=False)
-    g_lu = iota(T.lui[:], [[16, 8]], 0, small=False)
-    g_n = iota(T.nf[:], [[16, 52]], 0)
-    g_k, g_z = fresh(), fresh()
-    iota(z[:, 0:2 * H:H], [[0, 2]], int(Z0), sem=g_k)
-    iota(m[:, C:2 * H:H], [[0, 2]], 0, sem=g_k)
-    iota(T.kt[:], [[0, 192]], int(LOW), sem=g_k)
-    iota(win[:, 0:POFF], [[0, POFF]], 0, sem=g_z)
-    iota(win[:, 3 * WS + POFF + C:4 * WS], [[0, WS - POFF - C]], 0, sem=g_z)
-    v_one = ms(T.mask[:], 1.0, sem=True)
-    g_e = op("G", lambda: g.affine_select(T.et[:], T.mask[:, 0:520], [[-1, 520]], A.is_equal, 0.0, 3, 4), (v_one,), True)
-    g_pat = iota(T.pat[:], [[0, 29], [1, 2], [0, 16]], 0)
-    s_1 = act(T.one[:], T.mask[:, 0:C], F.Copy, deps=(v_one,))
-    for b in range(3):
-        act(win[:, WS * b + POFF + C:WS * (b + 1) + POFF], T.mask[:, 0:WS - C], F.Copy, sem=g_z, scale=0.0)
-    s_ev = act(T.sg[:, 0:2 * C:2], T.mask[:, 0:C], F.Copy, scale=-1.0)
-
-    v_p, v_c, v_l, v_u = fresh(), fresh(), fresh(), fresh()
+    iota("gp", "", T.pi[:, 0:1], [[0, 1]], 0, 1, small=False)
+    iota("glu", "", T.lui[:], [[16, 8]], 0, small=False)
+    iota("gn", "", T.nf[:], [[16, 52]], 0)
+    iota("gf0", "", fd[:], [[0, 304], [2, 2]], 0)
+    iota("gf1", "gf0", fd[:, 15:608:16], [[0, 38]], 4096)
+    iota("gf2", "gf0", fd[:, C - MID:608:H], [[0, 2]], 4096)
+    iota("gw0", "", T.nw[:, 0:58], [[0, 2], [-16, 29]], 249)
+    iota("gw1", "gw0", T.nw[:, 28:58:29], [[0, 2]], 256 - C - TM)
+    ms("one", "", mask[:], 1.0)
+    op("ge", "G", lambda: g.affine_select(T.et[:], mask[:, 0:520], [[-1, 520]], A.is_equal, 0.0, 3, 4), "one")
+    iota("gpat", "", T.pat[:], [[0, 29], [1, 2], [0, 16]], 0)
+    act("w0", "one", win[:, 0:POFF], mask[:, 0:POFF], F.Copy, scale=0.0)
+    for b in range(4):
+        w = WS - C if b < 3 else WS - C - POFF
+        act("w%d" % (b + 1), "one", win[:, WS * b + POFF + C:WS * b + POFF + C + w], mask[:, 0:w], F.Copy, scale=0.0)
+    act("sev", "one", sg[:, 0:2 * C:2], mask[:, 0:C], F.Copy, scale=-1.0)
+    act("m0", "one", T.m01[:, 0:768:2], mask[:, 0:384], F.Copy, scale=0.0)
+    act("m1", "one", T.m01[:, 1:768:2], mask[:, 0:384], F.Copy)
     res, hi, par = T.pj[:, 0:1], T.pj[:, 1:2], T.pj[:, 2:3]
-    colz, col0, colw, nhi = [T.cl[:, i:i + 1] for i in range(4)]
-    tw = [T.tw[:, 52 * i:52 * i + 52] for i in range(16)]
+    colz, col0, colw, nhi, cmb = [T.cl[:, i:i + 1] for i in range(5)]
+    ts("res", "gp", res, T.pi[:, 0:1], 15, None, A.bitwise_and)
+    ts("hi", "gp", hi, T.pi[:, 0:1], 4, 1, A.logical_shift_right, A.bitwise_and)
+    ts("par", "gp", par, T.pi[:, 0:1], 1, None, A.bitwise_and)
+    ts("colz", "res", colz, res, Z0 - 7.5, None, A.add)
+    ts("colw", "par", colw, par, 1280.0, None, A.add)
+    ts("cmb", "par", cmb, par, -1.0, POFF + C - 257.0, A.mult, A.add)
+    ts("col0", "colz colw", col0, colz, colw, C + 1024 + 7.5, A.subtract, A.add)
+    ts("nhi", "hi", nhi, hi, -CAP, None, A.mult)
+    act("mk", "gpat nhi", T.mk[:], T.pat[:], F.Abs, scale=CAP, bias=nhi)
+    cp("lu", "glu", T.lu[:], T.lui[:])
+    quant("uq", "du", T.uq[:], T.us[:], T.ut[:])
+    cp("uq2", "uq lu", T.uq2[:].bitcast(dt.uint32), T.uq[:].bitcast(dt.uint32).indirect(T.lu[:, 0:8]))
+    cp("us2", "uq lu", T.us2[:], T.us[:].indirect(T.lu[:, 0:8]))
+    ca, cb = C2, C2 + H
+    scan("ca", "one", fb[:, ca:ca + C + 1], mask[:, 0:C + 1], mask[:, 0:C + 1], 1023.0, A.add, A.mult)
+    ts("cb", "ca", fb[:, cb:cb + C + 1], fb[:, ca:ca + C + 1], 0.25, None, A.mult)
+    ts("fil", "one", fb[:, 0:SEL], mask[:, 0:SEL], 2048.0, None, A.mult)
+    ms("z0", "", z[:, 0:2 * H:H], Z0)
+    ms("z1", "", z[:, C + 1:H], LOW)
+    ms("z2", "", z[:, H + C + 1:2 * H], LOW)
+    ms("kt", "", kt[:], LOW)
+    iota("gm0", "ge w0 w1 w2 w3 w4 sev m0 m1 ca fil", mask[:, 0:812:29], [[0, 28]], 0)
+    iota("gm1", "ge w0 w1 w2 w3 w4 sev m0 m1 ca fil", mask[:, 28:812:28], [[0, 28]], 0)
+    for b in range(4):
+        quant("e%d" % b, "ge", T.eq[:, 128 * b:128 * b + 128], T.es[:, 128 * b:128 * b + 128], T.et[:, 3 - b:515 - b])
+    quant("vq", "dv", T.vq[:], T.vs[:], T.vt[:])
+    tw = [T.tw[:, 52 * i:52 * i + 52] for i in range(17)]
     qv = T.wi[:]
-    ts(res, T.pi[:, 0:1], 15, None, A.bitwise_and, deps=(g_p,), sem=v_p)
-    ts(hi, T.pi[:, 0:1], 4, 1, A.logical_shift_right, A.bitwise_and, sem=v_p)
-    ts(par, T.pi[:, 0:1], 1, None, A.bitwise_and, sem=v_p)
-    k_lu = cp(T.lu[:], T.lui[:], deps=(g_lu,), sem=True)
-    k_ci = scan(fb[:, 0:480], T.mask[:, 0:480], T.mask[:, 0:480], 1023.0, A.add, A.mult, deps=(v_one,))
-    k0 = ts(colz, res, Z0 - 7.5, None, A.add, deps=(v_p,))
-    ts(col0, res, 1024 + C + Z0, None, A.add, sem=v_c)
-    ms(tb[:], (1024 + C + TM) * 2.0 ** -20, sem=v_c)
-    k_ci = ts(fb[:, C:C + 1], T.nf[:, 0:1], 2048.0, None, A.add, deps=(k_ci, g_n), sem=True)
-    k1 = ts(tw[0], T.nf[:], colz, 7.5 - Z0, A.add, A.add, deps=(k0,))
-    k0 = quant(T.uq[:], T.us[:], T.ut[:], deps=(d_u,))
-    ts(colw, par, -1.0 / 64, -1296.0 / 64, A.mult, A.add, sem=v_c)
-    ts(nhi, hi, -CAP, None, A.mult, sem=v_c)
-    k2 = ts(tw[1], tw[0], -14.0, 1.0 / 29, A.add, A.mult, deps=(k1,))
-    cp(T.uq2[:].bitcast(dt.uint32), T.uq[:].bitcast(dt.uint32).indirect(T.lu[:, 0:8]), deps=(k0, k_lu), sem=v_u)
-    k3 = cp(qv, tw[1], deps=(k2,))
-    cp(T.us2[:], T.us[:].indirect(T.lu[:, 0:8]), sem=v_u)
-    k4 = ts(tw[2], qv, -29.0, None, A.mult, deps=(k3,))
-
-    def scores(r, h, dep):
-        a0, a1 = CUT[h:h + 2]
-        return mm(T.pss[:, 512 * h:512 * h + a1 - a0], T.uq2[:], T.us2[:], T["aq%d" % r][:, a0:a1],
-                  T["as%d" % r][:, a0:a1], deps=(v_u, dep))
-
-    def signs(h, dep):
-        a0, a1 = CUT[h:h + 2]
-        return ts(T.sb[:, a0:a1], T.pss[:, 512 * h:512 * h + a1 - a0], 0.0, 2.0, A.is_ge, A.mult, deps=(dep,), sem=True)
-
-    v_a = [quant(T.aq0[:, CUT[h]:CUT[h + 1]], T.as0[:, CUT[h]:CUT[h + 1]], T.xt[:, 4 * CUT[h]:4 * CUT[h + 1]],
-                 deps=(d_x[h],), sem=True) for h in range(2)]
-    t_s0 = scores(0, 0, v_a[0])
-    k5 = tt(tw[3], tw[2], tw[0], A.add, deps=(k4,), sem=True)
-    ts(T.c1[:], fb[:, 0:480], U1, None, A.mult, deps=(k_ci,), sem=v_c)
-    e = tt(tw[4], tw[3], qv, A.add, deps=(k5,))
-    ts(tw[6], qv, -1.0, 57.0, A.mult, A.add, sem=v_l)
-    v_s0 = signs(0, t_s0)
-    ts(tw[9], qv, 37.0, None, A.add, sem=v_l)
-    ts(tw[8], tw[3], 0.0, None, A.is_equal, sem=v_l)
-    ts(tw[5], tw[4], 28.0, None, A.is_ge, deps=(e,), sem=v_l)
-    ts(tw[11], qv, -1.0, 64.0, A.mult, A.add, sem=v_l)
-    kl = {}
-    late = [
-        lambda: kl.update(c=ts(tw[10], tw[4], 28.0, None, A.is_equal)),
-        lambda: kl.update(e=ts(tw[7], tw[3], -1.0, 28.0, A.mult, A.add, sem=True)),
-        lambda: kl.update(d=tt(tw[12], tw[5], tw[6], A.mult, deps=(v_l,), sem=True)),
-        lambda: kl.update(c=tt(tw[14], tw[10], tw[11], A.mult, deps=(kl["c"],), sem=True)),
-        lambda: kl.update(b=tt(tw[13], tw[8], tw[9], A.mult, sem=True)),
-        lambda: kl.update(a=tt(tw[15], tw[12], tw[7], A.add, deps=(kl["d"], kl["e"]), sem=True)),
-        lambda: kl.update(b=tt(tw[1], tw[13], tw[14], A.add, deps=(kl["b"], kl["c"]), sem=True)),
-    ]
-
-    def quant_e(b):
-        quant(T.eq[:, 128 * b:128 * b + 128], T.es[:, 128 * b:128 * b + 128], T.et[:, 3 - b:515 - b],
-              deps=(g_e,), sem=v_e)
+    ts("l0", "gn colz", tw[0], T.nf[:], colz, 7.5 - Z0, A.add, A.add)
+    ts("l1", "l0", tw[1], tw[0], -14.0, 1.0 / 29, A.add, A.mult)
+    cp("lq", "l1", qv, tw[1])
+    ts("l2", "lq", tw[2], qv, -29.0, None, A.mult)
+    tt("l3", "l2", tw[3], tw[2], tw[0], A.add)
+    tt("l4", "l3", tw[4], tw[3], qv, A.add)
+    ts("l5", "l4", tw[5], tw[4], 28.0, None, A.is_ge)
+    ts("l6", "lq", tw[6], qv, -1.0, 57.0, A.mult, A.add)
+    ts("l7", "l3", tw[7], tw[3], -1.0, 28.0, A.mult, A.add)
+    ts("l8", "l3", tw[8], tw[3], 0.0, None, A.is_equal)
+    ts("l9", "lq", tw[9], qv, 37.0, None, A.add)
+    ts("l10", "l4", tw[10], tw[4], 28.0, None, A.is_equal)
+    ts("l11", "lq", tw[11], qv, -1.0, 64.0, A.mult, A.add)
+    tt("l12", "l5 l6", tw[12], tw[5], tw[6], A.mult)
+    tt("l13", "l8 l9", tw[13], tw[8], tw[9], A.mult)
+    tt("l14", "l10 l11", tw[14], tw[10], tw[11], A.mult)
+    tt("l15", "l12 l7", tw[15], tw[12], tw[7], A.add)
+    tt("l16", "l13 l14", tw[16], tw[13], tw[14], A.add)
+    tt("l17", "l15 l16", tw[2], tw[15], tw[16], A.add)
+    ts("lp", "l17", T.lp[:], tw[2], 121.0, None, A.min)
+    for h in range(2):
+        quant("q%d_0" % h, "dx%d" % h, T.aq0[:, CUT[h]:CUT[h + 1]], T.as0[:, CUT[h]:CUT[h + 1]],
+              T.xt[:, 4 * CUT[h]:4 * CUT[h + 1]])
 
     def link(src_rank, dst_rank):
         src, dst = T.cores[src_rank], T.cores[dst_rank]
@@ -209,259 +249,162 @@ def rank_program(g, core, T, topo):
         rid, pid, _ = topo.addr(dst)
         return DstId(rid=rid, pnc=pid), sum(1 << e for e in eng), len(eng)
 
-    tot["loc"] = 0
-    s_mk = v_lp = None
-    v_e, v_v, v_m, v_c2 = fresh(), fresh(), fresh(), fresh()
-    prev_d = []
-    both = [fresh() for _ in range(14)]
+    others = [o for o in (rank - 1, rank + 1) if 0 <= o < n_ranks]
+    fixed["loc"] = ("loc", 2 * ROUNDS * sum(link(rank, o)[2] for o in others))
+    key, td, keyp, tb, tbw = kt[:, 0:58], kt[:, 64:192], kt[:, 192:250], kt[:, 320:378], kt[:, 320:448]
+    fv = nc[:, 0:2 * H:16]
+    plane = lambda b: win[:, WS * b:WS * (b + 1)]
+    own = lambda b: win[:, WS * b + POFF:WS * b + POFF + C]
     for r in range(ROUNDS):
-        R = lambda name: T[name + str(r)]
-        aq, asc = T["aq%d" % r], T["as%d" % r]
-        dz, acc = R("dz"), R("acc")
-        lqb, lsb = R("lq_"), R("ls_")
+        rnd[0] = r
+        aq, asc, nq, ns = T["aq%d" % r], T["as%d" % r], T["aq%d" % (r + 1)], T["as%d" % (r + 1)]
+        mq, msc, lqb, lsb = T["mq%d" % r], T["ms%d" % r], T["lq%d" % r], T["ls%d" % r]
         arr = "arr%d" % r
-        t_s1 = scores(r, 1, v_a[1])
-        v_z, zb, v_t, v_k, v_d, v_w = both[0:6]
-        s_p, d_p, v_f, v_rm, v_ml = both[6:10], both[10], both[11], both[12], both[13]
-        vv, ec, rm = R("vv"), R("ec"), R("rm")
-
-        def plane(b):
-            t = mm(T.psp[:, 512 * b:512 * b + C], T.wq[:, 128 * b:128 * b + 128], T.wsc[:, 128 * b:128 * b + 128],
-                   aq[:], asc[:], deps=[d_w] + prev_d)
-            act(win[:, WS * b + POFF:WS * b + POFF + C], T.psp[:, 512 * b:512 * b + C], F.Copy, deps=(t,), sem=s_p[b],
-                scale=0.0625)
-
-        def level(a0, a1, init, deps):
-            return scan(z[:, a0 + 1:a1 + 1], T.sb[:, a0:a1], T.one[:, a0:a1], init, A.add, A.subtract, deps=deps,
-                        sem=v_z)
-
-        def event(a0, a1, deps):
-            return scan(dz[:, a0:a1], z[:, a0 + 1:a1 + 1], z[:, a0:a1], 0.0, A.max, A.subtract, deps=deps)
-
-        def factor(a0, a1, deps, sem=None):
-            return ts(m[:, a0:a1], dz[:, a0:a1], 1.0 / 16, 1.0, A.mult, A.add, deps=deps, sem=sem)
-
-        def valid(h, d):
-            return ts(vv[:, 29 * h:29 * h + 28], nc[:, H * h:H * h + C:16], 2048 * U1, 16.0, A.is_lt, A.mult, deps=(d,))
-
-        def keys(h, d):
-            tt(key[:, 29 * h:29 * h + 28], z[:, H * h:H * h + C:16], vv[:, 29 * h:29 * h + 28], A.subtract,
-               deps=(d,), sem=v_k)
-            tt(tb[:, 29 * h:29 * h + 28], nc[:, H * h:H * h + C:16], vv[:, 29 * h:29 * h + 28], A.mult, sem=v_t)
-
-        def total(h, dep):
+        fixed[arr] = (arr, sum(2 * link(o, rank)[2] for o in others))
+        for h in range(2):
             a0, a1 = CUT[h:h + 2]
-            return act(T.sg[:, 2 * a0 + 1:2 * a1:2], T.sb[:, a0:a1], F.Identity, deps=(dep,), bias=-1.0,
-                       accum_out=acc[:, h:h + 1])
-
-        def copy_p(b):
-            cp(R("pc")[:, C * b:C * (b + 1)], win[:, WS * b + POFF:WS * b + POFF + C], deps=(s_p[b],), sem=d_p)
-
-        s_a0 = total(0, v_s0)
-        level(0, MID, colz, (v_s0, s_1))
-        if r == 0:
-            for f in late[0:3]:
-                f()
-        k1 = event(0, MID, (v_z, g_k))
-        v_s1 = signs(1, t_s1)
-        plane(0)
-        s_a1 = total(1, v_s1)
-        for b in range(1, 4):
-            plane(b)
-        factor(0, MID, (k1,), v_f)
-        k0 = ts(acc[:, 5:6], acc[:, 0:1], colz, None, A.add, deps=(s_a0,))
-        scan(z[:, H + 1:H + C + 1], T.one[:], T.sb[:, ::-1], colz, A.add, A.subtract, deps=(v_s1,), sem=zb)
-        level(MID, C, acc[:, 5:6], (k0,))
-        if r == 0:
-            for f in late[3:5]:
-                f()
-        k3 = event(H, H + C, (zb,))
-        k2 = event(MID, C, (v_z,))
-        ka = ts(acc[:, 3:4], acc[:, 0:1], acc[:, 1:2], col0, A.add, A.add, deps=(s_a1, v_c), sem=True)
-        kb = ts(acc[:, 4:5], acc[:, 0:1], acc[:, 1:2], col0, A.add, A.subtract, sem=True)
-        k3 = factor(H, H + C, (k3,))
-        factor(MID, C, (k2,), v_f)
-        ts(tb[:, 64:93], z[:, 0:C + 1:16], acc[:, 3:4], -2.0 ** -20, A.subtract, A.mult, deps=(ka,), sem=v_w)
-        ts(tb[:, 93:122], z[:, H:H + C + 1:16], acc[:, 4:5], -2.0 ** -20, A.add, A.mult, deps=(kb,), sem=v_w)
-        if r == 0:
-            late[5]()
-        k_nb = scan(nc[:, H + C:H - 1:-1], m[:, H + C:H - 1:-1], T.c1[:, C::-1], 0.0, A.mult, A.max, deps=(k3,))
-        if r == 0:
-            late[6]()
-        k_na = scan(nc[:, C::-1], m[:, C::-1], T.c1[:, C::-1], 0.0, A.mult, A.max, deps=(v_f,))
-        k0 = valid(1, k_nb)
-        if r == 0:
-            kl.update(a=tt(tw[2], tw[15], tw[1], A.add, deps=(kl["a"], kl["b"]), sem=True))
-        copy_p(0)
-        k1 = valid(0, k_na)
-        keys(1, k0)
-        if r == 0:
-            v_lp = ts(T.lp[:], tw[2], 121.0, None, A.min, deps=(kl["a"],), sem=True)
-        ts(key[:, 128:186], z[:, 0:2 * H:16], -1.0, LOW + 8, A.mult, A.add, sem=v_d)
-        keys(0, k1)
-        copy_p(1)
-        k_e = [ts(ec[:, 64 * c:64 * c + 58], key[:, 57::-1], 16.0 * c + 8 - Z0, None, A.add, deps=(v_k,))
-               for c in range(6)]
-        for c in range(6):
-            scan(rm[:, 64 * c:64 * c + 58], ec[:, 64 * c:64 * c + 58], tb[:, 57::-1], 0.0, A.min, A.max,
-                 deps=(k_e[c], v_t), sem=v_rm)
-        tt(key[:, 64:121], key[:, 0:57], key[:, 1:58], A.subtract, sem=v_d)
-        k_ms = ms(m[:, 0:2 * H:16], 0.0, sem=True)
-        if r == 0:
-            ms(T.mask[:, 0:812:29], 0.0, deps=(g_z, g_e, s_ev, s_1), sem=v_m)
-        ts(R("ml")[:, 0:6], rm[:, 57:384:64], 2.0 ** 20, POFF - 1024.0, A.mult, A.add, deps=(v_rm,), sem=v_ml)
-        ts(R("ml")[:, 6:12], rm[:, 28:384:64], -2.0 ** 20, POFF + C - 1 + 1024.0, A.mult, A.add, sem=v_ml)
-        dg, ee, rr = R("dg"), R("ee"), R("rr")
-        v_dg, s_wn = [fresh(), fresh()], fresh()
-
-        def steps(a0, a1):
-            cp(dg[:, 16 * a0:16 * a1], td.indirect(T.lp[:, a0:a1]), deps=(v_d, v_lp), sem=v_dg[0])
-
-        steps(0, D1)
-        act(R("wn")[:], tb[:].indirect(T.lp[:, 0:51]), F.Identity, deps=(v_t, v_w, v_lp, v_c), sem=s_wn,
-            scale=2.0 ** 14, bias=colw)
-        s_m = fresh()
+            mm("sc%d#" % h, "uq2 us2 q%d#" % h, T.pss[:, 512 * h:512 * h + a1 - a0], T.uq2[:], T.us2[:],
+               aq[:, a0:a1], asc[:, a0:a1])
+            act("sg%d#" % h, "sc%d#" % h, sg[:, 2 * a0 + 1:2 * a1:2], T.pss[:, 512 * h:512 * h + a1 - a0], F.Sign,
+                bias=2.0 ** -110, accum_out=acc[:, h:h + 1])
         for b in range(4):
-            pick("V" if b < 2 else "S", R("mt")[:, b:8 * TM:4],
-                 win[:, WS * b:WS * (b + 1)].indirect(R("ml")[:, 0:12]), (v_ml, s_p[b], g_z), s_m)
-        steps(D1, 28)
-        if r == 0:
-            ms(T.mask[:, 28:812:28], 0.0, sem=v_m)
-        v_mq = quant(R("mq")[:], R("ms")[:], R("mt")[:], deps=(s_m,), sem=True)
-        wait("G", (v_mq,))
-        for kind in range(2):
-            trs = []
-            for other, s0, d0 in ((rank - 1, 0, TM), (rank + 1, TM, 0)):
-                if 0 <= other < n_ranks:
-                    did, mask, ne = link(rank, other)
-                    if kind == 0:
-                        src, dst = R("mq")[:, s0:s0 + TM].bitcast(dt.uint8), lqb[:, d0:d0 + TM].bitcast(dt.uint8)
-                    else:
-                        src, dst = R("ms")[:, s0:s0 + TM], lsb[:, d0:d0 + TM]
-                    trs.append(RemoteDMATransfer(dst_ids=[did], dma_engine_mask=mask, remote_sem=T.sem[arr],
-                                                 src=src, dst=dst))
-                    tot["loc"] += ne
-            g.remote_dma_fused(trs, local_sem=T.sem["loc"])
-        tot[arr] = sum(2 * link(o, rank)[2] for o in (rank - 1, rank + 1) if 0 <= o < n_ranks)
+            mm("p%d#" % b, "dw dws q0# q1#", T.psp[:, 512 * b:512 * b + C], T.wq[:, 128 * b:128 * b + 128],
+               T.wsc[:, 128 * b:128 * b + 128], aq[:], asc[:])
+            act("c%d#" % b, "p%d#" % b, own(b), T.psp[:, 512 * b:512 * b + C], F.Copy, scale=0.0625)
+        for b in (0, 2):
+            dma("pc%d#" % b, "Y", "c%d#" % b, T.pc[:, C * (b // 2):C * (b // 2 + 1)], own(b))
+        s0, s1, sr = sg[:, 1:2 * MID:2], sg[:, 2 * MID + 1:2 * C:2], sg[:, 2 * C - 1:0:-2]
+        scan("za#", "sg0# colz", z[:, 1:MID + 1], s0, s0, colz, A.add, A.max)
+        ts("k0#", "sg0# colz", acc[:, 5:6], acc[:, 0:1], colz, None, A.add)
+        scan("fa#", "za# gf1 gf2", nc[:, MID - 1::-1], fd[:, 463:143:-1], z[:, MID:0:-1], 0.0, A.add, A.min)
+        scan("da#", "za# z0", dz[:, 0:MID], z[:, 1:MID + 1], z[:, 0:MID], 0.0, A.max, A.subtract)
+        ts("ma#", "da#", m[:, 0:MID], dz[:, 0:MID], 1.0 / 16, 1.0, A.mult, A.add)
+        scan("zb#", "sg0# sg1# colz", z[:, H + 1:H + C + 1], sr, sr, colz, A.max, A.subtract)
+        scan("zc#", "sg1# k0#", z[:, MID + 1:C + 1], s1, s1, acc[:, 5:6], A.add, A.max)
+        scan("fx#", "zb# zc# z0 z1 z2 gf1 gf2", nc[:, H + C:MID - 1:-1], fd[:, 592::-1], z[:, H + C + 1:MID:-1], 0.0,
+             A.add, A.min)
+        scan("dx#", "za# zb# zc# z0 z1", dz[:, MID:H + C], z[:, MID + 1:H + C + 1], z[:, MID:H + C], 0.0, A.max,
+             A.subtract)
+        ts("mx#", "dx#", m[:, MID:H + C], dz[:, MID:H + C], 1.0 / 16, 1.0, A.mult, A.add)
+        iota("gz#", "ma# mx#", m[:, 0:2 * H:16], [[0, 58]], 0)
+        ts("ka#", "sg0# sg1# col0", acc[:, 3:4], acc[:, 0:1], acc[:, 1:2], col0, A.add, A.add)
+        ts("kb#", "sg0# sg1# col0", acc[:, 4:5], acc[:, 0:1], acc[:, 1:2], col0, A.add, A.subtract)
+        ts("ta#", "ka# za# zc# z0 kt", kt[:, 384:413], z[:, 0:C + 1:16], acc[:, 3:4], -1.0, A.subtract, A.mult)
+        ts("tb#", "kb# zb# z0 kt", kt[:, 413:442], z[:, H:H + C + 1:16], acc[:, 4:5], -1.0, A.add, A.mult)
+        ts("nz#", "za# zb# zc# z0 kt", kt[:, 128:186], z[:, 0:2 * H:16], -1.0, LOW + 8, A.mult, A.add)
+        scan("kp#", "fa# fx# gw1 kt", keyp, T.nw[:, 0:58], fv, 4096.0, A.min, A.add)
+        ts("key#", "fa# fx# kt", key, fv, -7.0, None, A.add)
+        ts("e0#", "fa# fx#", T.ec[:, 0:58], fv, 1 - Z0, 1024.0, A.add, A.mult)
+        ts("e1#", "fa# fx#", T.ec[:, 58:116], fv, 17 - Z0, 1024.0, A.add, A.mult)
+        scan("t1#", "kp#", tb, fv, keyp, 0.0, A.max, A.subtract)
+        scan("t2#", "kp#", kt[:, 262:320], fv, keyp, 0.0, A.max, A.subtract)
+        for i in (1, 2):
+            ts("e%d#" % (i + 1), "e0# e1#", T.ec[:, 116 * i:116 * i + 116], T.ec[:, 0:116], 32768.0 * i, None, A.add)
+        scan("df#", "key#", kt[:, 64:121], kt[:, 0:57], kt[:, 1:58], 0.0, A.max, A.subtract)
+        for i in range(3):
+            back = slice(116 * i + 115, 116 * i - 1 if i else None, -1)
+            scan("rm%d#" % i, "t1# t2# e0# e1#" + (" e%d#" % (i + 1) if i else ""), T.rm[:, back], T.ec[:, back],
+                 kt[:, 377:261:-1], 0.0, A.min, A.max)
+        ts("mla#", "rm0# rm1# rm2# colw", T.ml[:, 0:6], T.rm[:, 0:348:58], colw, POFF - 1024.0, A.add, A.add)
+        ts("mlb#", "rm0# rm1# rm2# cmb", T.ml[:, 6:12], T.rm[:, 29:348:58], -1.0, cmb, A.mult, A.add)
+        for b in range(4):
+            pick("mo%d#" % b, "mla# mlb# c%d# w%d w%d" % (b, b, b + 1), T.mt[:, b:8 * TM:4],
+                 plane(b).indirect(T.ml[:, 0:12]))
+        quant("mq#", "mo0# mo1# mo2# mo3#", mq[:], msc[:], T.mt[:])
 
-        act(dg[:, C:NP], td.indirect(T.lp[:, 28:51]), F.Copy, deps=(v_d,), sem=v_dg[1])
-        if r == 0:
-            s_mk = act(T.mk[:], T.pat[:], F.Abs, deps=(g_pat,), scale=CAP, bias=nhi)
-        k0 = scan(ee[:, 0:C], T.mask[:, 0:C], dg[:, 0:C], 0.0, A.mult, A.add, deps=(v_dg[0], v_m))
-        if r == 0:
-            ts(fb[:, C2:C2 + C + 1], fb[:, 0:C + 1], 2.0 ** -12, None, A.mult, sem=v_c2)
-        k1 = scan(ee[:, C:NP], T.mask[:, C:NP], dg[:, C:NP], 0.0, A.mult, A.add, deps=(v_dg[1],))
-        if r == 0:
-            ts(fb[:, C2 + H:C2 + H + C + 1], fb[:, 0:C + 1], 2.0 ** -14, None, A.mult, sem=v_c2)
-        k0 = scan(rr[:, 0:C], ee[:, 0:C], R("wn")[:, 0:C], 0.0, A.min, A.max, deps=(k0, s_wn))
-        k1 = scan(rr[:, C:NP], ee[:, C:NP], R("wn")[:, C:NP], 0.0, A.min, A.max, deps=(k1,))
-        v_fill = []
+        def send(kind, mq=mq, msc=msc, lqb=lqb, lsb=lsb, arr=arr):
+            trs = []
+            for other in others:
+                did, engines, _ = link(rank, other)
+                s0, d0 = (0, TM) if other < rank else (TM, 0)
+                if kind == 0:
+                    src, dst = mq[:, s0:s0 + TM].bitcast(dt.uint8), lqb[:, d0:d0 + TM].bitcast(dt.uint8)
+                else:
+                    src, dst = msc[:, s0:s0 + TM], lsb[:, d0:d0 + TM]
+                trs.append(RemoteDMATransfer(dst_ids=[did], dma_engine_mask=engines, remote_sem=T.sem[arr], src=src,
+                                             dst=dst))
+            return g.remote_dma_fused(trs, local_sem=T.sem["loc"])
+
+        op("sd0#", "G", lambda send=send: send(0), "mq#")
+        op("sd1#", "G", lambda send=send: send(1), "mq#")
+        for b in (1, 3):
+            op("ib%d#" % b, "G", lambda b=b: g.affine_select(T.ib[:, b - 1:4 * C:4], own(b), [[0, C]], A.is_ge, 0.0,
+                                                             0, 0), "c%d#" % b)
+        for i in range(4):
+            a0, a1 = PP[i:i + 2]
+            pick("dg%d#" % i, "df# nz# lp", T.dg[:, 16 * a0:16 * a1], td.indirect(T.lp[:, a0:a1]), 128.0)
+        for i in range(4):
+            a0, a1 = PP[i:i + 2]
+            pick("wn%d#" % i, "t1# ta# tb# lp", T.wn[:, 16 * a0:16 * a1], tbw.indirect(T.lp[:, a0:a1]))
+        for h, (a0, a1) in enumerate(((0, C), (C, NP))):
+            scan("ee%d#" % h, "dg%d# dg%d# gm0 gm1" % (2 * h, 2 * h + 1), T.ee[:, a0:a1], mask[:, a0:a1],
+                 T.dg[:, a0:a1], 0.0, A.mult, A.add)
+            scan("rr%d#" % h, "ee%d# wn%d# wn%d#" % (h, 2 * h, 2 * h + 1), T.rr[:, a0:a1], T.ee[:, a0:a1],
+                 T.wn[:, a0:a1], 0.0, A.min, A.max)
+        fill = ""
         if not (has_l and has_r):
-            f0 = 2 * TM if has_r else TM
-            v_fill = [quant(lqb[:, f0:f0 + 128], lsb[:, f0:f0 + 128], T.xt[:, 0:512], sem=True)]
-        if r > 0:
-            quant(T.vq[:], T.vs[:], T.vt[:], deps=(d_v,), sem=v_v)
-        else:
-            quant_e(0)
-            quant_e(1)
-        ab, trb, ss, ev = R("ab"), R("tr"), R("ss"), R("ev")
-        ca, cb = C2, C2 + H
-        k1 = ts(fb[:, ca + 16:ca + C + 1:16], rr[:, 27:784:28], colw, 1.0 / 64, A.subtract, A.mult,
-                deps=(k0, k1, v_c2))
-        k2 = ts(fb[:, cb + C:cb:-16], rr[:, 28:812:29], colw, 1.0 / 256, A.subtract, A.mult)
-        if r == 0:
-            quant_e(2)
-            quant_e(3)
-        v_ab = fresh()
-        scan(ab[:, 2 * C - 2::-2], m[:, C:0:-1], fb[:, ca + C:ca:-1], 0.0, A.mult, A.max, deps=(k1, k_ms), sem=v_ab)
-        scan(ab[:, 1:2 * C:2], m[:, H + C:H:-1], fb[:, cb + C:cb:-1], 0.0, A.mult, A.max, deps=(k2,), sem=v_ab)
-        copy_p(2)
+            f0, fill = 2 * TM if has_r else TM, " fl#"
+            quant("fl#", "dx0", lqb[:, f0:f0 + 128], lsb[:, f0:f0 + 128], T.xt[:, 0:512])
+        ab, trb, ss, ev = T.ab, T.tr, T.ss, T.ev
+        ts("ia#", "rr0# rr1# cb colw", fb[:, ca + 16:ca + C + 1:16], T.rr[:, 27:784:28], colw, None, A.add)
+        ts("ib#", "rr0# rr1# cb colw", fb[:, cb + C:cb:-16], T.rr[:, 28:812:29], colw, 0.25, A.add, A.mult)
+        scan("sa#", "ia# gz#", ab[:, 2 * C - 2::-2], m[:, C:0:-1], fb[:, ca + C:ca:-1], 0.0, A.mult, A.max)
+        scan("sb#", "ib# gz#", ab[:, 1:2 * C:2], m[:, H + C:H:-1], fb[:, cb + C:cb:-1], 0.0, A.mult, A.max)
         l0 = 0 if has_l else TM
         ln = 2 * TM if has_l and has_r else 128
-        prev_d = []
         for b in range(4):
-            t_d = mm(T.psp[:, 512 * b:512 * b + ln], T.eq[:, 128 * b:128 * b + 128], T.es[:, 128 * b:128 * b + 128],
-                     lqb[:, l0:l0 + ln], lsb[:, l0:l0 + ln], deps=[v_e, s_p[b], arr] + v_fill)
-            s_d = fresh()
+            mm("u%d#" % b, "e%d c%d# %s" % (b, b, arr) + fill, T.psp[:, 512 * b:512 * b + ln],
+               T.eq[:, 128 * b:128 * b + 128], T.es[:, 128 * b:128 * b + 128], lqb[:, l0:l0 + ln], lsb[:, l0:l0 + ln])
             if has_l:
-                act(win[:, WS * b + POFF - 1:WS * b + 1:-1], T.psp[:, 512 * b:512 * b + TM], F.Copy,
-                    deps=(t_d, s_m), sem=s_d)
+                pick("dl%d#" % b, "u%d# mo%d#" % (b, b), win[:, WS * b + POFF - 1:WS * b + 1:-1],
+                     T.psp[:, 512 * b:512 * b + TM])
             if has_r:
                 o = 512 * b + (TM if has_l else 0)
-                act(win[:, WS * b + POFF + C:WS * b + POFF + C + TM], T.psp[:, o:o + TM], F.Copy,
-                    deps=(t_d, s_m), sem=s_d)
-            prev_d.append(s_d)
-        xn, nq, ns = R("xn"), T["aq%d" % (r + 1)], T["as%d" % (r + 1)]
-        v_g, k_el = [fresh(), fresh()], [fresh(), fresh()]
-        part = ((0, 8), (8, 28))
-
-        def least(a0, a1, d, sem=None):
-            return scan(ss[:, a0:a1], trb[:, a0:a1], T.mk[:, a0:a1], CAP, A.min, A.max, deps=(d, s_mk), sem=sem)
-
-        def decode(h, i, d):
-            a0, a1 = part[h]
-            if i == 0:
-                return tt(ev[:, a0:a1], ss[:, 15 + 16 * a0:16 * a1:16], ss[:, 479 + 16 * a0:464 + 16 * a1:16], A.min,
-                          deps=d)
-            if i == 1:
-                return ts(ev[:, 32 + a0:32 + a1], ev[:, a0:a1], -4.0, (2048.0 + C - 1) / 4096, A.mult, A.add, deps=d)
-            if i == 2:
-                return tt(ev[:, 64 + a0:64 + a1], ev[:, a0:a1], ev[:, 32 + a0:32 + a1], A.max, deps=d)
-            return ts(R("el")[:, a0:a1], ev[:, 64 + a0:64 + a1], 4096.0, POFF - 1024.0, A.mult, A.add, deps=d,
-                      sem=k_el[h])
-
-        def gather(a0, a1, b):
-            tt(xn[:, 4 * a0 + b:4 * a1:4], win[:, WS * b:WS * (b + 1)].indirect(R("el")[:, a0 // 16:a1 // 16]),
-               R("pc")[:, C * b + a0:C * b + a1], A.add, deps=(k_el[min(a0, 1)], prev_d[b], d_p), sem=v_g[a0 // MID])
-
-        def requant(h):
+                pick("dr%d#" % b, "u%d# mo%d#" % (b, b) + (" dl%d#" % b if has_l else ""),
+                     win[:, WS * b + POFF + C:WS * b + POFF + C + TM], T.psp[:, o:o + TM])
+        dd = [(" dl%d#" % b if has_l else "") + (" dr%d#" % b if has_r else "") for b in range(4)]
+        scan("va#", "sa# sb# sev", fb[:, SEL:SEL + 288], sg[:, 0:288], ab[:, 0:288], 0.0, A.mult, A.max)
+        scan("vb#", "sa# sb# sev", fb[:, SEL + 288:C2], sg[:, 288:2 * C], ab[:, 288:2 * C], 0.0, A.mult, A.max)
+        tr("r0#", "va# fil", trb[:, C:608], fb[:, SEL - 31:SEL + 288:2])
+        tr("r1#", "va#", trb[:, 0:128], fb[:, SEL + 1:SEL + 256:2])
+        tr("r2#", "vb# ca", trb[:, 608:928], fb[:, SEL + 289:C2 + 32:2])
+        tr("r3#", "va# vb#", trb[:, 128:C], fb[:, SEL + 257:C2:2])
+        for i, (a0, a1) in enumerate(((C, 608), (0, 128), (608, 928), (128, C))):
+            scan("n%d#" % i, "r%d# mk" % i, ss[:, a0:a1], trb[:, a0:a1], T.mk[:, a0:a1], CAP, A.min, A.max)
+        for h, (a0, a1) in enumerate(((0, 8), (8, 28))):
+            tt("o0%d#" % h, "n0# n1#" + (" n2# n3#" if h else ""), ev[:, a0:a1], ss[:, 15 + 16 * a0:16 * a1:16],
+               ss[:, 479 + 16 * a0:464 + 16 * a1:16], A.min)
+            ts("o1%d#" % h, "o0%d#" % h, ev[:, 32 + a0:32 + a1], ev[:, a0:a1], -4.0, 2048.0 + C - 1, A.mult, A.add)
+            tt("o2%d#" % h, "o1%d#" % h, ev[:, 64 + a0:64 + a1], ev[:, a0:a1], ev[:, 32 + a0:32 + a1], A.max)
+            ts("el%d#" % h, "o2%d#" % h, T.el[:, a0:a1], ev[:, 64 + a0:64 + a1], POFF - 1024.0, None, A.add)
+        for i in range(3):
+            a0, a1 = GP[i:i + 2]
+            el, lst = "el%d#" % min(i, 1), T.el[:, a0 // 16:a1 // 16]
+            if i > 0:
+                for b in (1, 3):
+                    act("h%d%d#" % (i, b), el + dd[b], T.ib[:, 4 * a0 + b:4 * a1:4], plane(b).indirect(lst), F.Copy)
+                scan("ad%d#" % i, "h%d1# h%d3# ib1# ib3# m0 m1" % (i, i), T.xn[:, 4 * a0:4 * a1],
+                     T.m01[:, 0:4 * (a1 - a0)], T.ib[:, 4 * a0:4 * a1], 0.0, A.mult, A.add)
+            for b in (0, 2) if i > 0 else range(4):
+                o = C * (b // 2)
+                p = T.ib[:, 4 * a0 + b - 1:4 * a1:4] if b % 2 else T.pc[:, o + a0:o + a1]
+                tt("x%d%d#" % (i, b), "%s %s%d#" % (el, "ib" if b % 2 else "pc", b) + dd[b]
+                   + (" ad%d#" % i if i > 0 else ""), T.xn[:, 4 * a0 + b:4 * a1:4], plane(b).indirect(lst), p, A.add)
+        for h in range(2):
             a0, a1 = CUT[h:h + 2]
-            return quant(nq[:, a0:a1], ns[:, a0:a1], xn[:, 4 * a0:4 * a1], deps=(v_g[h],), sem=True)
+            quant("q%d$" % h, "x20# x22#" if h else "x00# x01# x02# x03# x10# x12#", nq[:, a0:a1], ns[:, a0:a1],
+                  T.xn[:, 4 * a0:4 * a1])
 
-        va = scan(fb[:, SEL:SEL + 288], T.sg[:, 0:288], ab[:, 0:288], 0.0, A.min, A.max, deps=(v_ab, s_ev, s_a0, s_a1))
-        vb = scan(fb[:, SEL + 288:C2], T.sg[:, 288:2 * C], ab[:, 288:2 * C], 0.0, A.min, A.max)
-        k0 = tr(trb[:, C:608], fb[:, SEL - 31:SEL + 288:2], deps=(va,))
-        k1 = tr(trb[:, 0:128], fb[:, SEL + 1:SEL + 256:2])
-        k2 = tr(trb[:, 608:928], fb[:, SEL + 289:C2 + 32:2], deps=(vb,), sem=True)
-        k0 = least(C, 608, k0)
-        k1 = least(0, 128, k1)
-        k3 = tr(trb[:, 128:C], fb[:, SEL + 257:C2:2], sem=True)
-        k0 = decode(0, 0, (k0, k1))
-        k2 = least(608, 928, k2, True)
-        k0 = decode(0, 1, (k0,))
-        k3 = least(128, C, k3, True)
-        k0 = decode(0, 2, (k0,))
-        copy_p(3)
-        decode(0, 3, (k0,))
-        k1 = decode(1, 0, (k2, k3))
-        for b in range(4):
-            gather(0, 128, b)
-            if b < 3:
-                k1 = decode(1, b + 1, (k1,))
-        for b in range(4):
-            gather(128, MID, b)
-        gather(MID, C, 0)
-        v_a = [requant(0)]
-        if r + 1 < ROUNDS:
-            t = scores(r + 1, 0, v_a[0])
-        else:
-            t = mm(T.pss[:, 0:MID], T.vq[:], T.vs[:], nq[:, 0:MID], ns[:, 0:MID], deps=(v_v, v_a[0]))
-        for b in range(1, 4):
-            gather(MID, C, b)
-        if r + 1 < ROUNDS:
-            v_s0 = signs(0, t)
-        else:
-            v_y = cp(T.ysb[:, 0:MID], T.pss[:, 0:MID], deps=(t,), sem=True)
-        v_a.append(requant(1))
-
+    rnd[0] = ROUNDS
     fq, fs = T["aq%d" % ROUNDS], T["as%d" % ROUNDS]
-    t = mm(T.pss[:, 512:512 + C - MID], T.vq[:], T.vs[:], fq[:, MID:C], fs[:, MID:C], deps=(v_a[1],))
-    dma("Y", T.oc[:, 0:4 * MID], fq[:, 0:MID].bitcast(dt.uint8), deps=(v_a[0],), sem="st")
-    dma("Y", T.y[:, 0:MID], T.ysb[:, 0:MID], deps=(v_y,), sem="st")
-    dma("Y", T.oc[:, 4 * MID:4 * C], fq[:, MID:C].bitcast(dt.uint8), deps=(v_a[1],), sem="st")
-    for k in range(3):
-        dma("Y", T.osc[4 * k:4 * k + 4, :], fs[32 * k:32 * k + 4, :], sem="st")
-    s_y = act(T.ysb[:, MID:C], T.pss[:, 512:512 + C - MID], F.Copy, deps=(t,))
-    dma("S", T.osc[12:16, :], fs[96:100, :], sem="st")
-    dma("S", T.y[:, MID:C], T.ysb[:, MID:C], deps=(s_y,), sem="st")
-    wait("G", [s for s in tot if top.get(s, 0) < tot[s]])
+    for h in range(2):
+        a0, a1 = CUT[h:h + 2]
+        mm("y%d" % h, "vq q%d#" % h, T.pss[:, 512 * h:512 * h + a1 - a0], T.vq[:], T.vs[:], fq[:, a0:a1], fs[:, a0:a1])
+        pick("yc%d" % h, "y%d" % h, T.ysb[:, a0:a1], T.pss[:, 512 * h:512 * h + a1 - a0])
+        dma("so%d" % h, "Y", "q%d#" % h, T.oc[:, 4 * a0:4 * a1], fq[:, a0:a1].bitcast(dt.uint8), "st")
+        dma("sy%d" % h, "S" if h else "Y", "yc%d" % h, T.y[:, a0:a1], T.ysb[:, a0:a1], "st")
+    for k in range(4):
+        dma("ss%d" % k, "S" if k == 3 else "Y", "q0# q1#", T.osc[4 * k:4 * k + 4, :], fs[32 * k:32 * k + 4, :], "st")
+    fixed["st"] = ("st", 16 * 8)
+    op("end", "G", None, "st loc")
+    emit(g, T, ops, fixed)

@@ -4,7 +4,7 @@ from concourse.mybir import dt, AluOpType, ActivationFunctionType
 A = AluOpType
 F = ActivationFunctionType
 C, TM, ROUNDS = 448, 96, 2
-MID = 320
+MID = 256
 H = 464
 Z0 = 3072.0
 LOW = Z0 - 480
@@ -12,10 +12,12 @@ CAP = 1024.0 + C + TM
 POFF = 2 + TM
 WS = 656
 NP = 816
+W1 = MID // 16 + 1
 SEL, C2 = 32, 32 + 2 * C
+FD = C - MID + H + 16
 CUT = (0, MID, C)
 GP = (0, 128, MID, C)
-PP = (0, 14, 28, 40, 51)
+PP = (0, 16, 32, 42, 51)
 Q4, U8, BF, F16, F32, I32, U16 = "float8_e4m3fn_x4", "uint8", "bfloat16", "float16", "float32", "int32", "uint16"
 SCRATCH = {}
 for _n, _w, _d in [
@@ -24,7 +26,7 @@ for _n, _w, _d in [
     ("eq", 512, Q4), ("es", 512, U8), ("pi", 8, I32), ("pj", 8, I32), ("cl", 8, F32), ("nf", 52, F32),
     ("lui", 8, I32), ("lu", 8, U16), ("lp", 52, U16), ("tw", 17 * 52, F32), ("wi", 52, I32),
     ("fb", C2 + 2 * H, F16), ("pat", 928, BF), ("mk", 928, BF), ("mask", NP, BF), ("sg", 2 * C, BF),
-    ("ysb", C, F32), ("z", 2 * H, BF), ("kt", 448, BF), ("nw", 64, BF), ("fd", 608, BF), ("nc", 2 * H, F16),
+    ("ysb", C, F32), ("z", 2 * H, BF), ("kt", 448, BF), ("nw", 64, BF), ("fd", FD, BF), ("nc", 2 * H, F16),
     ("m", 2 * H, BF), ("win", 4 * WS, BF), ("m01", 768, BF), ("dz", 2 * H, BF), ("acc", 8, F32), ("ec", 348, BF),
     ("rm", 348, BF), ("ml", 12, U16), ("mt", 8 * TM, BF), ("dg", NP, BF), ("ee", NP, BF), ("wn", NP, BF),
     ("rr", NP, BF), ("ab", 2 * C, F16), ("tr", 928, F16), ("ss", 928, F16), ("ev", 96, F32), ("el", 28, U16),
@@ -38,24 +40,25 @@ SCRATCH["psp"] = ("psum", [128, 2048], F32)
 NSEM = 140
 SEMAPHORES = ["arr0", "arr1", "loc", "st"] + ["k%d" % _i for _i in range(NSEM)]
 
-ON_V = "dg0 dl3 dr0 dr1 mo0 mo1 wn2 yc1"
+ON_V = "dg0 mo0 mo1 yc1"
 ORDER = {
-    "V": "one res kt par hi colz ca z1 l0 colw lu l1 cb lq uq cmb nhi l9 l2 uq2 us2 l6 col0 l3 z2 q0_0 l4 l7 l11 fil l5 "
-         "l8 q1_0 e3 e1 l13 l10 l12 za_0 z0 k0_0 zb_0 l14 zc_0 kb_0 fa_0 fx_0 ka_0 l15 e0_0 kp_0 e1_0 l16 nz_0 ta_0 "
-         "t2_0 key_0 l17 e2_0 t1_0 e3_0 tb_0 df_0 lp rm1_0 rm0_0 rm2_0 da_0 mlb_0 mla_0 ma_0 mo0_0 mo1_0 e0 mq_0 dg0_0 "
-         "wn2_0 dx_0 ee0_0 mx_0 ee1_0 rr0_0 rr1_0 e2 fl_0 ib_0 ia_0 sb_0 sa_0 vq vb_0 va_0 r2_0 r3_0 r1_0 r0_0 n3_0 "
-         "n1_0 n0_0 n2_0 o00_0 dl3_0 o01_0 o10_0 o11_0 o20_0 dr1_0 o21_0 el0_0 el1_0 dr0_0 x03_0 x01_0 x02_0 x00_0 "
-         "ad1_0 ad2_0 x12_0 x10_0 x22_0 q0_1 x20_0 q1_1 fl_1 za_1 k0_1 da_1 zb_1 zc_1 fa_1 fx_1 kb_1 ka_1 kp_1 key_1 "
-         "e1_1 e0_1 tb_1 dx_1 nz_1 df_1 e2_1 ta_1 t1_1 e3_1 t2_1 ma_1 rm2_1 rm1_1 rm0_1 wn2_1 mlb_1 mla_1 mx_1 mo0_1 "
-         "mo1_1 dg0_1 mq_1 ee0_1 ee1_1 rr0_1 rr1_1 ib_1 ia_1 sb_1 sa_1 vb_1 va_1 r2_1 r0_1 r1_1 r3_1 n2_1 n1_1 n0_1 "
-         "n3_1 o00_1 dl3_1 o01_1 o10_1 dr0_1 o11_1 o20_1 o21_1 el0_1 dr1_1 el1_1 x00_1 x03_1 x01_1 x02_1 ad1_1 x12_1 "
-         "x10_1 ad2_1 q0_2 x20_1 x22_1 q1_2 yc0 yc1",
-    "S": "du w2 m0 w0 w1 m1 w4 sev w3 sg0_0 sg1_0 c1_0 c0_0 c3_0 c2_0 mo3_0 mo2_0 dg1_0 dg3_0 wn0_0 dg2_0 wn1_0 wn3_0 "
-         "mk dl1_0 dl0_0 dl2_0 dr3_0 dr2_0 h13_0 h11_0 h21_0 h23_0 sg0_1 sg1_1 c3_1 c1_1 c2_1 c0_1 dg3_1 dg2_1 dg1_1 "
-         "mo2_1 mo3_1 wn0_1 wn1_1 wn3_1 dl0_1 dl2_1 dl1_1 dr3_1 dr2_1 h11_1 h13_1 h21_1 h23_1 yc0 sy1 ss3",
-    "T": "sc0_0 sc1_0 p1_0 p0_0 p3_0 p2_0 u1_0 u0_0 u3_0 u2_0 sc0_1 sc1_1 p3_1 p1_1 p2_1 p0_1 u0_1 u3_1 u2_1 u1_1 y0 y1",
-    "G": "gp gn glu gf0 gw0 gf2 ge gm1 gf1 gw1 gm0 gpat sd0_0 sd1_0 gz_0 ib1_0 ib3_0 ib3_1 gz_1 sd0_1 sd1_1 ib1_1 end",
-    "Y": "dx0 dx1 dw dws dv pc0_0 pc2_0 pc2_1 pc0_1 so0 so1 ss1 sy0 ss0 ss2",
+    "V": "one res kt colz ca l0 par hi fil z0 l1 z2 z1 nhi colw lq lu cb l2 l11 l9 uq l6 l3 us2 uq2 l4 q0_0 l5 l8 l10 "
+         "q1_0 l12 l7 col0 l13 l14 e1 e3 k0_0 za_0 zb_0 zc_0 kb_0 fa_0 fx_0 l15 l16 kp_0 e1_0 e0_0 cmb t1_0 t2_0 e2_0 "
+         "e3_0 ka_0 rm0_0 rm1_0 rm2_0 key_0 nz_0 l17 mla_0 mlb_0 ta_0 lp tb_0 mo1_0 mo0_0 df_0 da_0 mq_0 dg0_0 dx_0 "
+         "ma_0 ee0_0 mx_0 rr0_0 gz_0 ee1_0 fl_0 ia0_0 ic0_0 e0 sa0_0 sb0_0 rr1_0 va_0 ia1_0 ic1_0 r0_0 r1_0 sb1_0 "
+         "sa1_0 n0_0 n1_0 vb_0 e2 o00_0 r2_0 r3_0 o10_0 n2_0 n3_0 o20_0 o01_0 el0_0 o11_0 x00_0 o21_0 x01_0 el1_0 "
+         "x02_0 ad1_0 x03_0 x10_0 x12_0 ad2_0 q0_1 x22_0 x20_0 q1_1 za_1 vq fa_1 fl_1 k0_1 zb_1 zc_1 ka_1 kb_1 fx_1 "
+         "nz_1 ta_1 kp_1 e0_1 e1_1 t2_1 t1_1 e2_1 e3_1 rm0_1 rm1_1 rm2_1 da_1 mla_1 mlb_1 key_1 tb_1 mo1_1 mo0_1 ma_1 "
+         "df_1 mq_1 dg0_1 dx_1 ee0_1 mx_1 rr0_1 gz_1 ia0_1 ic0_1 ee1_1 sa0_1 sb0_1 rr1_1 va_1 ic1_1 ia1_1 r0_1 r1_1 "
+         "sb1_1 sa1_1 n0_1 n1_1 vb_1 o00_1 r2_1 r3_1 o10_1 n2_1 n3_1 o20_1 o01_1 el0_1 o11_1 x03_1 o21_1 x02_1 el1_1 "
+         "x01_1 ad1_1 x00_1 x12_1 x10_1 ad2_1 q0_2 x20_1 x22_1 q1_2 yc1",
+    "S": "du w1 w3 w4 sev m1 w0 m0 w2 sg0_0 sg1_0 c1_0 c0_0 c3_0 c2_0 mo3_0 mo2_0 wn1_0 dg1_0 dg3_0 wn0_0 dg2_0 wn3_0 "
+         "wn2_0 mk dr1_0 dr0_0 dl3_0 dl0_0 dl1_0 dr3_0 dl2_0 dr2_0 h13_0 h11_0 h21_0 h23_0 sg0_1 sg1_1 c3_1 c1_1 c2_1 "
+         "c0_1 mo3_1 mo2_1 wn1_1 dg1_1 wn0_1 dg3_1 dg2_1 wn2_1 wn3_1 dl3_1 dr3_1 dr1_1 dl1_1 dl2_1 dr2_1 dr0_1 h11_1 "
+         "h13_1 dl0_1 h21_1 h23_1 yc0 sy1 ss3 ss2",
+    "T": "sc0_0 sc1_0 p1_0 p0_0 p3_0 p2_0 u1_0 u0_0 u3_0 u2_0 sc0_1 sc1_1 p3_1 p1_1 p2_1 p0_1 u3_1 u1_1 u2_1 u0_1 y0 y1",
+    "G": "gp gn glu ge gf0 gw0 gm1 gf2 gf1 gm0 gw1 gpat sd0_0 sd1_0 ib3_0 ib1_0 ib1_1 sd0_1 sd1_1 ib3_1 end",
+    "Y": "dx0 dx1 dw0 dws dw1 pc2_0 pc0_0 dv pc0_1 pc2_1 so0 sy0 so1 ss0 ss1",
 }
 
 
@@ -164,16 +167,16 @@ def rank_program(g, core, T, topo):
     dma("du", "S", "", T.ut[:], T.u[:])
     for h in range(2):
         dma("dx%d" % h, "Y", "", T.xt[:, 4 * CUT[h]:4 * CUT[h + 1]], T.x[:, 4 * CUT[h]:4 * CUT[h + 1]])
-    dma("dw", "Y", "", T.wq[:].bitcast(dt.uint8), T.wc[:])
+        dma("dw%d" % h, "Y", "", T.wq[:, 256 * h:256 * h + 256].bitcast(dt.uint8), T.wc[:, 1024 * h:1024 * h + 1024])
     dma("dws", "Y", "", T.wsc[:], T.ws[:])
-    dma("dv", "Y", "dw", T.vt[:], T.v[:])
+    dma("dv", "Y", "dw1", T.vt[:], T.v[:])
 
     iota("gp", "", T.pi[:, 0:1], [[0, 1]], 0, 1, small=False)
     iota("glu", "", T.lui[:], [[16, 8]], 0, small=False)
     iota("gn", "", T.nf[:], [[16, 52]], 0)
-    iota("gf0", "", fd[:], [[0, 304], [2, 2]], 0)
-    iota("gf1", "gf0", fd[:, 15:608:16], [[0, 38]], 4096)
-    iota("gf2", "gf0", fd[:, C - MID:608:H], [[0, 2]], 4096)
+    iota("gf0", "", fd[:], [[0, FD // 2], [2, 2]], 0)
+    iota("gf1", "gf0", fd[:, 15:FD:16], [[0, FD // 16]], 4096)
+    iota("gf2", "gf0", fd[:, C - MID:FD:H], [[0, 2]], 4096)
     iota("gw0", "", T.nw[:, 0:58], [[0, 2], [-16, 29]], 249)
     iota("gw1", "gw0", T.nw[:, 28:58:29], [[0, 2]], 256 - C - TM)
     ms("one", "", mask[:], 1.0)
@@ -268,25 +271,25 @@ def rank_program(g, core, T, topo):
             act("sg%d#" % h, "sc%d#" % h, sg[:, 2 * a0 + 1:2 * a1:2], T.pss[:, 512 * h:512 * h + a1 - a0], F.Sign,
                 bias=2.0 ** -110, accum_out=acc[:, h:h + 1])
         for b in range(4):
-            mm("p%d#" % b, "dw dws q0# q1#", T.psp[:, 512 * b:512 * b + C], T.wq[:, 128 * b:128 * b + 128],
-               T.wsc[:, 128 * b:128 * b + 128], aq[:], asc[:])
+            mm("p%d#" % b, "dw%d dws q0# q1#" % (b // 2), T.psp[:, 512 * b:512 * b + C],
+               T.wq[:, 128 * b:128 * b + 128], T.wsc[:, 128 * b:128 * b + 128], aq[:], asc[:])
             act("c%d#" % b, "p%d#" % b, own(b), T.psp[:, 512 * b:512 * b + C], F.Copy, scale=0.0625)
         for b in (0, 2):
             dma("pc%d#" % b, "Y", "c%d#" % b, T.pc[:, C * (b // 2):C * (b // 2 + 1)], own(b))
         s0, s1, sr = sg[:, 1:2 * MID:2], sg[:, 2 * MID + 1:2 * C:2], sg[:, 2 * C - 1:0:-2]
         scan("za#", "sg0# colz", z[:, 1:MID + 1], s0, s0, colz, A.add, A.max)
         ts("k0#", "sg0# colz", acc[:, 5:6], acc[:, 0:1], colz, None, A.add)
-        scan("fa#", "za# gf1 gf2", nc[:, MID - 1::-1], fd[:, 463:143:-1], z[:, MID:0:-1], 0.0, A.add, A.min)
+        scan("fa#", "za# gf1 gf2", nc[:, MID - 1::-1], fd[:, 511:511 - MID:-1], z[:, MID:0:-1], 0.0, A.add, A.min)
         scan("da#", "za# z0", dz[:, 0:MID], z[:, 1:MID + 1], z[:, 0:MID], 0.0, A.max, A.subtract)
         ts("ma#", "da#", m[:, 0:MID], dz[:, 0:MID], 1.0 / 16, 1.0, A.mult, A.add)
         scan("zb#", "sg0# sg1# colz", z[:, H + 1:H + C + 1], sr, sr, colz, A.max, A.subtract)
         scan("zc#", "sg1# k0#", z[:, MID + 1:C + 1], s1, s1, acc[:, 5:6], A.add, A.max)
-        scan("fx#", "zb# zc# z0 z1 z2 gf1 gf2", nc[:, H + C:MID - 1:-1], fd[:, 592::-1], z[:, H + C + 1:MID:-1], 0.0,
-             A.add, A.min)
+        scan("fx#", "zb# zc# z0 z1 z2 gf1 gf2", nc[:, H + C:MID - 1:-1], fd[:, C - MID + H::-1],
+             z[:, H + C + 1:MID:-1], 0.0, A.add, A.min)
         scan("dx#", "za# zb# zc# z0 z1", dz[:, MID:H + C], z[:, MID + 1:H + C + 1], z[:, MID:H + C], 0.0, A.max,
              A.subtract)
         ts("mx#", "dx#", m[:, MID:H + C], dz[:, MID:H + C], 1.0 / 16, 1.0, A.mult, A.add)
-        iota("gz#", "ma# mx#", m[:, 0:2 * H:16], [[0, 58]], 0)
+        ms("gz#", "ma# mx#", m[:, 0:2 * H:16], 0.0)
         ts("ka#", "sg0# sg1# col0", acc[:, 3:4], acc[:, 0:1], acc[:, 1:2], col0, A.add, A.add)
         ts("kb#", "sg0# sg1# col0", acc[:, 4:5], acc[:, 0:1], acc[:, 1:2], col0, A.add, A.subtract)
         ts("ta#", "ka# za# zc# z0 kt", kt[:, 384:413], z[:, 0:C + 1:16], acc[:, 3:4], -1.0, A.subtract, A.mult)
@@ -336,42 +339,49 @@ def rank_program(g, core, T, topo):
         for i in range(4):
             a0, a1 = PP[i:i + 2]
             pick("wn%d#" % i, "t1# ta# tb# lp", T.wn[:, 16 * a0:16 * a1], tbw.indirect(T.lp[:, a0:a1]))
-        for h, (a0, a1) in enumerate(((0, C), (C, NP))):
-            scan("ee%d#" % h, "dg%d# dg%d# gm0 gm1" % (2 * h, 2 * h + 1), T.ee[:, a0:a1], mask[:, a0:a1],
+        for h, (a0, a1) in enumerate(((0, 29 * W1), (29 * W1, NP))):
+            scan("ee%d#" % h, "dg0# dg1# gm0 gm1" + (" dg2# dg3#" if h else ""), T.ee[:, a0:a1], mask[:, a0:a1],
                  T.dg[:, a0:a1], 0.0, A.mult, A.add)
-            scan("rr%d#" % h, "ee%d# wn%d# wn%d#" % (h, 2 * h, 2 * h + 1), T.rr[:, a0:a1], T.ee[:, a0:a1],
+            scan("rr%d#" % h, "ee%d# wn0# wn1#" % h + (" wn2# wn3#" if h else ""), T.rr[:, a0:a1], T.ee[:, a0:a1],
                  T.wn[:, a0:a1], 0.0, A.min, A.max)
         fill = ""
         if not (has_l and has_r):
             f0, fill = 2 * TM if has_r else TM, " fl#"
             quant("fl#", "dx0", lqb[:, f0:f0 + 128], lsb[:, f0:f0 + 128], T.xt[:, 0:512])
         ab, trb, ss, ev = T.ab, T.tr, T.ss, T.ev
-        ts("ia#", "rr0# rr1# cb colw", fb[:, ca + 16:ca + C + 1:16], T.rr[:, 27:784:28], colw, None, A.add)
-        ts("ib#", "rr0# rr1# cb colw", fb[:, cb + C:cb:-16], T.rr[:, 28:812:29], colw, 0.25, A.add, A.mult)
-        scan("sa#", "ia# gz#", ab[:, 2 * C - 2::-2], m[:, C:0:-1], fb[:, ca + C:ca:-1], 0.0, A.mult, A.max)
-        scan("sb#", "ib# gz#", ab[:, 1:2 * C:2], m[:, H + C:H:-1], fb[:, cb + C:cb:-1], 0.0, A.mult, A.max)
+        for h, (w0, w1) in enumerate(((0, W1), (W1, 28))):
+            a0, a1 = 16 * w0, 16 * w1
+            ts("ia%d#" % h, "rr%d# cb colw" % h, fb[:, ca + a0 + 16:ca + a1 + 1:16], T.rr[:, 27 + 28 * w0:28 * w1:28],
+               colw, None, A.add)
+            ts("ic%d#" % h, "rr%d# cb colw" % h, fb[:, cb + C - a0:cb + C - a1:-16], T.rr[:, 28 + 29 * w0:29 * w1:29],
+               colw, 0.25, A.add, A.mult)
+            scan("sa%d#" % h, "ia%d# gz#" % h, ab[:, 2 * a1 - 2:(2 * a0 - 2 if h else None):-2], m[:, a1:a0:-1],
+                 fb[:, ca + a1:ca + a0:-1], 0.0, A.mult, A.max)
+            scan("sb%d#" % h, "ic%d# gz#" % h, ab[:, 2 * a0 + 1:2 * a1:2], m[:, H + C - a0:H + C - a1:-1],
+                 fb[:, cb + C - a0:cb + C - a1:-1], 0.0, A.mult, A.max)
         l0 = 0 if has_l else TM
         ln = 2 * TM if has_l and has_r else 128
         for b in range(4):
             mm("u%d#" % b, "e%d c%d# %s" % (b, b, arr) + fill, T.psp[:, 512 * b:512 * b + ln],
                T.eq[:, 128 * b:128 * b + 128], T.es[:, 128 * b:128 * b + 128], lqb[:, l0:l0 + ln], lsb[:, l0:l0 + ln])
             if has_l:
-                pick("dl%d#" % b, "u%d# mo%d#" % (b, b), win[:, WS * b + POFF - 1:WS * b + 1:-1],
-                     T.psp[:, 512 * b:512 * b + TM])
+                act("dl%d#" % b, "u%d# mo%d#" % (b, b), win[:, WS * b + POFF - 1:WS * b + 1:-1],
+                    T.psp[:, 512 * b:512 * b + TM], F.Copy)
             if has_r:
                 o = 512 * b + (TM if has_l else 0)
-                pick("dr%d#" % b, "u%d# mo%d#" % (b, b) + (" dl%d#" % b if has_l else ""),
-                     win[:, WS * b + POFF + C:WS * b + POFF + C + TM], T.psp[:, o:o + TM])
+                act("dr%d#" % b, "u%d# mo%d#" % (b, b), win[:, WS * b + POFF + C:WS * b + POFF + C + TM],
+                    T.psp[:, o:o + TM], F.Copy)
         dd = [(" dl%d#" % b if has_l else "") + (" dr%d#" % b if has_r else "") for b in range(4)]
-        scan("va#", "sa# sb# sev", fb[:, SEL:SEL + 288], sg[:, 0:288], ab[:, 0:288], 0.0, A.mult, A.max)
-        scan("vb#", "sa# sb# sev", fb[:, SEL + 288:C2], sg[:, 288:2 * C], ab[:, 288:2 * C], 0.0, A.mult, A.max)
-        tr("r0#", "va# fil", trb[:, C:608], fb[:, SEL - 31:SEL + 288:2])
-        tr("r1#", "va#", trb[:, 0:128], fb[:, SEL + 1:SEL + 256:2])
-        tr("r2#", "vb# ca", trb[:, 608:928], fb[:, SEL + 289:C2 + 32:2])
-        tr("r3#", "va# vb#", trb[:, 128:C], fb[:, SEL + 257:C2:2])
-        for i, (a0, a1) in enumerate(((C, 608), (0, 128), (608, 928), (128, C))):
+        v, t = 32 * W1, C + MID + 32
+        scan("va#", "sa0# sb0# sev", fb[:, SEL:SEL + v], sg[:, 0:v], ab[:, 0:v], 0.0, A.mult, A.max)
+        scan("vb#", "sa1# sb1# sev", fb[:, SEL + v:C2], sg[:, v:2 * C], ab[:, v:2 * C], 0.0, A.mult, A.max)
+        tr("r0#", "va# fil", trb[:, C:t], fb[:, SEL - 31:SEL + v:2])
+        tr("r1#", "va#", trb[:, 0:MID], fb[:, SEL + 1:SEL + 2 * MID:2])
+        tr("r2#", "vb# ca", trb[:, t:928], fb[:, SEL + v + 1:C2 + 32:2])
+        tr("r3#", "va# vb#", trb[:, MID:C], fb[:, SEL + 2 * MID + 1:C2:2])
+        for i, (a0, a1) in enumerate(((C, t), (0, MID), (t, 928), (MID, C))):
             scan("n%d#" % i, "r%d# mk" % i, ss[:, a0:a1], trb[:, a0:a1], T.mk[:, a0:a1], CAP, A.min, A.max)
-        for h, (a0, a1) in enumerate(((0, 8), (8, 28))):
+        for h, (a0, a1) in enumerate(((0, MID // 16), (MID // 16, 28))):
             tt("o0%d#" % h, "n0# n1#" + (" n2# n3#" if h else ""), ev[:, a0:a1], ss[:, 15 + 16 * a0:16 * a1:16],
                ss[:, 479 + 16 * a0:464 + 16 * a1:16], A.min)
             ts("o1%d#" % h, "o0%d#" % h, ev[:, 32 + a0:32 + a1], ev[:, a0:a1], -4.0, 2048.0 + C - 1, A.mult, A.add)
@@ -379,7 +389,7 @@ def rank_program(g, core, T, topo):
             ts("el%d#" % h, "o2%d#" % h, T.el[:, a0:a1], ev[:, 64 + a0:64 + a1], POFF - 1024.0, None, A.add)
         for i in range(3):
             a0, a1 = GP[i:i + 2]
-            el, lst = "el%d#" % min(i, 1), T.el[:, a0 // 16:a1 // 16]
+            el, lst = "el%d#" % (i // 2), T.el[:, a0 // 16:a1 // 16]
             if i > 0:
                 for b in (1, 3):
                     act("h%d%d#" % (i, b), el + dd[b], T.ib[:, 4 * a0 + b:4 * a1:4], plane(b).indirect(lst), F.Copy)
@@ -404,7 +414,7 @@ def rank_program(g, core, T, topo):
         dma("so%d" % h, "Y", "q%d#" % h, T.oc[:, 4 * a0:4 * a1], fq[:, a0:a1].bitcast(dt.uint8), "st")
         dma("sy%d" % h, "S" if h else "Y", "yc%d" % h, T.y[:, a0:a1], T.ysb[:, a0:a1], "st")
     for k in range(4):
-        dma("ss%d" % k, "S" if k == 3 else "Y", "q0# q1#", T.osc[4 * k:4 * k + 4, :], fs[32 * k:32 * k + 4, :], "st")
+        dma("ss%d" % k, "S" if k > 1 else "Y", "q0# q1#", T.osc[4 * k:4 * k + 4, :], fs[32 * k:32 * k + 4, :], "st")
     fixed["st"] = ("st", 16 * 8)
     op("end", "G", None, "st loc")
     emit(g, T, ops, fixed)

@@ -4,7 +4,7 @@ from concourse.mybir import dt, AluOpType, ActivationFunctionType
 A = AluOpType
 F = ActivationFunctionType
 C, TM, ROUNDS = 448, 96, 2
-MID = 256
+MID = 288
 H = 464
 Z0 = 3072.0
 LOW = Z0 - 480
@@ -13,11 +13,11 @@ POFF = 2 + TM
 WS = 656
 NP = 816
 W1 = MID // 16 + 1
-SEL, C2 = 32, 32 + 2 * C
-FD = C - MID + H + 16
+SEL, C2 = H, H + 2 * C
+MK = MID + 32
 CUT = (0, MID, C)
-GP = (0, 128, MID, C)
-PP = (0, 16, 32, 42, 51)
+GP = (0, 160, MID, C)
+PD, PW = (0, 16, 36, 51), (0, 36, 51)
 Q4, U8, BF, F16, F32, I32, U16 = "float8_e4m3fn_x4", "uint8", "bfloat16", "float16", "float32", "int32", "uint16"
 SCRATCH = {}
 for _n, _w, _d in [
@@ -25,40 +25,42 @@ for _n, _w, _d in [
     ("us", 128, U8), ("uq2", 128, Q4), ("us2", 128, U8), ("vq", 128, Q4), ("vs", 128, U8), ("et", 520, BF),
     ("eq", 512, Q4), ("es", 512, U8), ("pi", 8, I32), ("pj", 8, I32), ("cl", 8, F32), ("nf", 52, F32),
     ("lui", 8, I32), ("lu", 8, U16), ("lp", 52, U16), ("tw", 17 * 52, F32), ("wi", 52, I32),
-    ("fb", C2 + 2 * H, F16), ("pat", 928, BF), ("mk", 928, BF), ("mask", NP, BF), ("sg", 2 * C, BF),
-    ("ysb", C, F32), ("z", 2 * H, BF), ("kt", 448, BF), ("nw", 64, BF), ("fd", FD, BF), ("nc", 2 * H, F16),
-    ("m", 2 * H, BF), ("win", 4 * WS, BF), ("m01", 768, BF), ("dz", 2 * H, BF), ("acc", 8, F32), ("ec", 348, BF),
+    ("fb", C2 + H, F16), ("pat", MK, BF), ("mk", MK, BF), ("mask", NP, BF), ("sg", 2 * C, BF),
+    ("ysb", C, F32), ("z", 2 * H, BF), ("kt", 448, BF), ("nw", 64, BF), ("fd", H, BF), ("nc", 2 * H, F16),
+    ("m", 2 * H, BF), ("win", 4 * WS, BF), ("m01", 640, BF), ("dz", 2 * H, BF), ("acc", 8, F32), ("ec", 348, BF),
     ("rm", 348, BF), ("ml", 12, U16), ("mt", 8 * TM, BF), ("dg", NP, BF), ("ee", NP, BF), ("wn", NP, BF),
     ("rr", NP, BF), ("ab", 2 * C, F16), ("tr", 928, F16), ("ss", 928, F16), ("ev", 96, F32), ("el", 28, U16),
-    ("xn", 4 * C, BF), ("pc", 2 * C, BF), ("ib", 4 * C, BF),
+    ("xn", 4 * C, BF), ("pc", C, BF), ("ib", 4 * C, BF), ("jb", 2 * C, BF),
 ] + [(_n + str(_r), _w, _d) for _r in range(ROUNDS) for _n, _w, _d in [
     ("mq", 2 * TM, Q4), ("ms", 2 * TM, U8), ("lq", 320, Q4), ("ls", 320, U8)]
 ] + [(_n + str(_r), C, _d) for _r in range(ROUNDS + 1) for _n, _d in [("aq", Q4), ("as", U8)]]:
     SCRATCH[_n] = ("sbuf", [128, _w], _d)
-SCRATCH["pss"] = ("psum", [128, 1024], F32)
+SCRATCH["pss"] = ("psum", [128, 1536], F32)
 SCRATCH["psp"] = ("psum", [128, 2048], F32)
 NSEM = 140
 SEMAPHORES = ["arr0", "arr1", "loc", "st"] + ["k%d" % _i for _i in range(NSEM)]
 
-ON_V = "dg0 mo0 mo1 yc1"
+ON_V = "dg0 dl0 dl2 dr0 dr2 mo0 mo1 yc2"
 ORDER = {
-    "V": "one res kt colz ca l0 par hi fil z0 l1 z2 z1 nhi colw lq lu cb l2 l11 l9 uq l6 l3 us2 uq2 l4 q0_0 l5 l8 l10 "
-         "q1_0 l12 l7 col0 l13 l14 e1 e3 k0_0 za_0 zb_0 zc_0 kb_0 fa_0 fx_0 l15 l16 kp_0 e1_0 e0_0 cmb t1_0 t2_0 e2_0 "
-         "e3_0 ka_0 rm0_0 rm1_0 rm2_0 key_0 nz_0 l17 mla_0 mlb_0 ta_0 lp tb_0 mo1_0 mo0_0 df_0 da_0 mq_0 dg0_0 dx_0 "
-         "ma_0 ee0_0 mx_0 rr0_0 gz_0 ee1_0 fl_0 ia0_0 ic0_0 e0 sa0_0 sb0_0 rr1_0 va_0 ia1_0 ic1_0 r0_0 r1_0 sb1_0 "
-         "sa1_0 n0_0 n1_0 vb_0 e2 o00_0 r2_0 r3_0 o10_0 n2_0 n3_0 o20_0 o01_0 el0_0 o11_0 x00_0 o21_0 x01_0 el1_0 "
-         "x02_0 ad1_0 x03_0 x10_0 x12_0 ad2_0 q0_1 x22_0 x20_0 q1_1 za_1 vq fa_1 fl_1 k0_1 zb_1 zc_1 ka_1 kb_1 fx_1 "
-         "nz_1 ta_1 kp_1 e0_1 e1_1 t2_1 t1_1 e2_1 e3_1 rm0_1 rm1_1 rm2_1 da_1 mla_1 mlb_1 key_1 tb_1 mo1_1 mo0_1 ma_1 "
-         "df_1 mq_1 dg0_1 dx_1 ee0_1 mx_1 rr0_1 gz_1 ia0_1 ic0_1 ee1_1 sa0_1 sb0_1 rr1_1 va_1 ic1_1 ia1_1 r0_1 r1_1 "
-         "sb1_1 sa1_1 n0_1 n1_1 vb_1 o00_1 r2_1 r3_1 o10_1 n2_1 n3_1 o20_1 o01_1 el0_1 o11_1 x03_1 o21_1 x02_1 el1_1 "
-         "x01_1 ad1_1 x00_1 x12_1 x10_1 ad2_1 q0_2 x20_1 x22_1 q1_2 yc1",
-    "S": "du w1 w3 w4 sev m1 w0 m0 w2 sg0_0 sg1_0 c1_0 c0_0 c3_0 c2_0 mo3_0 mo2_0 wn1_0 dg1_0 dg3_0 wn0_0 dg2_0 wn3_0 "
-         "wn2_0 mk dr1_0 dr0_0 dl3_0 dl0_0 dl1_0 dr3_0 dl2_0 dr2_0 h13_0 h11_0 h21_0 h23_0 sg0_1 sg1_1 c3_1 c1_1 c2_1 "
-         "c0_1 mo3_1 mo2_1 wn1_1 dg1_1 wn0_1 dg3_1 dg2_1 wn2_1 wn3_1 dl3_1 dr3_1 dr1_1 dl1_1 dl2_1 dr2_1 dr0_1 h11_1 "
-         "h13_1 dl0_1 h21_1 h23_1 yc0 sy1 ss3 ss2",
-    "T": "sc0_0 sc1_0 p1_0 p0_0 p3_0 p2_0 u1_0 u0_0 u3_0 u2_0 sc0_1 sc1_1 p3_1 p1_1 p2_1 p0_1 u3_1 u1_1 u2_1 u0_1 y0 y1",
-    "G": "gp gn glu ge gf0 gw0 gm1 gf2 gf1 gm0 gw1 gpat sd0_0 sd1_0 ib3_0 ib1_0 ib1_1 sd0_1 sd1_1 ib3_1 end",
-    "Y": "dx0 dx1 dw0 dws dw1 pc2_0 pc0_0 dv pc0_1 pc2_1 so0 sy0 so1 ss0 ss1",
+    "V": "one par z0 res hi cma colz colw l0 col0 lu ca cmb l1 cb lq kt l2 l9 uq l6 nhi z1 l3 uq2 l7 l8 q0_0 l4 q1_0 "
+         "l13 q2_0 l10 l5 col1 e1 e3 za_0 l12 l16 fa_0 da_0 k0_0 zb_0 zc_0 fx_0 fy_0 ma_0 l15 kp_0 e0_0 e1_0 k1_0 t1_0 "
+         "t2_0 e3_0 e2_0 df_0 rm0_0 rm2_0 rm1_0 l17 dw_0 mla_0 mlb_0 ta_0 nz_0 tb_0 mo0_0 lp mo1_0 mw_0 dx_0 mq_0 "
+         "dg0_0 e2 dy_0 ee0_0 mx_0 my_0 rr0_0 e0 gz_0 fl_0 ic0_0 ia0_0 ee1_0 sb0_0 sa0_0 rr1_0 va_0 ia1_0 ic1_0 r0_0 "
+         "sb1_0 sa1_0 r1_0 n0_0 vb_0 n1_0 r2_0 r3_0 o00_0 n2_0 n3_0 o10_0 o01_0 o20_0 dl0_0 dr0_0 o11_0 el0_0 dr2_0 "
+         "dl2_0 o21_0 x00_0 el1_0 x03_0 x02_0 ad1_0 x01_0 ae1_0 ad2_0 x10_0 ae2_0 q0_1 x20_0 q1_1 q2_1 za_1 vq fl_1 "
+         "k0_1 da_1 fa_1 ma_1 zb_1 k1_1 zc_1 fx_1 fy_1 nz_1 dy_1 kp_1 e0_1 e1_1 tb_1 t2_1 t1_1 e3_1 e2_1 df_1 rm0_1 "
+         "rm2_1 rm1_1 ta_1 my_1 mlb_1 mla_1 dg0_1 mo0_1 mo1_1 dx_1 dw_1 mq_1 ee0_1 mw_1 mx_1 rr0_1 gz_1 ia0_1 ic0_1 "
+         "ee1_1 sa0_1 sb0_1 rr1_1 va_1 ia1_1 ic1_1 r1_1 sb1_1 sa1_1 r0_1 n1_1 vb_1 n0_1 r2_1 r3_1 o00_1 n2_1 n3_1 o10_1 "
+         "dl0_1 o01_1 o20_1 dr0_1 o11_1 el0_1 dr2_1 dl2_1 o21_1 x00_1 el1_1 x03_1 x02_1 ad1_1 x01_1 ae1_1 ad2_1 x10_1 "
+         "ae2_1 q0_2 x20_1 q1_2 q2_2 yc2",
+    "S": "du m1 w3 w1 w2 sev us2 w4 m0 sg0_0 sg1_0 sg2_0 w0 c1_0 c0_0 c3_0 c2_0 mo3_0 mo2_0 dg1_0 wn0_0 dg2_0 wn1_0 "
+         "mk ib3_0 ib2_0 dr1_0 dl1_0 dr3_0 dl3_0 h11_0 h13_0 h12_0 h23_0 h21_0 h22_0 sg0_1 sg1_1 sg2_1 c3_1 c1_1 c2_1 "
+         "c0_1 dg1_1 mo3_1 mo2_1 wn0_1 dg2_1 wn1_1 ib2_1 dl1_1 dr1_1 dr3_1 dl3_1 h11_1 h13_1 h12_1 h21_1 h23_1 h22_1 "
+         "yc0 ss3 yc1 ss2 sy2",
+    "T": "sc0_0 sc1_0 sc2_0 p1_0 p0_0 p3_0 p2_0 u1_0 u0_0 u3_0 u2_0 sc0_1 sc1_1 sc2_1 p3_1 p1_1 p2_1 p0_1 u1_1 u0_1 "
+         "u3_1 u2_1 y0 y1 y2",
+    "G": "gp gn glu gf0 ge gf1 gf2 gw0 gw1 gm1 gm0 gpat ib1_0 sd0_0 sd1_0 ib3_1 sd0_1 sd1_1 ib1_1 end",
+    "Y": "dx0 dx1 dw0 dws dw1 dv pc0_0 pc0_1 so0 so1 so2 sy0 ss0 sy1 ss1",
 }
 
 
@@ -142,11 +144,11 @@ def rank_program(g, core, T, topo):
     def act(n, d, out, a, fn, **kw):
         op(n, "S", lambda: S.activation(out, a, fn, **kw), d)
 
-    def pick(n, d, out, a, scale=None):
+    def pick(n, d, out, a, scale=None, bias=0.0):
         if n.rstrip("#") not in ON_V.split():
-            act(n, d, out, a, F.Copy, scale=scale or 1.0)
+            act(n, d, out, a, F.Identity, scale=scale or 1.0, bias=bias)
         elif scale:
-            ts(n, d, out, a, scale, None, A.mult)
+            ts(n, d, out, a, scale, bias, A.mult, A.add)
         else:
             cp(n, d, out, a)
 
@@ -174,23 +176,23 @@ def rank_program(g, core, T, topo):
     iota("gp", "", T.pi[:, 0:1], [[0, 1]], 0, 1, small=False)
     iota("glu", "", T.lui[:], [[16, 8]], 0, small=False)
     iota("gn", "", T.nf[:], [[16, 52]], 0)
-    iota("gf0", "", fd[:], [[0, FD // 2], [2, 2]], 0)
-    iota("gf1", "gf0", fd[:, 15:FD:16], [[0, FD // 16]], 4096)
-    iota("gf2", "gf0", fd[:, C - MID:FD:H], [[0, 2]], 4096)
+    iota("gf0", "", fd[:], [[0, H // 2], [2, 2]], 0)
+    iota("gf1", "gf0", fd[:, 15:H:16], [[0, H // 16]], 4096)
+    iota("gf2", "gf0", fd[:, C:C + 1], [[0, 1]], 4096)
     iota("gw0", "", T.nw[:, 0:58], [[0, 2], [-16, 29]], 249)
     iota("gw1", "gw0", T.nw[:, 28:58:29], [[0, 2]], 256 - C - TM)
     ms("one", "", mask[:], 1.0)
     op("ge", "G", lambda: g.affine_select(T.et[:], mask[:, 0:520], [[-1, 520]], A.is_equal, 0.0, 3, 4), "one")
-    iota("gpat", "", T.pat[:], [[0, 29], [1, 2], [0, 16]], 0)
+    iota("gpat", "", T.pat[:], [[0, MK // 32], [1, 2], [0, 16]], 0)
     act("w0", "one", win[:, 0:POFF], mask[:, 0:POFF], F.Copy, scale=0.0)
     for b in range(4):
         w = WS - C if b < 3 else WS - C - POFF
         act("w%d" % (b + 1), "one", win[:, WS * b + POFF + C:WS * b + POFF + C + w], mask[:, 0:w], F.Copy, scale=0.0)
     act("sev", "one", sg[:, 0:2 * C:2], mask[:, 0:C], F.Copy, scale=-1.0)
-    act("m0", "one", T.m01[:, 0:768:2], mask[:, 0:384], F.Copy, scale=0.0)
-    act("m1", "one", T.m01[:, 1:768:2], mask[:, 0:384], F.Copy)
+    act("m0", "one", T.m01[:, 0:640:2], mask[:, 0:320], F.Copy, scale=0.0)
+    act("m1", "one", T.m01[:, 1:640:2], mask[:, 0:320], F.Copy)
     res, hi, par = T.pj[:, 0:1], T.pj[:, 1:2], T.pj[:, 2:3]
-    colz, col0, colw, nhi, cmb = [T.cl[:, i:i + 1] for i in range(5)]
+    colz, col0, col1, colw, nhi, cmb, cma = [T.cl[:, i:i + 1] for i in range(7)]
     ts("res", "gp", res, T.pi[:, 0:1], 15, None, A.bitwise_and)
     ts("hi", "gp", hi, T.pi[:, 0:1], 4, 1, A.logical_shift_right, A.bitwise_and)
     ts("par", "gp", par, T.pi[:, 0:1], 1, None, A.bitwise_and)
@@ -198,22 +200,22 @@ def rank_program(g, core, T, topo):
     ts("colw", "par", colw, par, 1280.0, None, A.add)
     ts("cmb", "par", cmb, par, -1.0, POFF + C - 257.0, A.mult, A.add)
     ts("col0", "colz colw", col0, colz, colw, C + 1024 + 7.5, A.subtract, A.add)
+    ts("col1", "col0", col1, col0, -1.0, None, A.mult)
+    ts("cma", "par", cma, par, POFF + 256.0, None, A.add)
     ts("nhi", "hi", nhi, hi, -CAP, None, A.mult)
     act("mk", "gpat nhi", T.mk[:], T.pat[:], F.Abs, scale=CAP, bias=nhi)
     cp("lu", "glu", T.lu[:], T.lui[:])
     quant("uq", "du", T.uq[:], T.us[:], T.ut[:])
     cp("uq2", "uq lu", T.uq2[:].bitcast(dt.uint32), T.uq[:].bitcast(dt.uint32).indirect(T.lu[:, 0:8]))
-    cp("us2", "uq lu", T.us2[:], T.us[:].indirect(T.lu[:, 0:8]))
-    ca, cb = C2, C2 + H
-    scan("ca", "one", fb[:, ca:ca + C + 1], mask[:, 0:C + 1], mask[:, 0:C + 1], 1023.0, A.add, A.mult)
-    ts("cb", "ca", fb[:, cb:cb + C + 1], fb[:, ca:ca + C + 1], 0.25, None, A.mult)
-    ts("fil", "one", fb[:, 0:SEL], mask[:, 0:SEL], 2048.0, None, A.mult)
+    op("us2", "S", lambda: S.activation(T.us2[:], T.us[:].indirect(T.lu[:, 0:8]), F.Copy), "uq lu")
+    ca, cb = C2, 0
+    scan("ca", "one", fb[:, ca:ca + H], mask[:, 0:H], mask[:, 0:H], 1023.0, A.add, A.mult)
+    ts("cb", "ca", fb[:, cb:cb + H], fb[:, ca:ca + H], 0.25, None, A.mult)
     ms("z0", "", z[:, 0:2 * H:H], Z0)
-    ms("z1", "", z[:, C + 1:H], LOW)
-    ms("z2", "", z[:, H + C + 1:2 * H], LOW)
+    ms("z1", "", z[:, C + 1:2 * H:H], LOW)
     ms("kt", "", kt[:], LOW)
-    iota("gm0", "ge w0 w1 w2 w3 w4 sev m0 m1 ca fil", mask[:, 0:812:29], [[0, 28]], 0)
-    iota("gm1", "ge w0 w1 w2 w3 w4 sev m0 m1 ca fil", mask[:, 28:812:28], [[0, 28]], 0)
+    iota("gm0", "ge w0 w1 w2 w3 w4 sev m0 m1 ca", mask[:, 0:812:29], [[0, 28]], 0)
+    iota("gm1", "ge w0 w1 w2 w3 w4 sev m0 m1 ca", mask[:, 28:812:28], [[0, 28]], 0)
     for b in range(4):
         quant("e%d" % b, "ge", T.eq[:, 128 * b:128 * b + 128], T.es[:, 128 * b:128 * b + 128], T.et[:, 3 - b:515 - b])
     quant("vq", "dv", T.vq[:], T.vs[:], T.vt[:])
@@ -225,23 +227,21 @@ def rank_program(g, core, T, topo):
     ts("l2", "lq", tw[2], qv, -29.0, None, A.mult)
     tt("l3", "l2", tw[3], tw[2], tw[0], A.add)
     tt("l4", "l3", tw[4], tw[3], qv, A.add)
-    ts("l5", "l4", tw[5], tw[4], 28.0, None, A.is_ge)
+    ts("l5", "l4", tw[5], tw[4], 28.0, None, A.is_gt)
     ts("l6", "lq", tw[6], qv, -1.0, 57.0, A.mult, A.add)
     ts("l7", "l3", tw[7], tw[3], -1.0, 28.0, A.mult, A.add)
     ts("l8", "l3", tw[8], tw[3], 0.0, None, A.is_equal)
-    ts("l9", "lq", tw[9], qv, 37.0, None, A.add)
-    ts("l10", "l4", tw[10], tw[4], 28.0, None, A.is_equal)
-    ts("l11", "lq", tw[11], qv, -1.0, 64.0, A.mult, A.add)
+    ts("l9", "lq", tw[9], qv, -1.0, 92.0, A.mult, A.add)
+    ts("l10", "l4", tw[10], tw[4], 28.0, 64.0, A.is_equal, A.mult)
     tt("l12", "l5 l6", tw[12], tw[5], tw[6], A.mult)
     tt("l13", "l8 l9", tw[13], tw[8], tw[9], A.mult)
-    tt("l14", "l10 l11", tw[14], tw[10], tw[11], A.mult)
     tt("l15", "l12 l7", tw[15], tw[12], tw[7], A.add)
-    tt("l16", "l13 l14", tw[16], tw[13], tw[14], A.add)
+    tt("l16", "l13 l10", tw[16], tw[13], tw[10], A.add)
     tt("l17", "l15 l16", tw[2], tw[15], tw[16], A.add)
     ts("lp", "l17", T.lp[:], tw[2], 121.0, None, A.min)
-    for h in range(2):
-        quant("q%d_0" % h, "dx%d" % h, T.aq0[:, CUT[h]:CUT[h + 1]], T.as0[:, CUT[h]:CUT[h + 1]],
-              T.xt[:, 4 * CUT[h]:4 * CUT[h + 1]])
+    for h in range(3):
+        quant("q%d_0" % h, "dx%d" % (h // 2), T.aq0[:, GP[h]:GP[h + 1]], T.as0[:, GP[h]:GP[h + 1]],
+              T.xt[:, 4 * GP[h]:4 * GP[h + 1]])
 
     def link(src_rank, dst_rank):
         src, dst = T.cores[src_rank], T.cores[dst_rank]
@@ -254,64 +254,69 @@ def rank_program(g, core, T, topo):
 
     others = [o for o in (rank - 1, rank + 1) if 0 <= o < n_ranks]
     fixed["loc"] = ("loc", 2 * ROUNDS * sum(link(rank, o)[2] for o in others))
-    key, td, keyp, tb, tbw = kt[:, 0:58], kt[:, 64:192], kt[:, 192:250], kt[:, 320:378], kt[:, 320:448]
+    td, keyp, tb, tbw = kt[:, 64:192], kt[:, 192:250], kt[:, 320:378], kt[:, 320:448]
     fv = nc[:, 0:2 * H:16]
     plane = lambda b: win[:, WS * b:WS * (b + 1)]
     own = lambda b: win[:, WS * b + POFF:WS * b + POFF + C]
+    twin = lambda b, a0, a1: (T.pc[:, a0:a1] if b == 0 else T.jb[:, 2 * a0:2 * a1:2] if b == 2
+                              else T.ib[:, 4 * a0 + b - 1:4 * a1:4])
     for r in range(ROUNDS):
         rnd[0] = r
         aq, asc, nq, ns = T["aq%d" % r], T["as%d" % r], T["aq%d" % (r + 1)], T["as%d" % (r + 1)]
         mq, msc, lqb, lsb = T["mq%d" % r], T["ms%d" % r], T["lq%d" % r], T["ls%d" % r]
         arr = "arr%d" % r
         fixed[arr] = (arr, sum(2 * link(o, rank)[2] for o in others))
-        for h in range(2):
-            a0, a1 = CUT[h:h + 2]
+        for h in range(3):
+            a0, a1 = GP[h:h + 2]
             mm("sc%d#" % h, "uq2 us2 q%d#" % h, T.pss[:, 512 * h:512 * h + a1 - a0], T.uq2[:], T.us2[:],
                aq[:, a0:a1], asc[:, a0:a1])
             act("sg%d#" % h, "sc%d#" % h, sg[:, 2 * a0 + 1:2 * a1:2], T.pss[:, 512 * h:512 * h + a1 - a0], F.Sign,
                 bias=2.0 ** -110, accum_out=acc[:, h:h + 1])
         for b in range(4):
-            mm("p%d#" % b, "dw%d dws q0# q1#" % (b // 2), T.psp[:, 512 * b:512 * b + C],
+            mm("p%d#" % b, "dw%d dws q0# q1# q2#" % (b // 2), T.psp[:, 512 * b:512 * b + C],
                T.wq[:, 128 * b:128 * b + 128], T.wsc[:, 128 * b:128 * b + 128], aq[:], asc[:])
             act("c%d#" % b, "p%d#" % b, own(b), T.psp[:, 512 * b:512 * b + C], F.Copy, scale=0.0625)
-        for b in (0, 2):
-            dma("pc%d#" % b, "Y", "c%d#" % b, T.pc[:, C * (b // 2):C * (b // 2 + 1)], own(b))
-        s0, s1, sr = sg[:, 1:2 * MID:2], sg[:, 2 * MID + 1:2 * C:2], sg[:, 2 * C - 1:0:-2]
-        scan("za#", "sg0# colz", z[:, 1:MID + 1], s0, s0, colz, A.add, A.max)
-        ts("k0#", "sg0# colz", acc[:, 5:6], acc[:, 0:1], colz, None, A.add)
-        scan("fa#", "za# gf1 gf2", nc[:, MID - 1::-1], fd[:, 511:511 - MID:-1], z[:, MID:0:-1], 0.0, A.add, A.min)
-        scan("da#", "za# z0", dz[:, 0:MID], z[:, 1:MID + 1], z[:, 0:MID], 0.0, A.max, A.subtract)
-        ts("ma#", "da#", m[:, 0:MID], dz[:, 0:MID], 1.0 / 16, 1.0, A.mult, A.add)
-        scan("zb#", "sg0# sg1# colz", z[:, H + 1:H + C + 1], sr, sr, colz, A.max, A.subtract)
-        scan("zc#", "sg1# k0#", z[:, MID + 1:C + 1], s1, s1, acc[:, 5:6], A.add, A.max)
-        scan("fx#", "zb# zc# z0 z1 z2 gf1 gf2", nc[:, H + C:MID - 1:-1], fd[:, C - MID + H::-1],
-             z[:, H + C + 1:MID:-1], 0.0, A.add, A.min)
-        scan("dx#", "za# zb# zc# z0 z1", dz[:, MID:H + C], z[:, MID + 1:H + C + 1], z[:, MID:H + C], 0.0, A.max,
-             A.subtract)
-        ts("mx#", "dx#", m[:, MID:H + C], dz[:, MID:H + C], 1.0 / 16, 1.0, A.mult, A.add)
-        ms("gz#", "ma# mx#", m[:, 0:2 * H:16], 0.0)
-        ts("ka#", "sg0# sg1# col0", acc[:, 3:4], acc[:, 0:1], acc[:, 1:2], col0, A.add, A.add)
-        ts("kb#", "sg0# sg1# col0", acc[:, 4:5], acc[:, 0:1], acc[:, 1:2], col0, A.add, A.subtract)
-        ts("ta#", "ka# za# zc# z0 kt", kt[:, 384:413], z[:, 0:C + 1:16], acc[:, 3:4], -1.0, A.subtract, A.mult)
-        ts("tb#", "kb# zb# z0 kt", kt[:, 413:442], z[:, H:H + C + 1:16], acc[:, 4:5], -1.0, A.add, A.mult)
-        ts("nz#", "za# zb# zc# z0 kt", kt[:, 128:186], z[:, 0:2 * H:16], -1.0, LOW + 8, A.mult, A.add)
-        scan("kp#", "fa# fx# gw1 kt", keyp, T.nw[:, 0:58], fv, 4096.0, A.min, A.add)
-        ts("key#", "fa# fx# kt", key, fv, -7.0, None, A.add)
-        ts("e0#", "fa# fx#", T.ec[:, 0:58], fv, 1 - Z0, 1024.0, A.add, A.mult)
-        ts("e1#", "fa# fx#", T.ec[:, 58:116], fv, 17 - Z0, 1024.0, A.add, A.mult)
-        scan("t1#", "kp#", tb, fv, keyp, 0.0, A.max, A.subtract)
-        scan("t2#", "kp#", kt[:, 262:320], fv, keyp, 0.0, A.max, A.subtract)
+        dma("pc0#", "Y", "c0#", T.pc[:], own(0))
+        for b in (2,) if r else (2, 3):
+            act("ib%d#" % b, "c%d#" % b, twin(b, 0, C), own(b), F.Copy)
+        for b in (1, 3) if r else (1,):
+            op("ib%d#" % b, "G", lambda b=b: g.affine_select(twin(b, 0, C), own(b), [[0, C]], A.is_ge, 0.0, 0, 0),
+               "c%d#" % b)
+        e = GP[1]
+        s0, s1, sr = sg[:, 1:2 * e:2], sg[:, 2 * e + 1:2 * C:2], sg[:, 2 * C - 1:0:-2]
+        scan("za#", "sg0# colz", z[:, 1:e + 1], s0, s0, colz, A.add, A.max)
+        ts("k0#", "sg0# colz col0 col1", acc[:, 5:8], T.cl[:, 0:3], acc[:, 0:1], None, A.add)
+        ts("k1#", "sg1# sg2#", acc[:, 3:4], acc[:, 1:2], acc[:, 2:3], None, A.add)
+        scan("zb#", "sg0# sg1# sg2# colz", z[:, H + 1:H + C + 1], sr, sr, colz, A.max, A.subtract)
+        scan("zc#", "sg1# sg2# k0#", z[:, e + 1:C + 1], s1, s1, acc[:, 5:6], A.add, A.max)
+        scan("fa#", "za# gf1 gf2", nc[:, e - 1::-1], fd[:, e - 1::-1], z[:, e:0:-1], 0.0, A.add, A.min)
+        scan("fx#", "zb# z1 gf1 gf2", nc[:, H + C:H - 1:-1], fd[:, C::-1], z[:, H + C + 1:H:-1], 0.0, A.add, A.min)
+        scan("fy#", "zc# z1 gf1 gf2", nc[:, C:e - 1:-1], fd[:, C:e - 1:-1], z[:, C + 1:e:-1], 0.0, A.add, A.min)
+        for n, d, a0, a1 in (("a", "za# z0", 0, e), ("x", "za# zc#", e, C), ("y", "zb# z0", H, H + C // 2),
+                             ("w", "zb#", H + C // 2, H + C)):
+            scan("d%s#" % n, d, dz[:, a0:a1], z[:, a0 + 1:a1 + 1], z[:, a0:a1], 0.0, A.max, A.subtract)
+            ts("m%s#" % n, "d%s#" % n, m[:, a0:a1], dz[:, a0:a1], 1.0 / 16, 1.0, A.mult, A.add)
+        ms("gz#", "ma# mx# my# mw#", m[:, 0:2 * H:16], 0.0)
+        ts("ta#", "k0# k1# za# zc# z0 kt", kt[:, 441:412:-1], z[:, 0:C + 1:16], acc[:, 3:4], acc[:, 6:7], A.subtract,
+           A.subtract)
+        ts("tb#", "k0# k1# zb# z0 kt", kt[:, 412:383:-1], z[:, H:H + C + 1:16], acc[:, 3:4], acc[:, 7:8], A.add, A.add)
+        ts("nz#", "za# zb# zc# z0 kt", kt[:, 185:127:-1], z[:, 0:2 * H:16], -1.0, LOW + 8 - 80, A.mult, A.add)
+        scan("kp#", "fa# fx# fy# gw1 kt", keyp, T.nw[:, 0:58], fv, 4096.0, A.min, A.add)
+        ts("e0#", "fa# fx# fy#", T.ec[:, 0:58], fv, 1 - Z0, -1024.0, A.add, A.mult)
+        ts("e1#", "fa# fx# fy#", T.ec[:, 58:116], fv, 17 - Z0, -1024.0, A.add, A.mult)
+        scan("t1#", "kp#", tb, keyp, fv, 0.0, A.max, A.subtract)
+        scan("t2#", "kp#", kt[:, 262:320], keyp, fv, 0.0, A.max, A.subtract)
         for i in (1, 2):
-            ts("e%d#" % (i + 1), "e0# e1#", T.ec[:, 116 * i:116 * i + 116], T.ec[:, 0:116], 32768.0 * i, None, A.add)
-        scan("df#", "key#", kt[:, 64:121], kt[:, 0:57], kt[:, 1:58], 0.0, A.max, A.subtract)
+            ts("e%d#" % (i + 1), "e0# e1#", T.ec[:, 116 * i:116 * i + 116], T.ec[:, 0:116], -32768.0 * i, None, A.add)
+        scan("df#", "kp#", kt[:, 64:121], kt[:, 192:249], kt[:, 193:250], 0.0, A.max, A.subtract)
         for i in range(3):
             back = slice(116 * i + 115, 116 * i - 1 if i else None, -1)
             scan("rm%d#" % i, "t1# t2# e0# e1#" + (" e%d#" % (i + 1) if i else ""), T.rm[:, back], T.ec[:, back],
-                 kt[:, 377:261:-1], 0.0, A.min, A.max)
-        ts("mla#", "rm0# rm1# rm2# colw", T.ml[:, 0:6], T.rm[:, 0:348:58], colw, POFF - 1024.0, A.add, A.add)
-        ts("mlb#", "rm0# rm1# rm2# cmb", T.ml[:, 6:12], T.rm[:, 29:348:58], -1.0, cmb, A.mult, A.add)
+                 kt[:, 377:261:-1], 0.0, A.max, A.min)
+        ts("mla#", "rm0# rm1# rm2# cma", T.ml[:, 0:6], T.rm[:, 0:348:58], -1.0, cma, A.mult, A.add)
+        ts("mlb#", "rm0# rm1# rm2# cmb", T.ml[:, 6:12], T.rm[:, 29:348:58], cmb, None, A.add)
         for b in range(4):
-            pick("mo%d#" % b, "mla# mlb# c%d# w%d w%d" % (b, b, b + 1), T.mt[:, b:8 * TM:4],
+            pick("mo%d#" % b, "mla# mlb# c%d# w%d w%d" % (b, b, b + 1) + " mq_0" * r, T.mt[:, b:8 * TM:4],
                  plane(b).indirect(T.ml[:, 0:12]))
         quant("mq#", "mo0# mo1# mo2# mo3#", mq[:], msc[:], T.mt[:])
 
@@ -330,20 +335,17 @@ def rank_program(g, core, T, topo):
 
         op("sd0#", "G", lambda send=send: send(0), "mq#")
         op("sd1#", "G", lambda send=send: send(1), "mq#")
-        for b in (1, 3):
-            op("ib%d#" % b, "G", lambda b=b: g.affine_select(T.ib[:, b - 1:4 * C:4], own(b), [[0, C]], A.is_ge, 0.0,
-                                                             0, 0), "c%d#" % b)
-        for i in range(4):
-            a0, a1 = PP[i:i + 2]
-            pick("dg%d#" % i, "df# nz# lp", T.dg[:, 16 * a0:16 * a1], td.indirect(T.lp[:, a0:a1]), 128.0)
-        for i in range(4):
-            a0, a1 = PP[i:i + 2]
+        for i in range(3):
+            a0, a1 = PD[i:i + 2]
+            pick("dg%d#" % i, "df# nz# lp", T.dg[:, 16 * a0:16 * a1], td.indirect(T.lp[:, a0:a1]), -128.0, 2048.0)
+        for i in range(2):
+            a0, a1 = PW[i:i + 2]
             pick("wn%d#" % i, "t1# ta# tb# lp", T.wn[:, 16 * a0:16 * a1], tbw.indirect(T.lp[:, a0:a1]))
         for h, (a0, a1) in enumerate(((0, 29 * W1), (29 * W1, NP))):
-            scan("ee%d#" % h, "dg0# dg1# gm0 gm1" + (" dg2# dg3#" if h else ""), T.ee[:, a0:a1], mask[:, a0:a1],
+            scan("ee%d#" % h, "dg0# dg1# gm0 gm1" + (" dg2#" if h else ""), T.ee[:, a0:a1], mask[:, a0:a1],
                  T.dg[:, a0:a1], 0.0, A.mult, A.add)
-            scan("rr%d#" % h, "ee%d# wn0# wn1#" % h + (" wn2# wn3#" if h else ""), T.rr[:, a0:a1], T.ee[:, a0:a1],
-                 T.wn[:, a0:a1], 0.0, A.min, A.max)
+            scan("rr%d#" % h, "ee%d# wn0#" % h + (" wn1#" if h else ""), T.rr[:, a0:a1], T.ee[:, a0:a1],
+                 T.wn[:, a0:a1], 0.0, A.max, A.min)
         fill = ""
         if not (has_l and has_r):
             f0, fill = 2 * TM if has_r else TM, " fl#"
@@ -352,9 +354,9 @@ def rank_program(g, core, T, topo):
         for h, (w0, w1) in enumerate(((0, W1), (W1, 28))):
             a0, a1 = 16 * w0, 16 * w1
             ts("ia%d#" % h, "rr%d# cb colw" % h, fb[:, ca + a0 + 16:ca + a1 + 1:16], T.rr[:, 27 + 28 * w0:28 * w1:28],
-               colw, None, A.add)
+               -1.0, colw, A.mult, A.add)
             ts("ic%d#" % h, "rr%d# cb colw" % h, fb[:, cb + C - a0:cb + C - a1:-16], T.rr[:, 28 + 29 * w0:29 * w1:29],
-               colw, 0.25, A.add, A.mult)
+               colw, -0.25, A.subtract, A.mult)
             scan("sa%d#" % h, "ia%d# gz#" % h, ab[:, 2 * a1 - 2:(2 * a0 - 2 if h else None):-2], m[:, a1:a0:-1],
                  fb[:, ca + a1:ca + a0:-1], 0.0, A.mult, A.max)
             scan("sb%d#" % h, "ic%d# gz#" % h, ab[:, 2 * a0 + 1:2 * a1:2], m[:, H + C - a0:H + C - a1:-1],
@@ -365,25 +367,25 @@ def rank_program(g, core, T, topo):
             mm("u%d#" % b, "e%d c%d# %s" % (b, b, arr) + fill, T.psp[:, 512 * b:512 * b + ln],
                T.eq[:, 128 * b:128 * b + 128], T.es[:, 128 * b:128 * b + 128], lqb[:, l0:l0 + ln], lsb[:, l0:l0 + ln])
             if has_l:
-                act("dl%d#" % b, "u%d# mo%d#" % (b, b), win[:, WS * b + POFF - 1:WS * b + 1:-1],
-                    T.psp[:, 512 * b:512 * b + TM], F.Copy)
+                pick("dl%d#" % b, "u%d# mo%d#" % (b, b), win[:, WS * b + POFF - 1:WS * b + 1:-1],
+                     T.psp[:, 512 * b:512 * b + TM])
             if has_r:
                 o = 512 * b + (TM if has_l else 0)
-                act("dr%d#" % b, "u%d# mo%d#" % (b, b), win[:, WS * b + POFF + C:WS * b + POFF + C + TM],
-                    T.psp[:, o:o + TM], F.Copy)
+                pick("dr%d#" % b, "u%d# mo%d#" % (b, b), win[:, WS * b + POFF + C:WS * b + POFF + C + TM],
+                     T.psp[:, o:o + TM])
         dd = [(" dl%d#" % b if has_l else "") + (" dr%d#" % b if has_r else "") for b in range(4)]
-        v, t = 32 * W1, C + MID + 32
+        v, t, u = 32 * W1, 2 * MID + 32, 928 - C + MID
         scan("va#", "sa0# sb0# sev", fb[:, SEL:SEL + v], sg[:, 0:v], ab[:, 0:v], 0.0, A.mult, A.max)
         scan("vb#", "sa1# sb1# sev", fb[:, SEL + v:C2], sg[:, v:2 * C], ab[:, v:2 * C], 0.0, A.mult, A.max)
-        tr("r0#", "va# fil", trb[:, C:t], fb[:, SEL - 31:SEL + v:2])
+        tr("r0#", "va# cb", trb[:, MID:t], fb[:, SEL - 31:SEL + v:2])
         tr("r1#", "va#", trb[:, 0:MID], fb[:, SEL + 1:SEL + 2 * MID:2])
-        tr("r2#", "vb# ca", trb[:, t:928], fb[:, SEL + v + 1:C2 + 32:2])
-        tr("r3#", "va# vb#", trb[:, MID:C], fb[:, SEL + 2 * MID + 1:C2:2])
-        for i, (a0, a1) in enumerate(((C, t), (0, MID), (t, 928), (MID, C))):
-            scan("n%d#" % i, "r%d# mk" % i, ss[:, a0:a1], trb[:, a0:a1], T.mk[:, a0:a1], CAP, A.min, A.max)
+        tr("r2#", "vb# ca", trb[:, t:u], fb[:, SEL + v + 1:C2 + 32:2])
+        tr("r3#", "va# vb#", trb[:, u:928], fb[:, SEL + 2 * MID + 1:C2:2])
+        for i, (a0, a1) in enumerate(((MID, t), (0, MID), (t, u), (u, 928))):
+            scan("n%d#" % i, "r%d# mk" % i, ss[:, a0:a1], trb[:, a0:a1], T.mk[:, 0:a1 - a0], CAP, A.min, A.max)
         for h, (a0, a1) in enumerate(((0, MID // 16), (MID // 16, 28))):
-            tt("o0%d#" % h, "n0# n1#" + (" n2# n3#" if h else ""), ev[:, a0:a1], ss[:, 15 + 16 * a0:16 * a1:16],
-               ss[:, 479 + 16 * a0:464 + 16 * a1:16], A.min)
+            tt("o0%d#" % h, "n0# n1#" + " n2# n3#" * h, ev[:, a0:a1], ss[:, u * h + 15:(928 if h else MID):16],
+               ss[:, MID + 31 + 16 * a0:MID + 16 + 16 * a1:16], A.min)
             ts("o1%d#" % h, "o0%d#" % h, ev[:, 32 + a0:32 + a1], ev[:, a0:a1], -4.0, 2048.0 + C - 1, A.mult, A.add)
             tt("o2%d#" % h, "o1%d#" % h, ev[:, 64 + a0:64 + a1], ev[:, a0:a1], ev[:, 32 + a0:32 + a1], A.max)
             ts("el%d#" % h, "o2%d#" % h, T.el[:, a0:a1], ev[:, 64 + a0:64 + a1], POFF - 1024.0, None, A.add)
@@ -393,28 +395,28 @@ def rank_program(g, core, T, topo):
             if i > 0:
                 for b in (1, 3):
                     act("h%d%d#" % (i, b), el + dd[b], T.ib[:, 4 * a0 + b:4 * a1:4], plane(b).indirect(lst), F.Copy)
+                act("h%d2#" % i, el + dd[2], T.jb[:, 2 * a0 + 1:2 * a1:2], plane(2).indirect(lst), F.Copy)
                 scan("ad%d#" % i, "h%d1# h%d3# ib1# ib3# m0 m1" % (i, i), T.xn[:, 4 * a0:4 * a1],
                      T.m01[:, 0:4 * (a1 - a0)], T.ib[:, 4 * a0:4 * a1], 0.0, A.mult, A.add)
-            for b in (0, 2) if i > 0 else range(4):
-                o = C * (b // 2)
-                p = T.ib[:, 4 * a0 + b - 1:4 * a1:4] if b % 2 else T.pc[:, o + a0:o + a1]
-                tt("x%d%d#" % (i, b), "%s %s%d#" % (el, "ib" if b % 2 else "pc", b) + dd[b]
-                   + (" ad%d#" % i if i > 0 else ""), T.xn[:, 4 * a0 + b:4 * a1:4], plane(b).indirect(lst), p, A.add)
-        for h in range(2):
-            a0, a1 = CUT[h:h + 2]
-            quant("q%d$" % h, "x20# x22#" if h else "x00# x01# x02# x03# x10# x12#", nq[:, a0:a1], ns[:, a0:a1],
+                scan("ae%d#" % i, "h%d2# ib2# ad%d#" % (i, i), T.xn[:, 4 * a0:4 * a1:2],
+                     T.m01[:, 0:2 * (a1 - a0)], T.jb[:, 2 * a0:2 * a1], 0.0, A.mult, A.add)
+            for b in (0,) if i > 0 else range(4):
+                tt("x%d%d#" % (i, b), "%s %s%d#" % (el, "ib" if b else "pc", b) + dd[b]
+                   + (" ae%d#" % i if i > 0 else ""), T.xn[:, 4 * a0 + b:4 * a1:4], plane(b).indirect(lst),
+                   twin(b, a0, a1), A.add)
+            quant("q%d$" % i, "x%d0#" % i if i else "x00# x01# x02# x03#", nq[:, a0:a1], ns[:, a0:a1],
                   T.xn[:, 4 * a0:4 * a1])
 
     rnd[0] = ROUNDS
     fq, fs = T["aq%d" % ROUNDS], T["as%d" % ROUNDS]
-    for h in range(2):
-        a0, a1 = CUT[h:h + 2]
+    for h in range(3):
+        a0, a1 = GP[h:h + 2]
         mm("y%d" % h, "vq q%d#" % h, T.pss[:, 512 * h:512 * h + a1 - a0], T.vq[:], T.vs[:], fq[:, a0:a1], fs[:, a0:a1])
         pick("yc%d" % h, "y%d" % h, T.ysb[:, a0:a1], T.pss[:, 512 * h:512 * h + a1 - a0])
         dma("so%d" % h, "Y", "q%d#" % h, T.oc[:, 4 * a0:4 * a1], fq[:, a0:a1].bitcast(dt.uint8), "st")
-        dma("sy%d" % h, "S" if h else "Y", "yc%d" % h, T.y[:, a0:a1], T.ysb[:, a0:a1], "st")
+        dma("sy%d" % h, "S" if h == 2 else "Y", "yc%d" % h, T.y[:, a0:a1], T.ysb[:, a0:a1], "st")
     for k in range(4):
-        dma("ss%d" % k, "S" if k > 1 else "Y", "q0# q1#", T.osc[4 * k:4 * k + 4, :], fs[32 * k:32 * k + 4, :], "st")
-    fixed["st"] = ("st", 16 * 8)
+        dma("ss%d" % k, "S" if k > 1 else "Y", "q0# q1# q2#", T.osc[4 * k:4 * k + 4, :], fs[32 * k:32 * k + 4, :], "st")
+    fixed["st"] = ("st", 16 * 10)
     op("end", "G", None, "st loc")
     emit(g, T, ops, fixed)

from concourse.bass import DstId, RemoteDMATransfer
from concourse.mybir import dt, AluOpType, ActivationFunctionType

A = AluOpType
F = ActivationFunctionType
C, TM, ROUNDS = 448, 96, 2
MID = 288
H = 464
Z0 = 3072.0
LOW = Z0 - 480
CAP = 1024.0 + C + TM
POFF = 2 + TM
WS = 656
NP = 816
W1 = MID // 16 + 1
SEL, C2 = H, H + 2 * C
MK = MID + 32
CUT = (0, MID, C)
GP = (0, 160, MID, C)
PD, PW = (0, 16, 36, 51), (0, 36, 51)
Q4, U8, BF, F16, F32, I32, U16 = "float8_e4m3fn_x4", "uint8", "bfloat16", "float16", "float32", "int32", "uint16"
SCRATCH = {}
for _n, _w, _d in [
    ("xt", 4 * C, BF), ("ut", 512, BF), ("vt", 512, BF), ("wq", 512, Q4), ("wsc", 512, U8), ("uq", 128, Q4),
    ("us", 128, U8), ("uq2", 128, Q4), ("us2", 128, U8), ("vq", 128, Q4), ("vs", 128, U8), ("et", 520, BF),
    ("eq", 512, Q4), ("es", 512, U8), ("pi", 8, I32), ("pj", 8, I32), ("cl", 8, F32), ("nf", 52, F32),
    ("lui", 8, I32), ("lu", 8, U16), ("lp", 52, U16), ("tw", 17 * 52, F32), ("wi", 52, I32),
    ("fb", C2 + H, F16), ("pat", MK, BF), ("mk", MK, BF), ("mask", NP, BF), ("sg", 2 * C, BF),
    ("ysb", C, F32), ("z", 2 * H, BF), ("kt", 448, BF), ("nw", 64, BF), ("fd", H, BF), ("nc", 2 * H, F16),
    ("m", 2 * H, BF), ("win", 4 * WS, BF), ("m01", 640, BF), ("dz", 2 * H, BF), ("acc", 8, F32), ("ec", 348, BF),
    ("rm", 348, BF), ("ml", 12, U16), ("mt", 8 * TM, BF), ("dg", NP, BF), ("ee", NP, BF), ("wn", NP, BF),
    ("rr", NP, BF), ("ab", 2 * C, F16), ("tr", 928, F16), ("ss", 928, F16), ("ev", 96, F32), ("el", 28, U16),
    ("xn", 4 * C, BF), ("pc", C, BF), ("ib", 4 * C, BF), ("jb", 2 * C, BF),
] + [(_n + str(_r), _w, _d) for _r in range(ROUNDS) for _n, _w, _d in [
    ("mq", 2 * TM, Q4), ("ms", 2 * TM, U8), ("lq", 320, Q4), ("ls", 320, U8)]
] + [(_n + str(_r), C, _d) for _r in range(ROUNDS + 1) for _n, _d in [("aq", Q4), ("as", U8)]]:
    SCRATCH[_n] = ("sbuf", [128, _w], _d)
SCRATCH["pss"] = ("psum", [128, 1536], F32)
SCRATCH["psp"] = ("psum", [128, 2048], F32)
NSEM = 140
SEMAPHORES = ["arr0", "arr1", "loc", "st"] + ["k%d" % _i for _i in range(NSEM)]

ON_V = "dg0 dl0 dl2 dr0 dr2 mo0 mo1 yc2"
ORDER = {
    "V": "one par z0 res hi cma colz colw l0 col0 lu ca cmb l1 cb lq kt l2 l9 uq l6 nhi z1 l3 uq2 l7 l8 q0_0 l4 q1_0 "
         "l13 q2_0 l10 l5 col1 e1 e3 za_0 l12 l16 fa_0 da_0 k0_0 zb_0 zc_0 fx_0 fy_0 ma_0 l15 kp_0 e0_0 e1_0 k1_0 t1_0 "
         "t2_0 e3_0 e2_0 df_0 rm0_0 rm2_0 rm1_0 l17 dw_0 mla_0 mlb_0 ta_0 nz_0 tb_0 mo0_0 lp mo1_0 mw_0 dx_0 mq_0 "
         "dg0_0 e2 dy_0 ee0_0 mx_0 my_0 rr0_0 e0 gz_0 fl_0 ic0_0 ia0_0 ee1_0 sb0_0 sa0_0 rr1_0 va_0 ia1_0 ic1_0 r0_0 "
         "sb1_0 sa1_0 r1_0 n0_0 vb_0 n1_0 r2_0 r3_0 o00_0 n2_0 n3_0 o10_0 o01_0 o20_0 dl0_0 dr0_0 o11_0 el0_0 dr2_0 "
         "dl2_0 o21_0 x00_0 el1_0 x03_0 x02_0 ad1_0 x01_0 ae1_0 ad2_0 x10_0 ae2_0 q0_1 x20_0 q1_1 q2_1 za_1 vq fl_1 "
         "k0_1 da_1 fa_1 ma_1 zb_1 k1_1 zc_1 fx_1 fy_1 nz_1 dy_1 kp_1 e0_1 e1_1 tb_1 t2_1 t1_1 e3_1 e2_1 df_1 rm0_1 "
         "rm2_1 rm1_1 ta_1 my_1 mlb_1 mla_1 dg0_1 mo0_1 mo1_1 dx_1 dw_1 mq_1 ee0_1 mw_1 mx_1 rr0_1 gz_1 ia0_1 ic0_1 "
         "ee1_1 sa0_1 sb0_1 rr1_1 va_1 ia1_1 ic1_1 r1_1 sb1_1 sa1_1 r0_1 n1_1 vb_1 n0_1 r2_1 r3_1 o00_1 n2_1 n3_1 o10_1 "
         "dl0_1 o01_1 o20_1 dr0_1 o11_1 el0_1 dr2_1 dl2_1 o21_1 x00_1 el1_1 x03_1 x02_1 ad1_1 x01_1 ae1_1 ad2_1 x10_1 "
         "ae2_1 q0_2 x20_1 q1_2 q2_2 yc2",
    "S": "du m1 w3 w1 w2 sev us2 w4 m0 sg0_0 sg1_0 sg2_0 w0 c1_0 c0_0 c3_0 c2_0 mo3_0 mo2_0 dg1_0 wn0_0 dg2_0 wn1_0 "
         "mk ib3_0 ib2_0 dr1_0 dl1_0 dr3_0 dl3_0 h11_0 h13_0 h12_0 h23_0 h21_0 h22_0 sg0_1 sg1_1 sg2_1 c3_1 c1_1 c2_1 "
         "c0_1 dg1_1 mo3_1 mo2_1 wn0_1 dg2_1 wn1_1 ib2_1 dl1_1 dr1_1 dr3_1 dl3_1 h11_1 h13_1 h12_1 h21_1 h23_1 h22_1 "
         "yc0 ss3 yc1 ss2 sy2",
    "T": "sc0_0 sc1_0 sc2_0 p1_0 p0_0 p3_0 p2_0 u1_0 u0_0 u3_0 u2_0 sc0_1 sc1_1 sc2_1 p3_1 p1_1 p2_1 p0_1 u1_1 u0_1 "
         "u3_1 u2_1 y0 y1 y2",
    "G": "gp gn glu gf0 ge gf1 gf2 gw0 gw1 gm1 gm0 gpat ib1_0 sd0_0 sd1_0 ib3_1 sd0_1 sd1_1 ib1_1 end",
    "Y": "dx0 dx1 dw0 dws dw1 dv pc0_0 pc0_1 so0 so1 so2 sy0 ss0 sy1 ss1",
}


def emit(g, T, ops, fixed):
    Q = {"V": g.vector, "S": g.scalar, "T": g.tensor, "G": g, "Y": g.sync}
    order = {q: [n for n in ORDER[q].split() if n in ops and ops[n][0] == q] for q in Q}
    assert sum(len(v) for v in order.values()) == len(ops)
    pos, know, done, seq, waits = {q: 0 for q in Q}, {q: set() for q in Q}, {}, [], {}
    while len(seq) < len(ops):
        n0 = len(seq)
        for q in Q:
            while pos[q] < len(order[q]) and all(d in done or d in fixed for d in ops[order[q][pos[q]]][2]):
                n = order[q][pos[q]]
                deps = [d for d in ops[n][2] if d not in know[q]]
                deps = [d for d in deps if not any(e != d and d in done.get(e, ()) for e in deps)]
                for d in deps:
                    know[q] |= done.get(d, {d})
                waits[n], done[n] = deps, know[q] | {n}
                seq.append(n)
                pos[q] += 1
        assert len(seq) > n0
    needed = {d for w in waits.values() for d in w}
    last, count, sig, n_dma = {}, {}, dict(fixed), [0]
    for n in seq:
        q, f, _, inc = ops[n]
        for s, v in sorted({sig[d] for d in waits[n]}):
            Q[q].wait_ge(T.sem[s], v)
        if f is None:
            continue
        call = f()
        if inc == "st":
            call.then_inc(T.sem["st"], 16)
        elif n in needed:
            if inc == 16:
                n_dma[0] += 1
                s = "k%d" % (NSEM - n_dma[0])
            else:
                s = next("k%d" % i for i in range(NSEM - 16) if last.get("k%d" % i, n) in done[n])
            last[s], count[s] = n, count.get(s, 0) + inc
            sig[n] = (s, count[s])
            call.then_inc(T.sem[s], inc)


def rank_program(g, core, T, topo):
    rank = T.rank_of(core)
    if rank is None:
        return
    n_ranks = len(T.cores)
    has_l, has_r = rank > 0, rank < n_ranks - 1
    V, S, PE = g.vector, g.scalar, g.tensor
    ops, fixed, rnd = {}, {}, [0]

    def op(name, q, f, deps="", inc=1):
        fix = lambda s: s.replace("#", "_%d" % rnd[0]).replace("$", "_%d" % (rnd[0] + 1))
        ops[fix(name)] = (q, f, fix(deps).split(), inc)

    def ts(n, d, out, in0, s1, s2, o0, o1=None):
        if o1 is None:
            op(n, "V", lambda: V.tensor_scalar(out, in0, s1, None, o0), d)
        else:
            op(n, "V", lambda: V.tensor_scalar(out, in0, s1, s2, o0, o1), d)

    def tt(n, d, out, a, b, o):
        op(n, "V", lambda: V.tensor_tensor(out, a, b, o), d)

    def cp(n, d, out, a):
        op(n, "V", lambda: V.tensor_copy(out, a), d)

    def scan(n, d, out, a, b, init, o0, o1):
        op(n, "V", lambda: V.tensor_tensor_scan(out, a, b, init, o0, o1), d)

    def tr(n, d, out, a):
        op(n, "V", lambda: V.transpose(out, a), d)

    def ms(n, d, ap, c):
        op(n, "V", lambda: V.memset(ap, c), d)

    def quant(n, d, oc, osc, src):
        op(n, "V", lambda: V.quantize_mx(oc, osc, src), d)

    def act(n, d, out, a, fn, **kw):
        op(n, "S", lambda: S.activation(out, a, fn, **kw), d)

    def pick(n, d, out, a, scale=None, bias=0.0):
        if n.rstrip("#") not in ON_V.split():
            act(n, d, out, a, F.Identity, scale=scale or 1.0, bias=bias)
        elif scale:
            ts(n, d, out, a, scale, bias, A.mult, A.add)
        else:
            cp(n, d, out, a)

    def mm(n, d, out, lq, ls, rq, rs):
        op(n, "T", lambda: PE.matmul_mx(out, lq, ls, rq, rs, True, True), d)

    def dma(n, q, d, out, src, inc=16):
        op(n, q, lambda: (g.sync if q == "Y" else S).dma_start(out, src), d, inc)

    def iota(n, d, out, pat, base, cm=0, small=True):
        if small:
            op(n, "G", lambda: g.iota(out, pat, base, cm, allow_small_or_imprecise_dtypes=True), d)
        else:
            op(n, "G", lambda: g.iota(out, pat, base, cm), d)

    win, z, nc, m, fb, kt, fd, mask, sg, dz, acc = (T.win, T.z, T.nc, T.m, T.fb, T.kt, T.fd, T.mask, T.sg, T.dz,
                                                    T.acc)
    dma("du", "S", "", T.ut[:], T.u[:])
    for h in range(2):
        dma("dx%d" % h, "Y", "", T.xt[:, 4 * CUT[h]:4 * CUT[h + 1]], T.x[:, 4 * CUT[h]:4 * CUT[h + 1]])
        dma("dw%d" % h, "Y", "", T.wq[:, 256 * h:256 * h + 256].bitcast(dt.uint8), T.wc[:, 1024 * h:1024 * h + 1024])
    dma("dws", "Y", "", T.wsc[:], T.ws[:])
    dma("dv", "Y", "dw1", T.vt[:], T.v[:])

    iota("gp", "", T.pi[:, 0:1], [[0, 1]], 0, 1, small=False)
    iota("glu", "", T.lui[:], [[16, 8]], 0, small=False)
    iota("gn", "", T.nf[:], [[16, 52]], 0)
    iota("gf0", "", fd[:], [[0, H // 2], [2, 2]], 0)
    iota("gf1", "gf0", fd[:, 15:H:16], [[0, H // 16]], 4096)
    iota("gf2", "gf0", fd[:, C:C + 1], [[0, 1]], 4096)
    iota("gw0", "", T.nw[:, 0:58], [[0, 2], [-16, 29]], 249)
    iota("gw1", "gw0", T.nw[:, 28:58:29], [[0, 2]], 256 - C - TM)
    ms("one", "", mask[:], 1.0)
    op("ge", "G", lambda: g.affine_select(T.et[:], mask[:, 0:520], [[-1, 520]], A.is_equal, 0.0, 3, 4), "one")
    iota("gpat", "", T.pat[:], [[0, MK // 32], [1, 2], [0, 16]], 0)
    act("w0", "one", win[:, 0:POFF], mask[:, 0:POFF], F.Copy, scale=0.0)
    for b in range(4):
        w = WS - C if b < 3 else WS - C - POFF
        act("w%d" % (b + 1), "one", win[:, WS * b + POFF + C:WS * b + POFF + C + w], mask[:, 0:w], F.Copy, scale=0.0)
    act("sev", "one", sg[:, 0:2 * C:2], mask[:, 0:C], F.Copy, scale=-1.0)
    act("m0", "one", T.m01[:, 0:640:2], mask[:, 0:320], F.Copy, scale=0.0)
    act("m1", "one", T.m01[:, 1:640:2], mask[:, 0:320], F.Copy)
    res, hi, par = T.pj[:, 0:1], T.pj[:, 1:2], T.pj[:, 2:3]
    colz, col0, col1, colw, nhi, cmb, cma = [T.cl[:, i:i + 1] for i in range(7)]
    ts("res", "gp", res, T.pi[:, 0:1], 15, None, A.bitwise_and)
    ts("hi", "gp", hi, T.pi[:, 0:1], 4, 1, A.logical_shift_right, A.bitwise_and)
    ts("par", "gp", par, T.pi[:, 0:1], 1, None, A.bitwise_and)
    ts("colz", "res", colz, res, Z0 - 7.5, None, A.add)
    ts("colw", "par", colw, par, 1280.0, None, A.add)
    ts("cmb", "par", cmb, par, -1.0, POFF + C - 257.0, A.mult, A.add)
    ts("col0", "colz colw", col0, colz, colw, C + 1024 + 7.5, A.subtract, A.add)
    ts("col1", "col0", col1, col0, -1.0, None, A.mult)
    ts("cma", "par", cma, par, POFF + 256.0, None, A.add)
    ts("nhi", "hi", nhi, hi, -CAP, None, A.mult)
    act("mk", "gpat nhi", T.mk[:], T.pat[:], F.Abs, scale=CAP, bias=nhi)
    cp("lu", "glu", T.lu[:], T.lui[:])
    quant("uq", "du", T.uq[:], T.us[:], T.ut[:])
    cp("uq2", "uq lu", T.uq2[:].bitcast(dt.uint32), T.uq[:].bitcast(dt.uint32).indirect(T.lu[:, 0:8]))
    op("us2", "S", lambda: S.activation(T.us2[:], T.us[:].indirect(T.lu[:, 0:8]), F.Copy), "uq lu")
    ca, cb = C2, 0
    scan("ca", "one", fb[:, ca:ca + H], mask[:, 0:H], mask[:, 0:H], 1023.0, A.add, A.mult)
    ts("cb", "ca", fb[:, cb:cb + H], fb[:, ca:ca + H], 0.25, None, A.mult)
    ms("z0", "", z[:, 0:2 * H:H], Z0)
    ms("z1", "", z[:, C + 1:2 * H:H], LOW)
    ms("kt", "", kt[:], LOW)
    iota("gm0", "ge w0 w1 w2 w3 w4 sev m0 m1 ca", mask[:, 0:812:29], [[0, 28]], 0)
    iota("gm1", "ge w0 w1 w2 w3 w4 sev m0 m1 ca", mask[:, 28:812:28], [[0, 28]], 0)
    for b in range(4):
        quant("e%d" % b, "ge", T.eq[:, 128 * b:128 * b + 128], T.es[:, 128 * b:128 * b + 128], T.et[:, 3 - b:515 - b])
    quant("vq", "dv", T.vq[:], T.vs[:], T.vt[:])
    tw = [T.tw[:, 52 * i:52 * i + 52] for i in range(17)]
    qv = T.wi[:]
    ts("l0", "gn colz", tw[0], T.nf[:], colz, 7.5 - Z0, A.add, A.add)
    ts("l1", "l0", tw[1], tw[0], -14.0, 1.0 / 29, A.add, A.mult)
    cp("lq", "l1", qv, tw[1])
    ts("l2", "lq", tw[2], qv, -29.0, None, A.mult)
    tt("l3", "l2", tw[3], tw[2], tw[0], A.add)
    tt("l4", "l3", tw[4], tw[3], qv, A.add)
    ts("l5", "l4", tw[5], tw[4], 28.0, None, A.is_gt)
    ts("l6", "lq", tw[6], qv, -1.0, 57.0, A.mult, A.add)
    ts("l7", "l3", tw[7], tw[3], -1.0, 28.0, A.mult, A.add)
    ts("l8", "l3", tw[8], tw[3], 0.0, None, A.is_equal)
    ts("l9", "lq", tw[9], qv, -1.0, 92.0, A.mult, A.add)
    ts("l10", "l4", tw[10], tw[4], 28.0, 64.0, A.is_equal, A.mult)
    tt("l12", "l5 l6", tw[12], tw[5], tw[6], A.mult)
    tt("l13", "l8 l9", tw[13], tw[8], tw[9], A.mult)
    tt("l15", "l12 l7", tw[15], tw[12], tw[7], A.add)
    tt("l16", "l13 l10", tw[16], tw[13], tw[10], A.add)
    tt("l17", "l15 l16", tw[2], tw[15], tw[16], A.add)
    ts("lp", "l17", T.lp[:], tw[2], 121.0, None, A.min)
    for h in range(3):
        quant("q%d_0" % h, "dx%d" % (h // 2), T.aq0[:, GP[h]:GP[h + 1]], T.as0[:, GP[h]:GP[h + 1]],
              T.xt[:, 4 * GP[h]:4 * GP[h + 1]])

    def link(src_rank, dst_rank):
        src, dst = T.cores[src_rank], T.cores[dst_rank]
        eng = topo.engines(src, dst)
        if 0 < src_rank < n_ranks - 1:
            k = len(eng) // 2
            eng = eng[:k] if dst_rank < src_rank else eng[k:]
        rid, pid, _ = topo.addr(dst)
        return DstId(rid=rid, pnc=pid), sum(1 << e for e in eng), len(eng)

    others = [o for o in (rank - 1, rank + 1) if 0 <= o < n_ranks]
    fixed["loc"] = ("loc", 2 * ROUNDS * sum(link(rank, o)[2] for o in others))
    td, keyp, tb, tbw = kt[:, 64:192], kt[:, 192:250], kt[:, 320:378], kt[:, 320:448]
    fv = nc[:, 0:2 * H:16]
    plane = lambda b: win[:, WS * b:WS * (b + 1)]
    own = lambda b: win[:, WS * b + POFF:WS * b + POFF + C]
    twin = lambda b, a0, a1: (T.pc[:, a0:a1] if b == 0 else T.jb[:, 2 * a0:2 * a1:2] if b == 2
                              else T.ib[:, 4 * a0 + b - 1:4 * a1:4])
    for r in range(ROUNDS):
        rnd[0] = r
        aq, asc, nq, ns = T["aq%d" % r], T["as%d" % r], T["aq%d" % (r + 1)], T["as%d" % (r + 1)]
        mq, msc, lqb, lsb = T["mq%d" % r], T["ms%d" % r], T["lq%d" % r], T["ls%d" % r]
        arr = "arr%d" % r
        fixed[arr] = (arr, sum(2 * link(o, rank)[2] for o in others))
        for h in range(3):
            a0, a1 = GP[h:h + 2]
            mm("sc%d#" % h, "uq2 us2 q%d#" % h, T.pss[:, 512 * h:512 * h + a1 - a0], T.uq2[:], T.us2[:],
               aq[:, a0:a1], asc[:, a0:a1])
            act("sg%d#" % h, "sc%d#" % h, sg[:, 2 * a0 + 1:2 * a1:2], T.pss[:, 512 * h:512 * h + a1 - a0], F.Sign,
                bias=2.0 ** -110, accum_out=acc[:, h:h + 1])
        for b in range(4):
            mm("p%d#" % b, "dw%d dws q0# q1# q2#" % (b // 2), T.psp[:, 512 * b:512 * b + C],
               T.wq[:, 128 * b:128 * b + 128], T.wsc[:, 128 * b:128 * b + 128], aq[:], asc[:])
            act("c%d#" % b, "p%d#" % b, own(b), T.psp[:, 512 * b:512 * b + C], F.Copy, scale=0.0625)
        dma("pc0#", "Y", "c0#", T.pc[:], own(0))
        for b in (2,) if r else (2, 3):
            act("ib%d#" % b, "c%d#" % b, twin(b, 0, C), own(b), F.Copy)
        for b in (1, 3) if r else (1,):
            op("ib%d#" % b, "G", lambda b=b: g.affine_select(twin(b, 0, C), own(b), [[0, C]], A.is_ge, 0.0, 0, 0),
               "c%d#" % b)
        e = GP[1]
        s0, s1, sr = sg[:, 1:2 * e:2], sg[:, 2 * e + 1:2 * C:2], sg[:, 2 * C - 1:0:-2]
        scan("za#", "sg0# colz", z[:, 1:e + 1], s0, s0, colz, A.add, A.max)
        ts("k0#", "sg0# colz col0 col1", acc[:, 5:8], T.cl[:, 0:3], acc[:, 0:1], None, A.add)
        ts("k1#", "sg1# sg2#", acc[:, 3:4], acc[:, 1:2], acc[:, 2:3], None, A.add)
        scan("zb#", "sg0# sg1# sg2# colz", z[:, H + 1:H + C + 1], sr, sr, colz, A.max, A.subtract)
        scan("zc#", "sg1# sg2# k0#", z[:, e + 1:C + 1], s1, s1, acc[:, 5:6], A.add, A.max)
        scan("fa#", "za# gf1 gf2", nc[:, e - 1::-1], fd[:, e - 1::-1], z[:, e:0:-1], 0.0, A.add, A.min)
        scan("fx#", "zb# z1 gf1 gf2", nc[:, H + C:H - 1:-1], fd[:, C::-1], z[:, H + C + 1:H:-1], 0.0, A.add, A.min)
        scan("fy#", "zc# z1 gf1 gf2", nc[:, C:e - 1:-1], fd[:, C:e - 1:-1], z[:, C + 1:e:-1], 0.0, A.add, A.min)
        for n, d, a0, a1 in (("a", "za# z0", 0, e), ("x", "za# zc#", e, C), ("y", "zb# z0", H, H + C // 2),
                             ("w", "zb#", H + C // 2, H + C)):
            scan("d%s#" % n, d, dz[:, a0:a1], z[:, a0 + 1:a1 + 1], z[:, a0:a1], 0.0, A.max, A.subtract)
            ts("m%s#" % n, "d%s#" % n, m[:, a0:a1], dz[:, a0:a1], 1.0 / 16, 1.0, A.mult, A.add)
        ms("gz#", "ma# mx# my# mw#", m[:, 0:2 * H:16], 0.0)
        ts("ta#", "k0# k1# za# zc# z0 kt", kt[:, 441:412:-1], z[:, 0:C + 1:16], acc[:, 3:4], acc[:, 6:7], A.subtract,
           A.subtract)
        ts("tb#", "k0# k1# zb# z0 kt", kt[:, 412:383:-1], z[:, H:H + C + 1:16], acc[:, 3:4], acc[:, 7:8], A.add, A.add)
        ts("nz#", "za# zb# zc# z0 kt", kt[:, 185:127:-1], z[:, 0:2 * H:16], -1.0, LOW + 8 - 80, A.mult, A.add)
        scan("kp#", "fa# fx# fy# gw1 kt", keyp, T.nw[:, 0:58], fv, 4096.0, A.min, A.add)
        ts("e0#", "fa# fx# fy#", T.ec[:, 0:58], fv, 1 - Z0, -1024.0, A.add, A.mult)
        ts("e1#", "fa# fx# fy#", T.ec[:, 58:116], fv, 17 - Z0, -1024.0, A.add, A.mult)
        scan("t1#", "kp#", tb, keyp, fv, 0.0, A.max, A.subtract)
        scan("t2#", "kp#", kt[:, 262:320], keyp, fv, 0.0, A.max, A.subtract)
        for i in (1, 2):
            ts("e%d#" % (i + 1), "e0# e1#", T.ec[:, 116 * i:116 * i + 116], T.ec[:, 0:116], -32768.0 * i, None, A.add)
        scan("df#", "kp#", kt[:, 64:121], kt[:, 192:249], kt[:, 193:250], 0.0, A.max, A.subtract)
        for i in range(3):
            back = slice(116 * i + 115, 116 * i - 1 if i else None, -1)
            scan("rm%d#" % i, "t1# t2# e0# e1#" + (" e%d#" % (i + 1) if i else ""), T.rm[:, back], T.ec[:, back],
                 kt[:, 377:261:-1], 0.0, A.max, A.min)
        ts("mla#", "rm0# rm1# rm2# cma", T.ml[:, 0:6], T.rm[:, 0:348:58], -1.0, cma, A.mult, A.add)
        ts("mlb#", "rm0# rm1# rm2# cmb", T.ml[:, 6:12], T.rm[:, 29:348:58], cmb, None, A.add)
        for b in range(4):
            pick("mo%d#" % b, "mla# mlb# c%d# w%d w%d" % (b, b, b + 1) + " mq_0" * r, T.mt[:, b:8 * TM:4],
                 plane(b).indirect(T.ml[:, 0:12]))
        quant("mq#", "mo0# mo1# mo2# mo3#", mq[:], msc[:], T.mt[:])

        def send(kind, mq=mq, msc=msc, lqb=lqb, lsb=lsb, arr=arr):
            trs = []
            for other in others:
                did, engines, _ = link(rank, other)
                s0, d0 = (0, TM) if other < rank else (TM, 0)
                if kind == 0:
                    src, dst = mq[:, s0:s0 + TM].bitcast(dt.uint8), lqb[:, d0:d0 + TM].bitcast(dt.uint8)
                else:
                    src, dst = msc[:, s0:s0 + TM], lsb[:, d0:d0 + TM]
                trs.append(RemoteDMATransfer(dst_ids=[did], dma_engine_mask=engines, remote_sem=T.sem[arr], src=src,
                                             dst=dst))
            return g.remote_dma_fused(trs, local_sem=T.sem["loc"])

        op("sd0#", "G", lambda send=send: send(0), "mq#")
        op("sd1#", "G", lambda send=send: send(1), "mq#")
        for i in range(3):
            a0, a1 = PD[i:i + 2]
            pick("dg%d#" % i, "df# nz# lp", T.dg[:, 16 * a0:16 * a1], td.indirect(T.lp[:, a0:a1]), -128.0, 2048.0)
        for i in range(2):
            a0, a1 = PW[i:i + 2]
            pick("wn%d#" % i, "t1# ta# tb# lp", T.wn[:, 16 * a0:16 * a1], tbw.indirect(T.lp[:, a0:a1]))
        for h, (a0, a1) in enumerate(((0, 29 * W1), (29 * W1, NP))):
            scan("ee%d#" % h, "dg0# dg1# gm0 gm1" + (" dg2#" if h else ""), T.ee[:, a0:a1], mask[:, a0:a1],
                 T.dg[:, a0:a1], 0.0, A.mult, A.add)
            scan("rr%d#" % h, "ee%d# wn0#" % h + (" wn1#" if h else ""), T.rr[:, a0:a1], T.ee[:, a0:a1],
                 T.wn[:, a0:a1], 0.0, A.max, A.min)
        fill = ""
        if not (has_l and has_r):
            f0, fill = 2 * TM if has_r else TM, " fl#"
            quant("fl#", "dx0", lqb[:, f0:f0 + 128], lsb[:, f0:f0 + 128], T.xt[:, 0:512])
        ab, trb, ss, ev = T.ab, T.tr, T.ss, T.ev
        for h, (w0, w1) in enumerate(((0, W1), (W1, 28))):
            a0, a1 = 16 * w0, 16 * w1
            ts("ia%d#" % h, "rr%d# cb colw" % h, fb[:, ca + a0 + 16:ca + a1 + 1:16], T.rr[:, 27 + 28 * w0:28 * w1:28],
               -1.0, colw, A.mult, A.add)
            ts("ic%d#" % h, "rr%d# cb colw" % h, fb[:, cb + C - a0:cb + C - a1:-16], T.rr[:, 28 + 29 * w0:29 * w1:29],
               colw, -0.25, A.subtract, A.mult)
            scan("sa%d#" % h, "ia%d# gz#" % h, ab[:, 2 * a1 - 2:(2 * a0 - 2 if h else None):-2], m[:, a1:a0:-1],
                 fb[:, ca + a1:ca + a0:-1], 0.0, A.mult, A.max)
            scan("sb%d#" % h, "ic%d# gz#" % h, ab[:, 2 * a0 + 1:2 * a1:2], m[:, H + C - a0:H + C - a1:-1],
                 fb[:, cb + C - a0:cb + C - a1:-1], 0.0, A.mult, A.max)
        l0 = 0 if has_l else TM
        ln = 2 * TM if has_l and has_r else 128
        for b in range(4):
            mm("u%d#" % b, "e%d c%d# %s" % (b, b, arr) + fill, T.psp[:, 512 * b:512 * b + ln],
               T.eq[:, 128 * b:128 * b + 128], T.es[:, 128 * b:128 * b + 128], lqb[:, l0:l0 + ln], lsb[:, l0:l0 + ln])
            if has_l:
                pick("dl%d#" % b, "u%d# mo%d#" % (b, b), win[:, WS * b + POFF - 1:WS * b + 1:-1],
                     T.psp[:, 512 * b:512 * b + TM])
            if has_r:
                o = 512 * b + (TM if has_l else 0)
                pick("dr%d#" % b, "u%d# mo%d#" % (b, b), win[:, WS * b + POFF + C:WS * b + POFF + C + TM],
                     T.psp[:, o:o + TM])
        dd = [(" dl%d#" % b if has_l else "") + (" dr%d#" % b if has_r else "") for b in range(4)]
        v, t, u = 32 * W1, 2 * MID + 32, 928 - C + MID
        scan("va#", "sa0# sb0# sev", fb[:, SEL:SEL + v], sg[:, 0:v], ab[:, 0:v], 0.0, A.mult, A.max)
        scan("vb#", "sa1# sb1# sev", fb[:, SEL + v:C2], sg[:, v:2 * C], ab[:, v:2 * C], 0.0, A.mult, A.max)
        tr("r0#", "va# cb", trb[:, MID:t], fb[:, SEL - 31:SEL + v:2])
        tr("r1#", "va#", trb[:, 0:MID], fb[:, SEL + 1:SEL + 2 * MID:2])
        tr("r2#", "vb# ca", trb[:, t:u], fb[:, SEL + v + 1:C2 + 32:2])
        tr("r3#", "va# vb#", trb[:, u:928], fb[:, SEL + 2 * MID + 1:C2:2])
        for i, (a0, a1) in enumerate(((MID, t), (0, MID), (t, u), (u, 928))):
            scan("n%d#" % i, "r%d# mk" % i, ss[:, a0:a1], trb[:, a0:a1], T.mk[:, 0:a1 - a0], CAP, A.min, A.max)
        for h, (a0, a1) in enumerate(((0, MID // 16), (MID // 16, 28))):
            tt("o0%d#" % h, "n0# n1#" + " n2# n3#" * h, ev[:, a0:a1], ss[:, u * h + 15:(928 if h else MID):16],
               ss[:, MID + 31 + 16 * a0:MID + 16 + 16 * a1:16], A.min)
            ts("o1%d#" % h, "o0%d#" % h, ev[:, 32 + a0:32 + a1], ev[:, a0:a1], -4.0, 2048.0 + C - 1, A.mult, A.add)
            tt("o2%d#" % h, "o1%d#" % h, ev[:, 64 + a0:64 + a1], ev[:, a0:a1], ev[:, 32 + a0:32 + a1], A.max)
            ts("el%d#" % h, "o2%d#" % h, T.el[:, a0:a1], ev[:, 64 + a0:64 + a1], POFF - 1024.0, None, A.add)
        for i in range(3):
            a0, a1 = GP[i:i + 2]
            el, lst = "el%d#" % (i // 2), T.el[:, a0 // 16:a1 // 16]
            if i > 0:
                for b in (1, 3):
                    act("h%d%d#" % (i, b), el + dd[b], T.ib[:, 4 * a0 + b:4 * a1:4], plane(b).indirect(lst), F.Copy)
                act("h%d2#" % i, el + dd[2], T.jb[:, 2 * a0 + 1:2 * a1:2], plane(2).indirect(lst), F.Copy)
                scan("ad%d#" % i, "h%d1# h%d3# ib1# ib3# m0 m1" % (i, i), T.xn[:, 4 * a0:4 * a1],
                     T.m01[:, 0:4 * (a1 - a0)], T.ib[:, 4 * a0:4 * a1], 0.0, A.mult, A.add)
                scan("ae%d#" % i, "h%d2# ib2# ad%d#" % (i, i), T.xn[:, 4 * a0:4 * a1:2],
                     T.m01[:, 0:2 * (a1 - a0)], T.jb[:, 2 * a0:2 * a1], 0.0, A.mult, A.add)
            for b in (0,) if i > 0 else range(4):
                tt("x%d%d#" % (i, b), "%s %s%d#" % (el, "ib" if b else "pc", b) + dd[b]
                   + (" ae%d#" % i if i > 0 else ""), T.xn[:, 4 * a0 + b:4 * a1:4], plane(b).indirect(lst),
                   twin(b, a0, a1), A.add)
            quant("q%d$" % i, "x%d0#" % i if i else "x00# x01# x02# x03#", nq[:, a0:a1], ns[:, a0:a1],
                  T.xn[:, 4 * a0:4 * a1])

    rnd[0] = ROUNDS
    fq, fs = T["aq%d" % ROUNDS], T["as%d" % ROUNDS]
    for h in range(3):
        a0, a1 = GP[h:h + 2]
        mm("y%d" % h, "vq q%d#" % h, T.pss[:, 512 * h:512 * h + a1 - a0], T.vq[:], T.vs[:], fq[:, a0:a1], fs[:, a0:a1])
        pick("yc%d" % h, "y%d" % h, T.ysb[:, a0:a1], T.pss[:, 512 * h:512 * h + a1 - a0])
        dma("so%d" % h, "Y", "q%d#" % h, T.oc[:, 4 * a0:4 * a1], fq[:, a0:a1].bitcast(dt.uint8), "st")
        dma("sy%d" % h, "S" if h == 2 else "Y", "yc%d" % h, T.y[:, a0:a1], T.ysb[:, a0:a1], "st")
    for k in range(4):
        dma("ss%d" % k, "S" if k > 1 else "Y", "q0# q1# q2#", T.osc[4 * k:4 * k + 4, :], fs[32 * k:32 * k + 4, :], "st")
    fixed["st"] = ("st", 16 * 10)
    op("end", "G", None, "st loc")
    emit(g, T, ops, fixed)
